import numpy as np, ml_dtypes
CORES = [13,21,141,149]
N = 4
BF = ml_dtypes.bfloat16
Q, W, ND, T, S, SH, KS, WM, DM = 256, 2048, 1024, 5, 1, 5, 29, 8, 4
def pick(a, i):
    return np.take_along_axis(a, i.reshape(N, 8, 1, -1), 3).reshape((N, 8, 16) + i.shape[2:])
def bf(a):
    return np.ascontiguousarray(a).astype(np.float32).astype(BF)
def limits(rng, X, lo, hi):
    s = np.sort(np.add.reduce(np.abs(pick(X, rng.integers(0, W, (N, 8, 512))) - pick(X, rng.integers(0, W, (N, 8, 512)))), axis=2), axis=2)
    return np.concatenate([np.take_along_axis(s, rng.choice(np.array(v), (N, 8, 1)), 2) for v in (lo, hi)], axis=2)
def parts(rng):
    top = rng.choice(np.array([64, 128, 256]), (1, 8, 1, 1)) - 1
    X = rng.integers(0, 256, (N, 8, 16, W)) & top; z = rng.integers(0, 256, (N, 8, 16, Q)) & top
    DL = rng.integers(0, 256, (N, 8, 16, ND)); L = rng.integers(0, 256, (N, 8, 16, Q)); R = rng.integers(0, 256, (N, 8, 16, Q))
    n = rng.integers(1, 5, (N, 8, Q)); kp = rng.integers(0, 256, (N, 8, 16, 1)); w = rng.integers(0, 256, (N, 8, 16, 1))
    return X, DL, L, R, z, n, kp, w, limits(rng, X, [10, 26, 51, 77], [410, 450, 480])
def pack(X, DL, L, R, z, n, kp, w, lm):
    return {"stock": bf(X.reshape(N, 128, W)), "donor": bf(DL.reshape(N, 128, ND)), "lend": bf(L.reshape(N, 128, Q)), "rend": bf(R.reshape(N, 128, Q)), "zed": bf(z.reshape(N, 128, Q)),
            "cnt": n.astype(np.int32), "kap": kp.reshape(N, 128, 1).astype(np.int32), "wt": w.reshape(N, 128, 1).astype(np.int32), "lim": lm.astype(np.int32)}
def setup_inputs(rng):
    return pack(*parts(rng))
def setup_inputs_spread(rng):
    def col(m): return (np.exp2(8 * rng.random((N, 8, 1, m))) * rng.random((N, 8, 16, m))).astype(np.int64)
    def few(m): return np.exp2(8 * rng.random((N, 8, 16, m))).astype(np.int64) - rng.integers(0, 2, (N, 8, 16, m))
    X, z = col(W), col(Q)
    return pack(X, few(ND), few(Q), few(Q), z, rng.choice(np.array([1, 1, 1, 2, 3, 4]), (N, 8, Q)), few(1), few(1), limits(rng, X, [1, 10, 40, 120, 300], [200, 400, 460, 490, 508]))
def ends(rng, m):
    k = rng.integers(0, 3, (N, 8, 1, m))
    return np.where(k == 2, 255 * rng.integers(0, 2, (N, 8, 16, m)), 255 * k)
def setup_inputs_ends(rng):
    X, DL, L, R, z = ends(rng, W), ends(rng, ND), ends(rng, Q), ends(rng, Q), ends(rng, Q)
    n = 1 + 3 * rng.integers(0, 2, (N, 8, Q)); kp = 255 * rng.integers(0, 2, (N, 8, 16, 1)); w = 255 * rng.integers(0, 2, (N, 8, 16, 1))
    kp[:, :, 3] = 0; kp[:, :, 15] = 255; w[:, :, 2] = 0; w[:, :, 5] = 255; w[:, 4] = 255
    n[:, :, 0] = 4; n[:, :, 1] = 1; n[:, :, Q - 2] = 1; n[:, :, Q - 1] = 4
    for g in (0, 6):
        w[:, g, 14] = 1; w[:, g, 15] = 16
        for i in (0, 3, Q - 1): z[:, g, :, i] = 0; z[:, g, 14, i] = 15; z[:, g, 15, i] = 255
    for i in (2, 5, Q - 1): z[:, 7, :, i] = 0; z[:, 5, :, i] = 0
    X[:, 7, :, 0] = 255; X[:, 5, :, 0] = 0
    for i in (1, 4, Q - 1): z[:, 4, :, i] = 255
    lm = 4080 * rng.integers(0, 2, (N, 8, 2))
    lm[:, 2, 0] = 0; lm[:, 3, 0] = 4080; lm[:, 0, 1] = 0; lm[:, 1, 1] = 4080; lm[:, 7, 1] = 4080; lm[N - 1, :, 0] = 4080
    return pack(X, DL, L, R, z, n, kp, w, lm)
def far(d):
    return np.minimum(np.maximum(d - 255 * np.arange(16), 0), 255)
def setup_inputs_corners(rng):
    X, DL, L, R, z, n, kp, w, lm = parts(rng); o = KS * np.arange(16); k = np.arange(16)[:, None]
    for q in range(N):
        for g in range(8):
            j = (g // 2 + q) % 4
            if g % 2 == 1 and j == 3: continue
            w[q, g] = 0; DL[q, g, :, 0] = 0
            if g % 2 == 0:
                b = (2, 5, 15, 16)[j]; s = int(rng.integers(20, 100)); v = int(rng.integers(20, 100))
                y = np.full((16, 16), 100); y[0, b:] += s
            else:
                b = 7; s, v = ((4080, 4079), (2049, 2048), (1, 0))[j]
                y = np.zeros((16, 16), np.int64); y[:, b:] = far(s)[:, None]
            for e in range(3):
                X[q, g][:, o + e] = y + far((0, v, v + 1)[e])[:, None] * np.where(y >= 128, -1, 1)
            sb = s if q == 1 else s - 1
            lm[q, g, 0] = v; lm[q, g, 1] = sb
            m = n[q, g]; f = np.where((b > m) & (sb < s), b, 16)
            c = rng.integers(0, 6, Q); p = np.choose(c, [m - 1, m, f - 1, f, 15 + 0 * m, 16 + 0 * m])
            late = np.where((c == 0) | (c == 3), 2, rng.integers(1, 3, (16, Q)))
            R[q, g] = np.where(k == p, 1, np.where(k < p, 2, late))
    return pack(X, DL, L, R, z, n, kp, w, lm)
def setup_inputs_crowd(rng):
    X, DL, L, R, z, n, kp, w, lm = parts(rng); o = KS * np.arange(16)
    lm[:, :, 0] = 4080; lm[4:, :, 0] = rng.choice(np.array([0, 4080]), (N - 4, 8))
    s = (3 - S) % N
    for v in (DL, L, R): v[s] = np.minimum(v[s], 253)
    def plant(q, g, who):
        w[q, g] = 0; DL[q, g, :, 0] = 0; X[q, g][:, o] = 0; X[q, g][:, o + 1] = 255
        R[q, g] = np.where(who, 0, 1); lm[q, g, 0] = rng.choice(np.array([0, 4079])); lm[q, g, 1] = rng.choice(np.array([0, 4080]))
    i = np.arange(Q)
    plant(0, 7, i >= 0); plant(1, 0, i < Q - 1)
    for g in range(8):
        plant(2, g, i < 0); plant(3, g, (i == 0) & (g == 7))
    DL[3, :, :, 1] = 255 - (np.arange(16) & 1); lm[3, :, 0] = 0; lm[3, ::2, 1] = 0
    return pack(X, DL, L, R, z, n, kp, w, lm)
def setup_inputs_ties(rng):
    X, DL, L, R, z, n, kp, w, lm = parts(rng)
    pal = np.repeat(rng.integers(0, 256, (1, 8, 16, 5)), N, axis=0)
    X = pick(pal, rng.integers(0, 5, (N, 8, W))); z = pick(pal, rng.integers(0, 5, (N, 8, Q)))
    kp = rng.choice(np.array([0, 1, 7, 128, 255]), kp.shape); few = np.array([0, 1, 3, 100, 254, 255])
    DL[:, ::2] = rng.choice(few, (N, 4, 16, ND)); R[:, 1::2] = rng.choice(few, (N, 4, 16, Q))
    return pack(X, DL, L, R, z, n, kp, w, limits(rng, X, [10, 51, 150, 256], [150, 256, 400, 480]))
def check_inputs(d):
    bad = []
    for k, lo, hi in (("stock", 0, 255), ("donor", 0, 255), ("lend", 0, 255), ("rend", 0, 255), ("zed", 0, 255), ("cnt", 1, 4), ("kap", 0, 255), ("wt", 0, 255), ("lim", 0, 4080)):
        v = np.asarray(d[k]).astype(np.float64)
        if not np.all((v >= lo) & (v <= hi)): bad.append("range of " + k)
        elif not np.all(v == np.floor(v)): bad.append("whole numbers of " + k)
    return bad
def reference(stock, donor, lend, rend, zed, cnt, kap, wt, lim):
    def whole(a, m): return np.asarray(a).astype(np.float32).astype(np.int64).reshape(N, 8, 16, m)
    X, DL, L, R, z = whole(stock, W), whole(donor, ND), whole(lend, Q), whole(rend, Q), whole(zed, Q)
    n = cnt.astype(np.int64); kp, w = whole(kap, 1), whole(wt, 1)
    th = lim[:, :, 0].astype(np.int64)[:, :, None, None]; sb = lim[:, :, 1].astype(np.int64)[:, :, None, None]
    k = np.arange(16)[:, None]; lane = np.arange(Q); A = np.zeros((N, 1, 1, 1), np.int64)
    for t in range(T):
        if t > 0: L, R, z, n = [np.roll(v, S, axis=0) for v in (L, R, z, n)]
        u = np.add.reduce(w * z, axis=2) & 4095
        ub = u[:, :, None]; nb = n[:, :, None]
        c = ((ub * ub >> SH) + kp * ub + A) & (W - 1)
        m = np.argmin(np.add.reduce(np.abs(pick(X, c) - z[:, :, :, None]), axis=2), axis=2)
        c = np.take_along_axis(c, m[:, :, None], 2)[:, :, 0]
        xc = pick(X, c); D = pick(DL, c & (ND - 1))
        y = pick(X, ((D * ub >> SH) + D + KS * k) & (W - 1))
        h = pick(X, ((R * ub >> SH) + R + KS * k) & (W - 1))
        jump = np.add.reduce(np.abs(y[:, :, :, 1:] - y[:, :, :, :-1]), axis=2)
        f = np.min(np.where((jump > sb) & (k[1:] > nb), k[1:], 16), axis=2); fb = f[:, :, None]
        meet = (np.add.reduce(np.abs(y - h), axis=2) <= th) & (k >= nb) & (k < fb)
        a = np.min(np.where(meet, k, 16), axis=2); ab = a[:, :, None]
        found = a < 16; e = np.where(found, a, f - 1)
        ye = np.take_along_axis(y, e[:, :, None, None], 3)[:, :, :, 0]
        L = np.where((k >= nb) & (k < fb), D, L); L = np.where(k >= ab, R, L)
        done = found | (f == 16)
        R = np.where(done[:, :, None], L, R); n = np.where(done, 1 + (u & 3), f)
        z = (z + ye) >> 1
        ix = np.broadcast_to((WM * lane + (u & (WM - 1)))[:, :, None], (N, 8, 16, Q)); np.put_along_axis(X, ix, (xc + ye) >> 1, 3)
        ix = np.broadcast_to((DM * lane + (u & (DM - 1)))[:, :, None], (N, 8, 16, Q))
        np.put_along_axis(DL, ix, np.where(done[:, :, None], L, np.take_along_axis(DL, ix, 3)), 3)
        A = np.add.reduce(found.astype(np.int64).reshape(N, -1), axis=1).reshape(N, 1, 1, 1)
    return {"yl": bf(L.reshape(N, 128, Q)), "yr": bf(R.reshape(N, 128, Q)), "yd": bf(DL.reshape(N, 128, ND)), "yx": bf(X.reshape(N, 128, W)), "yz": bf(z.reshape(N, 128, Q)), "yn": n.astype(np.float32)}

@@ -1,0 +1,672 @@
+from concourse.mybir import AluOpType, ActivationFunctionType
+
+OP = AluOpType
+AF = ActivationFunctionType
+LANES, HALF, NQ, VISITS = 256, 128, 8, 5
+W, EXT, ND = 2048, 448, 1024
+MAGIC = 25165824.0
+
+GS, HS, YE = (128, 32), (64, -1), ("vs", "vs")
+NUDGE = {
+    "c": [-10, 0, -7, 0, -6, 0, 5, 4, 0, -4, 0, -5, 0, 1, 0, 4, -6, -2, 0, 2, 2, 1, 3, -4, 9, -4, 0, 1, 0, -6, -6, -3, 2, 3, 1, 1,
+          -2, 2, 2, 3, -1, 13, 10, -1, 3, 0, -10, 0, -8, 0, 0, 4, -2, 3, 0, -8, -3, -7, 8, 4, -1, 0, 0, -7, 16, 0, 0, -11, -9,
+          -1, 5, 1, 4, 11, -2, 0, 0, -4, 5, 7, -5, 2, -7, 0, 0, -1, 2, 2, -10, 0, -5, 0, 12, 6, -7, 0, 1, 0, -11, -5, 2, 2, 0,
+          -8, 0, 3, 6, -1, 0, 10, -4, 0, -3, 1, 4, 4, -5, 1, 3, -5, -7, -5, 8, -2, -8, -1],
+    "e0": [5, 0, -1, -2, 0, 6, -2, 0, 0, 1, -1, 9, -5],
+    "f0": [7, -1, 0, 1, 0, 5, 0, 8, 0, -2, 2, 6, -4, -2, 2, 16, -6, -1, 10, -4, -5, -3, 0, 0, 4, 6, 5, 1, 5, 8, 15, -1, -2, 10,
+           1, -5, 0, 2, -3, 2, 9, -6, 0, 0, 0, -9, 0, -1, 0, -9, 14, -3],
+    "f1": [5, 1, 0, 10, 3, 0, 0, 4, -14, -6, -5, 0, -10, 6, -7, -10, -7, -5, -8, -13, -3, 0, -2, 6, -3, -1, 0, -3, -3, -9, 5, 11,
+           2, 0, 12, 0, 1, -7, -10, -4, 0, -3, 0, 7, -2, 0, -1, -8, -6, 3, 7],
+    "t0": [0, -14, -3, 1, 2, -7, -7, 0, 2, 0, 0, -7, -4, 1, -3, -2, 0, 0, -9, 4, 0, 4, -3, -8, -4, 0, 0, 15, 8, -3, -10, 2],
+    "t1": [-1, 5, 3, -2, 0, -7, -4, -1, 10, 2, 4, 2, 0, 0, 0, 0, -1, 5, 0, 1, 0, 9, -3, 0, -3, 9, 0, 3],
+    "u0": [11, 14, 5, 4, 0, 0, 12, 11, -4, -6, -16, 0, 0, 9],
+    "u1": [5, 11, 5, 0, 0, 1, 2, 4, 2, 2, 14, 2, -3, -2],
+    "w0": [9, -8, -9, -4],
+}
+
+SCRATCH = {
+    "pi": ("sbuf", [128, 8448], "int32"), "pf": ("sbuf", [128, 3072], "float32"),
+    "pb": ("sbuf", [128, 52000], "bfloat16"), "pu": ("sbuf", [128, 2048], "uint16"),
+    "xs": ("sbuf", [128, W + EXT], "bfloat16"), "dn": ("sbuf", [128, 2 * ND], "bfloat16"),
+    "zed0": ("sbuf", [128, LANES], "bfloat16"), "rend0": ("sbuf", [128, LANES], "bfloat16"),
+    "lend0": ("sbuf", [128, LANES], "bfloat16"), "cnt0": ("sbuf", [8, LANES], "int32"),
+    "kap0": ("sbuf", [128, 1], "int32"), "wt0": ("sbuf", [128, 1], "int32"), "lim0": ("sbuf", [8, 2], "int32"),
+    "yn0": ("sbuf", [8, LANES], "float32"), "yz0": ("sbuf", [128, LANES], "bfloat16"),
+}
+SEMAPHORES = ["sv", "ss", "st", "sg", "zsent", "rsent"]
+for _i in range(8):
+    SCRATCH["ps%d" % _i] = ("psum", [128, 512], "float32")
+for _i in range(24):
+    SEMAPHORES.append("dma%d" % _i)
+for _t in range(VISITS):
+    for _b in range(2):
+        SCRATCH["zo%d%d" % (_t, _b)] = ("sbuf", [128, HALF], "bfloat16")
+        SCRATCH["ro%d%d" % (_t, _b)] = ("sbuf", [128, 3 * HALF], "bfloat16")
+        if _t < VISITS - 1:
+            SCRATCH["zi%d%d" % (_t, _b)] = ("sbuf", [128, HALF], "bfloat16")
+            SCRATCH["ri%d%d" % (_t, _b)] = ("sbuf", [128, 3 * HALF], "bfloat16")
+            SEMAPHORES.append("az%d%d" % (_t, _b))
+            SEMAPHORES.append("ar%d%d" % (_t, _b))
+
+
+def relays(topo, cores, q):
+    src, dst = cores[q], cores[(q + 1) % len(cores)]
+    c = [h for h in topo.cores_of(src) if h not in cores and topo.die(h) == topo.die(src)
+         and topo.may_write(src, h) and topo.may_write(h, dst)]
+    return c[0], c[1 % len(c)]
+
+
+def relay_program(g, core, T, topo, dst, src, kinds):
+    n_in = len(topo.engines(src, core))
+    n_out = len(topo.engines(core, dst))
+    rid, pid = topo.addr(dst, core)
+    sent = {"z": 0, "r": 0}
+    for t in range(VISITS - 1):
+        for b in range(2):
+            for k in kinds:
+                g.wait_ge(T.sem["a%s%d%d" % (k, t, b)], n_in)
+                buf = T["%si%d%d" % (k, t, b)]
+                g.remote_dma(buf[:], buf[:], T.sem["a%s%d%d" % (k, t, b)], T.sem[k + "sent"], pid, rid, topo.mask(core, dst))
+                sent[k] += n_out
+    for k in kinds:
+        g.wait_ge(T.sem[k + "sent"], sent[k])
+
+
+def rank_program(g, core, T, topo):
+    rank = T.rank_of(core)
+    cores = list(T.cores)
+    if rank is None:
+        for q in range(len(cores)):
+            rl = relays(topo, cores, q)
+            if core in rl:
+                kinds = [k for k, h in zip("zr", rl) if h == core]
+                relay_program(g, core, T, topo, cores[(q + 1) % len(cores)], cores[q], kinds)
+        return
+
+    ops, acc, used = [], {}, {"pi": 0, "pf": 0, "pb": 0, "pu": 0}
+    SIZE = {"pi": 4, "pf": 4, "pb": 2, "pu": 2}
+
+    def alloc(pool, n):
+        lo = used[pool]
+        used[pool] = lo + -(-n // 16) * 16
+        return (pool, lo, lo + n, 1)
+
+    def sub(t, a, b, s=1):
+        return (t[0], t[1] + a, t[1] + b, s)
+
+    def whole(name, n):
+        return (name, 0, n, 1)
+
+    def ap(t, rows=128):
+        buf = T[t[0]]
+        if rows < 128:
+            return buf[0:rows, t[1]:t[2]]
+        return buf[:, t[1]:t[2]] if t[3] == 1 else buf[:, t[1]:t[2]:t[3]]
+
+    def cnt(t):
+        return -(-(t[2] - t[1]) // t[3])
+
+    def size(t):
+        return 4 if t[0][:2] == "ps" else SIZE.get(t[0], 2)
+
+    stage, seq = ["c"], {}
+
+    def op(eng, fns, reads, writes, dur, done=None, lat=0.0, extra=()):
+        me = len(ops)
+        place = seq[stage[0]] = seq.get(stage[0], -1) + 1
+        nudge = NUDGE.get(stage[0][:2], [])
+        deps = set(extra)
+        for regs, wr in ((reads, False), (writes, True)):
+            for name, lo, hi, _s in regs:
+                bank = name[:2] == "ps"
+                if bank:
+                    lo, hi = 0, 512
+                keep = []
+                for (a, b, o, w_) in acc.get(name, []):
+                    if o != me and a < hi and lo < b and (wr or w_ or bank):
+                        deps.add(o)
+                    if o == me or not ((wr or bank) and lo <= a and b <= hi):
+                        keep.append((a, b, o, w_))
+                keep.append((lo, hi, me, wr or bank))
+                acc[name] = keep
+        ops.append(dict(eng=eng, fns=fns, deps=deps, dur=dur, done=done, lat=lat, cls=(stage[0][:2], place),
+                        bias=nudge[place] if place < len(nudge) else 0))
+        return me
+
+    CY, GF = 0.00083, 1.5
+
+    def vd(cyc):
+        return 0.06 + CY * max(64, cyc)
+
+    def fast(*tiles):
+        return 0.5 if all(size(t) == 2 for t in tiles) else 1
+
+    def tt(out, a, b, o):
+        c = 1 if "ps" in (a[0][:2], b[0][:2]) else 2
+        return op("v", [lambda: g.vector.tensor_tensor(ap(out), ap(a), ap(b), o)], [a, b], [out], vd(c * cnt(out)))
+
+    def ts(out, a, s1, o1, s2=None, o2=None):
+        def val(s):
+            return ap(s) if isinstance(s, tuple) else s
+
+        def call():
+            if o2 is None:
+                return g.vector.tensor_scalar(ap(out), ap(a), val(s1), None, o1)
+            return g.vector.tensor_scalar(ap(out), ap(a), val(s1), val(s2), o1, o2)
+        return op("v", [call], [a] + [s for s in (s1, s2) if isinstance(s, tuple)], [out], vd(fast(out, a) * cnt(out)))
+
+    def cp(out, a, rows=128):
+        return op("v", [lambda: g.vector.tensor_copy(ap(out, rows), ap(a, rows))], [a], [out], vd(fast(out, a) * cnt(out)))
+
+    def fill(out, v):
+        return op("v", [lambda: g.vector.memset(ap(out), v)], [], [out], vd(cnt(out) * size(out) / 4))
+
+    def act(out, a, f, scale=1.0, bias=0.0, accum=None):
+        def call():
+            kw = {}
+            if scale != 1.0:
+                kw["scale"] = scale
+            if isinstance(bias, tuple):
+                kw["bias"] = ap(bias)
+            elif bias != 0.0:
+                kw["bias"] = bias
+            if accum is not None:
+                kw["accum_out"] = ap(accum)
+            return g.scalar.activation(ap(out), ap(a), f, **kw)
+        rd = [a] + ([bias] if isinstance(bias, tuple) else [])
+        return op("s", [call], rd, [out] + ([accum] if accum else []), 0.08 + CY * cnt(out))
+
+    def win(a, off):
+        return T[a[0]][:, a[1]:a[2]].indirect(ap(off))
+
+    def gat(eng, out, a, off):
+        n = cnt(out)
+        if eng == "v":
+            return op("v", [lambda: g.vector.tensor_copy(ap(out), win(a, off))], [a, off], [out], 0.05 + CY * GF * n)
+        return op("s", [lambda: g.scalar.activation(ap(out), win(a, off), AF.Copy)], [a, off], [out], 0.065 + CY * GF * n)
+
+    def gat2(split, out, st, a, off, w):
+        if split < w:
+            gat("v", sub(out, 16 * st * split, 16 * st * w, st), a, sub(off, split, w))
+        if split:
+            gat("s", sub(out, 0, 16 * st * split, st), a, sub(off, 0, split))
+
+    def gtt(out, a, off, b, o):
+        return op("v", [lambda: g.vector.tensor_tensor(ap(out), win(a, off), ap(b), o)], [a, off, b], [out],
+                  0.05 + CY * GF * cnt(out))
+
+    def scat(a, off, src):
+        return op("v", [lambda: g.vector.tensor_copy(win(a, off), ap(src))], [src, off], [a], 0.05 + CY * 3.8 * cnt(src))
+
+    def mm(groups, keep_open=False, cont=False, k8=False, m8=False):
+        fns, rd, wr, cyc = [], [], [], 0
+        for out, pairs in groups:
+            for j, (l, r) in enumerate(pairs):
+                o_ = out
+                if len(r) == 2:
+                    o_, r = r
+                start, stop = j == 0 and not cont, j == len(pairs) - 1 and not keep_open
+
+                def call(o_=o_, l=l, r=r, start=start, stop=stop):
+                    return g.tensor.matmul(ap(o_, 8 if m8 else 128), ap(l, 8 if k8 else 128), ap(r, 8 if k8 else 128), start, stop)
+                fns.append(call)
+                rd += [l, r]
+                wr.append(o_)
+                cyc += max(64, cnt(r)) * (4 if size(l) == 4 else 1)
+        return op("t", fns, list(dict.fromkeys(rd)), list(dict.fromkeys(wr)), 0.05 + cyc * 0.00042)
+
+    def gps(fn, rd, wr, dur):
+        return op("g", [fn], rd, wr, dur)
+
+    n_dma = [0]
+
+    def dma(out_ap, in_ap, rd, wr, eng="y", dur=2.5):
+        sem = "dma%d" % n_dma[0]
+        n_dma[0] += 1
+        q = g.sync if eng == "y" else g.scalar
+        return op(eng, [lambda: q.dma_start(out_ap, in_ap)], rd, wr, 0.1, done=(sem, 16), lat=dur)
+
+    xs, dn = whole("xs", W + EXT), whole("dn", ND)
+    zed0, rend0, lend0 = whole("zed0", LANES), whole("rend0", LANES), whole("lend0", LANES)
+    dma(T.zed0[:], T.zed[:], [], [zed0])
+    dma(T.wt0[:], T.wt[:], [], [whole("wt0", 1)], "s")
+    dma(T.kap0[:], T.kap[:], [], [whole("kap0", 1)], "s")
+    dma(T.xs[:, 0:W], T.stock[:], [], [sub(xs, 0, W)], dur=4.0)
+    dma(T.xs[:, W:W + EXT], T.stock[:, 0:EXT], [], [sub(xs, W, W + EXT)])
+    dma(T.rend0[:], T.rend[:], [], [rend0])
+    dma(T.cnt0[:], T.cnt[:], [], [whole("cnt0", LANES)])
+    dma(T.lim0[:], T.lim[:], [], [whole("lim0", 2)])
+    dma(T.dn[:, 0:ND], T.donor[:], [], [dn], dur=3.0)
+    dma(T.lend0[:], T.lend[:], [], [lend0])
+
+    ones = alloc("pb", 128)
+    fill(ones, 1.0)
+    bo1, BO, ID, TRI, TRS = [alloc("pb", 128) for _ in range(5)]
+
+    def sel(out, a, pattern, cmp_, base, cm):
+        gps(lambda: g.affine_select(ap(out), ap(a), pattern, cmp_, 0.0, base, cm), [a], [out], 0.4)
+    sel(bo1, ones, [[-16, 8], [0, 16]], OP.is_ge, 0, 1)
+    sel(BO, bo1, [[16, 8], [0, 16]], OP.is_ge, 15, -1)
+    pidx, q16 = alloc("pi", 1), alloc("pi", 16)
+    gps(lambda: g.iota(ap(pidx), [[0, 1]], 0, 1), [], [pidx], 0.15)
+    gps(lambda: g.iota(ap(q16), [[16, 16]], 0, 0), [], [q16], 0.2)
+    sel(ID, ones, [[-1, 128]], OP.is_equal, 0, 1)
+    mq = alloc("pf", 128)
+    gps(lambda: g.iota(ap(mq), [[1, 16], [0, NQ]], 0, 0, allow_small_or_imprecise_dtypes=True), [], [mq], 0.4)
+    sel(TRI, BO, [[1, 128]], OP.is_ge, 0, -1)
+    sel(TRS, BO, [[1, 128]], OP.is_ge, 1, -1)
+
+    wtf, kapf, kc, k29, k256, nbias = [alloc("pf", 1) for _ in range(6)]
+    ts(wtf, whole("wt0", 1), 0.5, OP.mult)
+    WB = alloc("pb", 128)
+    ts(WB, BO, wtf, OP.mult)
+    EA, FA, WA = alloc("pb", 2048), alloc("pb", 2048), alloc("pb", 2048)
+    fill(WA, 0.0)
+
+    def col8(t, r, k):
+        return sub(t, 128 * r + k, 128 * r + 128, 16)
+    cp(kapf, whole("kap0", 1))
+    kci = alloc("pi", 1)
+    ts(kci, pidx, 15, OP.bitwise_and)
+    cp(kc, kci)
+    ts(k29, kci, 29.0, OP.mult)
+    for r in range(16):
+        if r % 2:
+            act(col8(WA, r, r), sub(WB, r, 128, 16), AF.Copy)
+        else:
+            cp(col8(WA, r, r), sub(WB, r, 128, 16))
+    zz = {}
+    for b in range(2):
+        zz[b] = alloc("pb", HALF)
+        act(zz[b], sub(zed0, b * HALF, (b + 1) * HALF), AF.Copy, scale=2.0)
+    nID, hID, mB, pB, TRB, BOM, I64, pS, nS = [alloc("pb", 128) for _ in range(9)]
+    ts(nID, ID, -1.0, OP.mult)
+    ts(hID, ID, -0.5, OP.mult)
+    ts(k256, kci, 256.0, OP.mult)
+    KD1, KD2 = alloc("pb", 128), alloc("pb", 128)
+    ts(KD1, mq, kc, OP.is_equal, kapf, OP.mult)
+    ts(KD2, mq, kc, OP.is_equal, k256, OP.mult)
+    fill(EA, 0.0)
+    for r in range(16):
+        act(col8(EA, r, r), sub(BO, r, 128, 16), AF.Copy)
+    il, l8c = alloc("pi", 16), alloc("pi", 16)
+    l32, l4c, neg = alloc("pb", 16), alloc("pb", 16), alloc("pb", NQ)
+    fill(neg, -1.0)
+    ts(il, q16, kc, OP.add)
+    ts(l32, il, 32.0, OP.mult)
+    ts(l8c, il, 8.0, OP.mult)
+    ts(l4c, il, 4.0, OP.mult)
+    fill(FA, 0.0)
+    for k in range(16):
+        act(col8(FA, k, k), sub(BO, k, 128, 16), AF.Copy, scale=-0.5)
+        if k < 15:
+            act(col8(FA, k, k + 1), sub(BO, k, 128, 16), AF.Copy, scale=0.5)
+    fill(sub(mB, 0, 1), 0.0)
+    ts(sub(mB, 1, 128), sub(ID, 0, 127), -8192.0, OP.mult)
+    ts(pB, ID, 8192.0, OP.mult)
+    ts(TRB, TRI, 8192.0, OP.mult)
+    ts(BOM, BO, -1048576.0, OP.mult)
+    ts(pS, ID, 0.015625, OP.mult)
+    ts(nS, ID, -0.015625, OP.mult)
+    ts(I64, ID, 64.0, OP.mult)
+    ts(nbias, kc, 14.5, OP.is_lt, 2.0, OP.mult)
+    o16 = alloc("pf", 128)
+    fill(o16, 0.0625)
+    cntb, limf, b8b, b8f, nB0 = alloc("pb", LANES), alloc("pf", 2), alloc("pb", 128), alloc("pf", 128), alloc("pb", LANES)
+    cp(cntb, whole("cnt0", LANES), rows=8)
+    cp(limf, whole("lim0", 2), rows=8)
+    gps(lambda: g.affine_select(ap(b8b, 8), ap(ones, 8), [[1, 8], [0, 16]], OP.is_equal, 0.0, 0, -1), [ones], [b8b], 0.4)
+    cp(b8f, b8b, rows=8)
+    mm([(("ps7", 0, LANES, 1), [(b8b, cntb)])], k8=True)
+    ts(nB0, ("ps7", 0, LANES, 1), kc, OP.is_gt)
+    mm([(("ps7", 0, 2, 1), [(b8f, limf)])], k8=True)
+    thc, sbc = alloc("pf", 1), alloc("pf", 1)
+    act(thc, ("ps7", 0, 1, 1), AF.Copy, bias=1.0)
+    act(sbc, ("ps7", 1, 2, 1), AF.Copy, scale=-1.0)
+    G8 = alloc("pb", 8)
+    cp(G8, sub(BO, 0, 128, 16))
+
+    H16, w = 16 * HALF, HALF
+    Gb, Hb, ADb, AD2, ZY, REL = [[alloc("pb", n) for _ in range(2)] for n in (H16, H16, H16, H16, 2 * H16, 2 * H16)]
+    for b in range(2):
+        fill(ZY[b], 0.0)
+    par = {}
+
+    def til(pool, n, key, t, b):
+        k = (key, t % 2, b)
+        if k not in par:
+            par[k] = alloc(pool, n)
+        return par[k]
+    A0 = alloc("pf", 1)
+    fill(A0, 0.0)
+    accs = [alloc("pf", 2) for _ in range(2)]
+    state = {b: dict(z2=zz[b], R=sub(rend0, b * w, (b + 1) * w), L=sub(lend0, b * w, (b + 1) * w),
+                     n=sub(nB0, b * w, (b + 1) * w)) for b in range(2)}
+
+    def E(k):
+        return sub(EA, 128 * k, 128 * k + 128)
+
+    def F(k):
+        return sub(FA, 128 * k, 128 * k + 128)
+
+    def ps(bank, a, b):
+        return ("ps%d" % bank, a, b, 1)
+
+    def front(t, b, A):
+        s = state[b]
+        BS, BM = 4 + 2 * b, 5 + 2 * b
+
+        def ti(key, n=w):
+            return til("pi", n, key, t, b)
+        z2 = s["z2"]
+        UW = w + NQ
+        U = ps(BS, 0, UW)
+        mm([(ps(BS, 0, w), [(WB, z2)]),
+            (ps(BS, w, UW), [(sub(WA, 128 * r, 128 * r + 128), sub(z2, r, w, 16)) for r in range(16)])])
+        ui, u, uu, s1 = [ti(k, UW) for k in ("ui", "u", "uu", "s1")]
+        u4 = ti("u4")
+        s3, c = ti("s3"), ti("c")
+        s2 = ps(BS, 256, 256 + w)
+        cl = til("pu", w, "cl", t, b)
+        cp(ui, U)
+        ts(u, ui, 4095, OP.bitwise_and)
+        uA, ul, sA, sl = sub(u, 0, w), sub(u, w, UW), sub(s1, 0, w), sub(s1, w, UW)
+        tt(uu, u, u, OP.mult)
+        ts(s2, uA, kapf, OP.mult, A, OP.add)
+        ts(s1, uu, 5, OP.arith_shift_right)
+        tt(s3, sA, s2, OP.add)
+        ts(c, s3, 2047, OP.bitwise_and)
+        cp(cl, c)
+        gat2(GS[b], Gb[b], 1, sub(xs, 0, W), cl, w)
+        up, pr, pr2 = til("pf", w, "up", t, b), ti("pr"), ti("pr2")
+        hl = til("pu", w, "hl", t, b)
+        ts(up, uA, 32.0, OP.add)
+        tt(pr, s["R"], up, OP.mult)
+        ts(pr2, pr, 5, OP.arith_shift_right, 2047, OP.bitwise_and)
+        ts(hl, pr2, k29, OP.add)
+        if HS[b] >= 0:
+            gat2(HS[b], Hb[b], 1, xs, hl, w)
+        s1a, x8, l8 = [ti(k, NQ) for k in ("s1a", "x8", "l8")]
+        l8u = til("pu", NQ, "l8u", t, b)
+        ts(s1a, sl, A, OP.add)
+        ts(x8, ul, 7, OP.bitwise_and)
+        tt(l8, x8, sub(l8c, 0, NQ), OP.add)
+        cp(l8u, l8)
+        ts(u4, uA, 3, OP.bitwise_and)
+        ku = til("pb", w, "ku", t, b)
+        ts(ku, u4, kc, OP.is_ge)
+        zm = til("pf", w, "zm", t, b)
+        act(zm, z2, AF.Copy, scale=0.5, bias=-0.5)
+        k0 = til("pf", 8 * NQ, "k0", t, b)
+        for mc in range(4):
+            D = 2 * b + mc % 2
+            mm([(ps(D, j * w, (j + 1) * w), [(ID, sub(Gb[b], 4 * mc + j, H16, 16)), (hID, z2)]) for j in range(4)])
+            act(sub(ADb[b], mc * 4 * w, (mc + 1) * 4 * w), ps(D, 0, 512), AF.Abs, scale=4096.0)
+            if mc % 2 == 1:
+                h = mc // 2
+                K = ps(BS if h == 0 else BM, 0, 8 * NQ)
+                mm([(K, [(BO, sub(KD1, 64 * h, 64 * h + 64)), (BO, sub(KD2, 64 * h, 64 * h + 64))]
+                     + [(E(r), sub(ADb[b], h * 8 * w + r, (h + 1) * 8 * w, 16)) for r in range(16)])])
+                if h == 0:
+                    act(k0, K, AF.Copy)
+        t1, t2, t3 = [til("pf", n, "tm%d" % n, t, b) for n in (64, 32, 16)]
+        vi, ka, pa, pc, cd, cx = [ti(k, NQ) for k in ("vi", "ka", "pa", "pc", "cd", "cx")]
+        cdu, cxu = til("pu", NQ, "cdu", t, b), til("pu", NQ, "cxu", t, b)
+        tt(t1, ps(BM, 0, 64), k0, OP.min)
+        tt(t2, sub(t1, 0, 32), sub(t1, 32, 64), OP.min)
+        tt(t3, sub(t2, 0, 16), sub(t2, 16, 32), OP.min)
+        tt(vi, sub(t3, 0, 8), sub(t3, 8, 16), OP.min)
+        ts(ka, vi, 255, OP.bitwise_and)
+        tt(pa, ka, ul, OP.mult)
+        tt(pc, pa, s1a, OP.add)
+        ts(cd, pc, 1023, OP.bitwise_and)
+        cp(cdu, cd)
+        P, P2 = ti("P"), ti("P2")
+        yl = til("pu", w, "yl", t, b)
+        gtt(P, dn, cdu, up, OP.mult)
+        ts(P2, P, 5, OP.arith_shift_right, 2047, OP.bitwise_and)
+        ts(yl, P2, k29, OP.add)
+        ts(cx, pc, 2047, OP.bitwise_and)
+        cp(cxu, cx)
+        Dk, xc = til("pb", w, "Dk", t, b), til("pb", w, "xc", t, b)
+        for h in range(2):
+            gat(YE[b][h], sub(ZY[b], h * H16, (h + 1) * H16, 2), xs, sub(yl, h * w // 2, (h + 1) * w // 2))
+        gat("s", Dk, dn, cdu)
+        gat("s", xc, sub(xs, 0, W), cxu)
+        s.update(hl=hl, zm=zm, Dk=Dk, xc=xc, ku=ku, l8u=l8u)
+
+    def tail(t, b):
+        s = state[b]
+        BS, BM = 4 + 2 * b, 5 + 2 * b
+        z, H, rel = ZY[b], Hb[b], REL[b]
+        fused = HS[b] < 0
+
+        def tb(key):
+            return til("pb", w, key, t, b)
+        J, M, e = ps(BS, 0, w), ps(BM, 0, w), w // 2
+        for h in range(2):
+            lo, hi = h * H16, (h + 1) * H16
+            op("v", [lambda lo=lo, hi=hi: g.vector.tensor_tensor_scan(
+                ap(sub(rel, lo, hi - 1)), ap(sub(z, lo + 1, hi)), ap(sub(z, lo, hi - 1)), 0.0, OP.subtract, OP.max)],
+               [sub(z, lo, hi)], [sub(rel, lo, hi - 1)], vd(0.5 * H16))
+            if fused:
+                gtt(sub(H, lo // 2, hi // 2), xs, sub(s["hl"], h * e, (h + 1) * e), sub(z, lo, hi, 2), OP.subtract)
+                act(sub(AD2[b], lo // 2, hi // 2), sub(H, lo // 2, hi // 2), AF.Abs)
+            for kq in range(0 if fused else 2):
+                D = 2 * b + kq
+                mm([(ps(D, j * e, (j + 1) * e), [(ID, sub(z, lo + 2 * (8 * kq + j), hi, 32)),
+                                                 (nID, sub(H, lo // 2 + 8 * kq + j, hi // 2, 16))]) for j in range(8)])
+                act(sub(AD2[b], lo // 2 + kq * 512, lo // 2 + (kq + 1) * 512), ps(D, 0, 512), AF.Abs)
+            jh, mh = sub(J, h * e, (h + 1) * e), sub(M, h * e, (h + 1) * e)
+            mm([(jh, ([(mB, (J, s["n"]))] if h == 0 else [])
+                 + [(F(k), sub(z, lo + 2 * k, hi, 32)) for k in range(16)]
+                 + [(E(k), sub(rel, lo + 2 * k - 1, hi - 1, 32)) for k in range(1, 16)])], keep_open=h == 0, cont=h == 1)
+            mm([(mh, ([(pB, (M, s["n"]))] if h == 0 else [])
+                 + [(E(k), sub(AD2[b], lo // 2 + k, hi // 2, 16) if fused else
+                     sub(AD2[b], lo // 2 + k * e, lo // 2 + (k + 1) * e)) for k in range(16)])], keep_open=True, cont=h == 1)
+        jm, me, ne = tb("jm"), tb("me"), tb("ne")
+        act(jm, J, AF.Relu, scale=2.0, bias=sbc)
+        mm([(M, [(TRB, jm)])], cont=True)
+        act(me, M, AF.Relu, scale=-1.0, bias=thc)
+        mm([(ps(BS, 0, w), [(TRI, me), (TRS, jm)])])
+        act(ne, ps(BS, 0, w), AF.Relu, scale=-2.0, bias=nbias)
+        mm([(ps(BM, 0, NQ), [(ID, sub(l32, 0, NQ))] + [(E(r), sub(ne, r, w, 16)) for r in range(16)])])
+        yel = til("pu", NQ, "yel", t, b)
+        cp(yel, ps(BM, 0, NQ))
+        sz = til("pf", w, "sz", t, b)
+        zo = whole("zo%d%d" % (t, b), w)
+        gtt(sz, z, yel, s["zm"], OP.add)
+        ts(zo, sz, MAGIC, OP.add, MAGIC, OP.subtract)
+        if t < VISITS - 1:
+            send("z", t, b, zo)
+        sx, sx2 = til("pi", w, "sx", t, b), til("pi", w, "sx2", t, b)
+        gtt(sx, z, yel, s["xc"], OP.add)
+        ts(sx2, sx, 1, OP.arith_shift_right)
+        mm([(ps(BS, 0, w), [(BO, me)]), (ps(BS, w, 2 * w), [(BO, jm), (BOM, me)]), (ps(BS, 2 * w, 3 * w), [(TRI, me)]),
+            (ps(BS, 3 * w, 4 * w), [(TRI, jm), (I64, s["n"])])])
+        an, nm2, m1, nd6 = tb("an"), tb("nm2"), tb("m1"), tb("nd6")
+        act(an, ps(BS, 0, w), AF.Sign, accum=sub(accs[t % 2], b, b + 1))
+        act(m1, ps(BS, 3 * w, 4 * w), AF.Relu, scale=-1.0, bias=1.0)
+        act(nm2, ps(BS, 2 * w, 3 * w), AF.Relu, scale=-1.0, bias=1.0)
+        ts(nd6, ps(BS, w, 2 * w), 0.5, OP.is_gt, 64.0, OP.mult)
+        s.update(sx2=sx2, nd6=nd6, m1=m1, nm2=nm2)
+
+    def count(t):
+        A = ps(6, 0, 1)
+        mm([(A, [(o16, sub(accs[t % 2], b, b + 1)) for b in range(2)])])
+        ac = til("pf", 1, "A", t, 0)
+        act(ac, A, AF.Copy)
+        return ac
+
+    def writes_x(t, b):
+        scat(sub(xs, b * W // 2, (b + 1) * W // 2), state[b]["l8u"], state[b]["sx2"])
+        if b == 0 and t < VISITS - 1:
+            cp(sub(xs, W, W + EXT), sub(xs, 0, EXT))
+
+    def update(t, b):
+        s = state[b]
+        BS, BM = 4 + 2 * b, 5 + 2 * b
+
+        def tb(key):
+            return til("pb", w, key, t, b)
+        tl, Q, Q2 = [tb(k) for k in ("tl", "Q", "Q2")]
+        r3 = til("pb", 4 * w, "r3", t, b)
+        L, R = s["L"], s["R"]
+        mm([(ps(BM, 0, w), [(ID, s["Dk"]), (nID, L)])])
+        mm([(ps(BS, 0, w), [(nID, ones), (ID, s["n"]), (ID, s["m1"]), (pS, s["nd6"])]),
+            (ps(BS, w, 2 * w), [(ID, s["ku"]), (nS, s["nd6"])]), (ps(BS, 2 * w, 3 * w), [(ID, s["nm2"]), (nS, s["nd6"])]),
+            (ps(BS, 3 * w, 4 * w), [(ID, s["ku"]), (ID, s["nd6"])])])
+        act(r3, ps(BS, 0, 4 * w), AF.Relu)
+        tt(tl, s["m1"], ps(BM, 0, w), OP.mult)
+        mm([(ps(BM, 0, w), [(ID, tl), (ID, L), (nID, R)])])
+        tt(Q, s["nm2"], ps(BM, 0, w), OP.mult)
+        tt(Q2, sub(r3, 2 * w, 3 * w), ps(BM, 0, w), OP.mult)
+        mm([(ps(BM, 0, w), [(ID, R), (ID, Q2)]), (ps(BM, w, 2 * w), [(ID, sub(r3, 0, w)), (ID, sub(r3, w, 2 * w))]),
+            (ps(BM, 2 * w, 3 * w), [(ID, R), (ID, Q)])])
+        ro = whole("ro%d%d" % (t, b), 3 * w)
+        act(ro, ps(BM, 0, 3 * w), AF.Copy)
+        if t < VISITS - 1:
+            send("r", t, b, ro)
+        mm([(ps(BS, 0, NQ), [(ID, sub(l4c, b * NQ, (b + 1) * NQ)), (ID, neg)]
+             + [(E(r), sub(r3, 3 * w + r, 4 * w, 16)) for r in range(16)])])
+        dlu = til("pu", NQ, "dlu", t, b)
+        cp(dlu, ps(BS, 0, NQ))
+        scat(whole("dn", 2 * ND), dlu, sub(ro, 2 * w, 3 * w))
+
+    snt = {"z": 0, "r": 0}
+
+    def send(k, t, b, tile):
+        dst = relays(topo, cores, rank)["zr".index(k)]
+        rid, pid = topo.addr(dst, core)
+        m = topo.mask(core, dst)
+        snt[k] += len(topo.engines(core, dst))
+        name = "%s%d%d" % (k, t, b)
+        o = op("g", [lambda: g.remote_dma(T[k + "i" + name[1:]][:], ap(tile), T.sem["a" + name], T.sem[k + "sent"], pid, rid, m)],
+               [tile], [], 1.0, done=(k + "sent", 0))
+        n = len(topo.engines(relays(topo, cores, (rank - 1) % len(cores))["zr".index(k)], core))
+        op(None, [], [], [whole(k + "i" + name[1:], cnt(tile))], 0.0, done=("a" + name, n), lat=4.0, extra=(o,))
+
+    A = A0
+    for t in range(VISITS):
+        for b in range(2):
+            stage[0] = "f%d%d" % (b, t)
+            front(t, b, A)
+        for b in range(2):
+            stage[0] = "t%d%d" % (b, t)
+            tail(t, b)
+        stage[0] = "w0%d" % t
+        A = count(t)
+        for b in range(2):
+            writes_x(t, b)
+        for b in range(2):
+            stage[0] = "u%d%d" % (b, t)
+            update(t, b)
+        stage[0] = "e0%d" % t
+        for b in range(2):
+            if t < VISITS - 1:
+                r = whole("ri%d%d" % (t, b), 3 * w)
+                state[b] = dict(z2=whole("zi%d%d" % (t, b), w), R=sub(r, 0, w), n=sub(r, w, 2 * w), L=sub(r, 2 * w, 3 * w))
+            else:
+                zo, r = whole("zo%d%d" % (t, b), w), whole("ro%d%d" % (t, b), 3 * w)
+                lo, hi = b * w, (b + 1) * w
+                act(sub(whole("yz0", LANES), lo, hi), zo, AF.Copy, scale=0.5)
+                dma(T.yz[:, lo:hi], T.yz0[:, lo:hi], [("yz0", lo, hi, 1)], [])
+                mm([(ps(4, 0, w), [(G8, sub(r, w, 2 * w))])], m8=True)
+                op("s", [lambda lo=lo, hi=hi: g.scalar.activation(T.yn0[:, lo:hi], T.ps4[0:8, 0:w], AF.Copy)],
+                   [ps(4, 0, w)], [("yn0", lo, hi, 1)], 0.2)
+                dma(T.yr[:, lo:hi], ap(sub(r, 0, w)), [r], [])
+                dma(T.yl[:, lo:hi], ap(sub(r, 2 * w, 3 * w)), [r], [])
+    dma(T.yn[:], T.yn0[:], [("yn0", 0, LANES, 1)], [])
+    for b in range(2):
+        lo, hi = b * W // 2, (b + 1) * W // 2
+        dma(T.yx[:, lo:hi], T.xs[:, lo:hi], [sub(xs, lo, hi)], [])
+    dma(T.yd[:], T.dn[:, 0:ND], [dn], [])
+
+    N = len(ops)
+    succ = [[] for _ in range(N)]
+    for i, o in enumerate(ops):
+        for d in o["deps"]:
+            succ[d].append(i)
+    prio = [0.0] * N
+    for i in range(N - 1, -1, -1):
+        prio[i] = ops[i]["dur"] + ops[i]["lat"] + max([prio[j] for j in succ[i]] + [0.0])
+    left = [len(o["deps"]) for o in ops]
+    ready = {e: [] for e in ("v", "s", "t", "g", "y", None)}
+    avail = [0.0] * N
+    free = {e: 0.0 for e in ready}
+    for i in range(N):
+        if left[i] == 0:
+            ready[ops[i]["eng"]].append(i)
+    order = []
+    while len(order) < N:
+        best = None
+        for e, lst in ready.items():
+            if lst:
+                st = max(free[e], min(avail[i] for i in lst)) if e is not None else min(avail[i] for i in lst)
+                if best is None or st < best[0]:
+                    best = (st, e)
+        st, e = best
+        i = max((j for j in ready[e] if avail[j] <= st + 1e-9), key=lambda j: prio[j] + ops[j]["bias"])
+        ready[e].remove(i)
+        end = st + ops[i]["dur"]
+        if e is not None:
+            free[e] = end
+        order.append((st, i))
+        for j in succ[i]:
+            left[j] -= 1
+            avail[j] = max(avail[j], end + ops[i]["lat"] + 0.06)
+            if left[j] == 0:
+                ready[ops[j]["eng"]].append(j)
+
+    QUEUE = {"v": g.vector, "s": g.scalar, "t": g.tensor, "g": g, "y": g.sync}
+    SEM = {"v": "sv", "s": "ss", "t": "st", "g": "sg"}
+    made = {k: 0 for k in SEM.values()}
+    know = {e: {} for e in QUEUE}
+    final = {}
+    for st, i in order:
+        o = ops[i]
+        e = o["eng"]
+        if e is None:
+            o["clock"], o["mark"] = {}, o["done"]
+            final[o["done"][0]] = o["done"][1]
+            continue
+        kn = know[e]
+        need = {}
+        for d in o["deps"]:
+            m = ops[d]["mark"]
+            if m is not None and kn.get(m[0], 0) < m[1]:
+                need[m[0]] = max(need.get(m[0], 0), m[1])
+        for d in sorted(o["deps"], reverse=True):
+            m = ops[d]["mark"]
+            if m is None or need.get(m[0], 0) != m[1]:
+                continue
+            for k, v in ops[d]["clock"].items():
+                if k != m[0] and k in need and need[k] <= v:
+                    need.pop(k)
+        for k in need:
+            QUEUE[e].wait_ge(T.sem[k], need[k])
+        for d in o["deps"]:
+            m = ops[d]["mark"]
+            if m is not None:
+                kn[m[0]] = max(kn.get(m[0], 0), m[1])
+                for k, v in ops[d]["clock"].items():
+                    kn[k] = max(kn.get(k, 0), v)
+        o["clock"] = dict(kn)
+        for f in o["fns"]:
+            ins = f()
+        if o["done"] is None:
+            made[SEM[e]] += 1
+            ins.then_inc(T.sem[SEM[e]], 1)
+            o["mark"] = (SEM[e], made[SEM[e]])
+        elif o["done"][1] == 16:
+            ins.then_inc(T.sem[o["done"][0]], 16)
+            o["mark"] = o["done"]
+            final[o["done"][0]] = 16
+        else:
+            o["mark"] = None
+    for k in SEM.values():
+        g.wait_ge(T.sem[k], made[k])
+    for k, v in final.items():
+        g.wait_ge(T.sem[k], v)
+    for k in ("z", "r"):
+        g.wait_ge(T.sem[k + "sent"], snt[k])

@@ -4,29 +4,18 @@ OP = AluOpType
 AF = ActivationFunctionType
 LANES, HALF, NQ, VISITS = 256, 128, 8, 5
 W, EXT, ND = 2048, 448, 1024
-MAGIC = 25165824.0
+M2, M4096 = 1.5 * 2 ** 24, 1.5 * 2 ** 35
+B = 256.0
 
-GS, HS, YE = (128, 32), (64, -1), ("vs", "vs")
-NUDGE = {
-    "c": [-10, 0, -7, 0, -6, 0, 5, 4, 0, -4, 0, -5, 0, 1, 0, 4, -6, -2, 0, 2, 2, 1, 3, -4, 9, -4, 0, 1, 0, -6, -6, -3, 2, 3, 1, 1,
-          -2, 2, 2, 3, -1, 13, 10, -1, 3, 0, -10, 0, -8, 0, 0, 4, -2, 3, 0, -8, -3, -7, 8, 4, -1, 0, 0, -7, 16, 0, 0, -11, -9,
-          -1, 5, 1, 4, 11, -2, 0, 0, -4, 5, 7, -5, 2, -7, 0, 0, -1, 2, 2, -10, 0, -5, 0, 12, 6, -7, 0, 1, 0, -11, -5, 2, 2, 0,
-          -8, 0, 3, 6, -1, 0, 10, -4, 0, -3, 1, 4, 4, -5, 1, 3, -5, -7, -5, 8, -2, -8, -1],
-    "e0": [5, 0, -1, -2, 0, 6, -2, 0, 0, 1, -1, 9, -5],
-    "f0": [7, -1, 0, 1, 0, 5, 0, 8, 0, -2, 2, 6, -4, -2, 2, 16, -6, -1, 10, -4, -5, -3, 0, 0, 4, 6, 5, 1, 5, 8, 15, -1, -2, 10,
-           1, -5, 0, 2, -3, 2, 9, -6, 0, 0, 0, -9, 0, -1, 0, -9, 14, -3],
-    "f1": [5, 1, 0, 10, 3, 0, 0, 4, -14, -6, -5, 0, -10, 6, -7, -10, -7, -5, -8, -13, -3, 0, -2, 6, -3, -1, 0, -3, -3, -9, 5, 11,
-           2, 0, 12, 0, 1, -7, -10, -4, 0, -3, 0, 7, -2, 0, -1, -8, -6, 3, 7],
-    "t0": [0, -14, -3, 1, 2, -7, -7, 0, 2, 0, 0, -7, -4, 1, -3, -2, 0, 0, -9, 4, 0, 4, -3, -8, -4, 0, 0, 15, 8, -3, -10, 2],
-    "t1": [-1, 5, 3, -2, 0, -7, -4, -1, 10, 2, 4, 2, 0, 0, 0, 0, -1, 5, 0, 1, 0, 9, -3, 0, -3, 9, 0, 3],
-    "u0": [11, 14, 5, 4, 0, 0, 12, 11, -4, -6, -16, 0, 0, 9],
-    "u1": [5, 11, 5, 0, 0, 1, 2, 4, 2, 2, 14, 2, -3, -2],
-    "w0": [9, -8, -9, -4],
-}
+OPT = dict(
+    gs=(64, 16),
+    runs=(((64, "s", "va"), (64, "s", "va")), ((64, "s", "va"), (64, "v", "va"))),
+    bias={},
+)
 
 SCRATCH = {
-    "pi": ("sbuf", [128, 8448], "int32"), "pf": ("sbuf", [128, 3072], "float32"),
-    "pb": ("sbuf", [128, 52000], "bfloat16"), "pu": ("sbuf", [128, 2048], "uint16"),
+    "pi": ("sbuf", [128, 6144], "int32"), "pf": ("sbuf", [128, 4096], "float32"),
+    "pb": ("sbuf", [128, 44000], "bfloat16"), "pu": ("sbuf", [128, 2048], "uint16"),
     "xs": ("sbuf", [128, W + EXT], "bfloat16"), "dn": ("sbuf", [128, 2 * ND], "bfloat16"),
     "zed0": ("sbuf", [128, LANES], "bfloat16"), "rend0": ("sbuf", [128, LANES], "bfloat16"),
     "lend0": ("sbuf", [128, LANES], "bfloat16"), "cnt0": ("sbuf", [8, LANES], "int32"),
@@ -36,15 +25,15 @@ SCRATCH = {
 SEMAPHORES = ["sv", "ss", "st", "sg", "zsent", "rsent"]
 for _i in range(8):
     SCRATCH["ps%d" % _i] = ("psum", [128, 512], "float32")
-for _i in range(24):
+for _i in range(28):
     SEMAPHORES.append("dma%d" % _i)
 for _t in range(VISITS):
     for _b in range(2):
         SCRATCH["zo%d%d" % (_t, _b)] = ("sbuf", [128, HALF], "bfloat16")
-        SCRATCH["ro%d%d" % (_t, _b)] = ("sbuf", [128, 3 * HALF], "bfloat16")
+        SCRATCH["ro%d%d" % (_t, _b)] = ("sbuf", [128, 5 * HALF], "bfloat16")
         if _t < VISITS - 1:
             SCRATCH["zi%d%d" % (_t, _b)] = ("sbuf", [128, HALF], "bfloat16")
-            SCRATCH["ri%d%d" % (_t, _b)] = ("sbuf", [128, 3 * HALF], "bfloat16")
+            SCRATCH["ri%d%d" % (_t, _b)] = ("sbuf", [128, 4 * HALF], "bfloat16")
             SEMAPHORES.append("az%d%d" % (_t, _b))
             SEMAPHORES.append("ar%d%d" % (_t, _b))
 
@@ -109,13 +98,11 @@ def rank_program(g, core, T, topo):
     def size(t):
         return 4 if t[0][:2] == "ps" else SIZE.get(t[0], 2)
 
-    stage, seq = ["c"], {}
+    stage = ["c"]
 
-    def op(eng, fns, reads, writes, dur, done=None, lat=0.0, extra=()):
+    def op(eng, fns, reads, writes, dur, done=None, lat=0.0, extra=(), cont=False):
         me = len(ops)
-        place = seq[stage[0]] = seq.get(stage[0], -1) + 1
-        nudge = NUDGE.get(stage[0][:2], [])
-        deps = set(extra)
+        deps, soft = set(extra), set()
         for regs, wr in ((reads, False), (writes, True)):
             for name, lo, hi, _s in regs:
                 bank = name[:2] == "ps"
@@ -124,16 +111,16 @@ def rank_program(g, core, T, topo):
                 keep = []
                 for (a, b, o, w_) in acc.get(name, []):
                     if o != me and a < hi and lo < b and (wr or w_ or bank):
-                        deps.add(o)
+                        (soft if cont and bank and ops[o]["eng"] == "t" else deps).add(o)
                     if o == me or not ((wr or bank) and lo <= a and b <= hi):
                         keep.append((a, b, o, w_))
                 keep.append((lo, hi, me, wr or bank))
                 acc[name] = keep
-        ops.append(dict(eng=eng, fns=fns, deps=deps, dur=dur, done=done, lat=lat, cls=(stage[0][:2], place),
-                        bias=nudge[place] if place < len(nudge) else 0))
+        ops.append(dict(eng=eng, fns=fns, deps=deps, after=deps | soft, dur=dur, done=done, lat=lat,
+                        bias=OPT["bias"].get(stage[0], 0)))
         return me
 
-    CY, GF = 0.00083, 1.5
+    CY, GF = 0.00083, 1.45
 
     def vd(cyc):
         return 0.06 + CY * max(64, cyc)
@@ -145,14 +132,14 @@ def rank_program(g, core, T, topo):
         c = 1 if "ps" in (a[0][:2], b[0][:2]) else 2
         return op("v", [lambda: g.vector.tensor_tensor(ap(out), ap(a), ap(b), o)], [a, b], [out], vd(c * cnt(out)))
 
-    def ts(out, a, s1, o1, s2=None, o2=None):
+    def ts(out, a, s1, o1, s2=None, o2=None, rows=128):
         def val(s):
             return ap(s) if isinstance(s, tuple) else s
 
         def call():
             if o2 is None:
-                return g.vector.tensor_scalar(ap(out), ap(a), val(s1), None, o1)
-            return g.vector.tensor_scalar(ap(out), ap(a), val(s1), val(s2), o1, o2)
+                return g.vector.tensor_scalar(ap(out, rows), ap(a, rows), val(s1), None, o1)
+            return g.vector.tensor_scalar(ap(out, rows), ap(a, rows), val(s1), val(s2), o1, o2)
         return op("v", [call], [a] + [s for s in (s1, s2) if isinstance(s, tuple)], [out], vd(fast(out, a) * cnt(out)))
 
     def cp(out, a, rows=128):
@@ -161,10 +148,16 @@ def rank_program(g, core, T, topo):
     def fill(out, v):
         return op("v", [lambda: g.vector.memset(ap(out), v)], [], [out], vd(cnt(out) * size(out) / 4))
 
-    def act(out, a, f, scale=1.0, bias=0.0, accum=None):
+    def scan(out, d0, d1, first):
+        return op("v", [lambda: g.vector.tensor_tensor_scan(ap(out), ap(d0), ap(d1), first, OP.min, OP.max)],
+                  [d0, d1], [out], vd(fast(out, d0, d1) * cnt(out)))
+
+    def act(out, a, f, scale=1.0, bias=0.0, accum=None, rows=128):
         def call():
             kw = {}
-            if scale != 1.0:
+            if isinstance(scale, tuple):
+                kw["scale"] = ap(scale)
+            elif scale != 1.0:
                 kw["scale"] = scale
             if isinstance(bias, tuple):
                 kw["bias"] = ap(bias)
@@ -172,8 +165,8 @@ def rank_program(g, core, T, topo):
                 kw["bias"] = bias
             if accum is not None:
                 kw["accum_out"] = ap(accum)
-            return g.scalar.activation(ap(out), ap(a), f, **kw)
-        rd = [a] + ([bias] if isinstance(bias, tuple) else [])
+            return g.scalar.activation(ap(out, rows), ap(a, rows), f, **kw)
+        rd = [a] + [s for s in (bias, scale) if isinstance(s, tuple)]
         return op("s", [call], rd, [out] + ([accum] if accum else []), 0.08 + CY * cnt(out))
 
     def win(a, off):
@@ -185,12 +178,6 @@ def rank_program(g, core, T, topo):
             return op("v", [lambda: g.vector.tensor_copy(ap(out), win(a, off))], [a, off], [out], 0.05 + CY * GF * n)
         return op("s", [lambda: g.scalar.activation(ap(out), win(a, off), AF.Copy)], [a, off], [out], 0.065 + CY * GF * n)
 
-    def gat2(split, out, st, a, off, w):
-        if split < w:
-            gat("v", sub(out, 16 * st * split, 16 * st * w, st), a, sub(off, split, w))
-        if split:
-            gat("s", sub(out, 0, 16 * st * split, st), a, sub(off, 0, split))
-
     def gtt(out, a, off, b, o):
         return op("v", [lambda: g.vector.tensor_tensor(ap(out), win(a, off), ap(b), o)], [a, off, b], [out],
                   0.05 + CY * GF * cnt(out))
@@ -198,21 +185,31 @@ def rank_program(g, core, T, topo):
     def scat(a, off, src):
         return op("v", [lambda: g.vector.tensor_copy(win(a, off), ap(src))], [src, off], [a], 0.05 + CY * 3.8 * cnt(src))
 
-    def mm(groups, keep_open=False, cont=False, k8=False, m8=False):
+    def mm(calls, start=True, stop=True, rows=128, out_rows=128, cont=False):
+        fns, rd, wr, cyc = [], [], [], 0
+        for j, (o_, l, r) in enumerate(calls):
+            def call(o_=o_, l=l, r=r, a=start and j == 0, z=stop and j == len(calls) - 1):
+                return g.tensor.matmul(ap(o_, out_rows), ap(l, rows), ap(r, rows), a, z)
+            fns.append(call)
+            rd += [l, r]
+            wr.append(o_)
+            cyc += max(min(64, cnt(l)), cnt(r)) * (4 if size(l) == 4 else 1)
+        return op("t", fns, list(dict.fromkeys(rd)), list(dict.fromkeys(wr)), 0.05 + cyc * 0.00042, cont=cont)
+
+    def sums(groups, **kw):
         fns, rd, wr, cyc = [], [], [], 0
         for out, pairs in groups:
             for j, (l, r) in enumerate(pairs):
                 o_ = out
                 if len(r) == 2:
                     o_, r = r
-                start, stop = j == 0 and not cont, j == len(pairs) - 1 and not keep_open
 
-                def call(o_=o_, l=l, r=r, start=start, stop=stop):
-                    return g.tensor.matmul(ap(o_, 8 if m8 else 128), ap(l, 8 if k8 else 128), ap(r, 8 if k8 else 128), start, stop)
+                def call(o_=o_, l=l, r=r, a=j == 0, z=j == len(pairs) - 1):
+                    return g.tensor.matmul(ap(o_, kw.get("out_rows", 128)), ap(l, kw.get("rows", 128)), ap(r, kw.get("rows", 128)), a, z)
                 fns.append(call)
                 rd += [l, r]
                 wr.append(o_)
-                cyc += max(64, cnt(r)) * (4 if size(l) == 4 else 1)
+                cyc += max(min(64, cnt(l)), cnt(r)) * (4 if size(l) == 4 else 1)
         return op("t", fns, list(dict.fromkeys(rd)), list(dict.fromkeys(wr)), 0.05 + cyc * 0.00042)
 
     def gps(fn, rd, wr, dur):
@@ -226,6 +223,9 @@ def rank_program(g, core, T, topo):
         q = g.sync if eng == "y" else g.scalar
         return op(eng, [lambda: q.dma_start(out_ap, in_ap)], rd, wr, 0.1, done=(sem, 16), lat=dur)
 
+    def ps(bank, a, b, s=1):
+        return ("ps%d" % bank, a, b, s)
+
     xs, dn = whole("xs", W + EXT), whole("dn", ND)
     zed0, rend0, lend0 = whole("zed0", LANES), whole("rend0", LANES), whole("lend0", LANES)
     dma(T.zed0[:], T.zed[:], [], [zed0])
@@ -234,102 +234,143 @@ def rank_program(g, core, T, topo):
     dma(T.xs[:, 0:W], T.stock[:], [], [sub(xs, 0, W)], dur=4.0)
     dma(T.xs[:, W:W + EXT], T.stock[:, 0:EXT], [], [sub(xs, W, W + EXT)])
     dma(T.rend0[:], T.rend[:], [], [rend0])
+    dma(T.dn[:, 0:ND], T.donor[:], [], [dn], dur=3.0)
     dma(T.cnt0[:], T.cnt[:], [], [whole("cnt0", LANES)])
     dma(T.lim0[:], T.lim[:], [], [whole("lim0", 2)])
-    dma(T.dn[:, 0:ND], T.donor[:], [], [dn], dur=3.0)
     dma(T.lend0[:], T.lend[:], [], [lend0])
 
-    ones = alloc("pb", 128)
-    fill(ones, 1.0)
-    bo1, BO, ID, TRI, TRS = [alloc("pb", 128) for _ in range(5)]
+    w, H16 = HALF, 16 * HALF
+    ones144 = alloc("pb", 144)
+    fill(ones144, 1.0)
+    ones = sub(ones144, 0, 128)
+    bo1, BO, ID = [alloc("pb", 128) for _ in range(3)]
 
-    def sel(out, a, pattern, cmp_, base, cm):
-        gps(lambda: g.affine_select(ap(out), ap(a), pattern, cmp_, 0.0, base, cm), [a], [out], 0.4)
+    def sel(out, a, pattern, cmp_, base, cm, rows=128):
+        gps(lambda: g.affine_select(ap(out, rows), ap(a, rows), pattern, cmp_, 0.0, base, cm), [a], [out], 0.17 + 2 * CY * cnt(out))
+
+    def iota(out, pattern, base, cm):
+        small = dict(allow_small_or_imprecise_dtypes=True) if out[0] != "pi" else {}
+        gps(lambda: g.iota(ap(out), pattern, base, cm, **small), [], [out], 0.13 + 2 * CY * cnt(out))
     sel(bo1, ones, [[-16, 8], [0, 16]], OP.is_ge, 0, 1)
     sel(BO, bo1, [[16, 8], [0, 16]], OP.is_ge, 15, -1)
-    pidx, q16 = alloc("pi", 1), alloc("pi", 16)
-    gps(lambda: g.iota(ap(pidx), [[0, 1]], 0, 1), [], [pidx], 0.15)
-    gps(lambda: g.iota(ap(q16), [[16, 16]], 0, 0), [], [q16], 0.2)
     sel(ID, ones, [[-1, 128]], OP.is_equal, 0, 1)
+    pidx, q16 = alloc("pi", 1), alloc("pi", 16)
+    iota(pidx, [[0, 1]], 0, 1)
+    iota(q16, [[16, 16]], 0, 0)
     mq = alloc("pf", 128)
-    gps(lambda: g.iota(ap(mq), [[1, 16], [0, NQ]], 0, 0, allow_small_or_imprecise_dtypes=True), [], [mq], 0.4)
-    sel(TRI, BO, [[1, 128]], OP.is_ge, 0, -1)
-    sel(TRS, BO, [[1, 128]], OP.is_ge, 1, -1)
+    iota(mq, [[1, 16], [0, NQ]], 0, 0)
+    G8 = sub(BO, 0, 128, 16)
 
-    wtf, kapf, kc, k29, k256, nbias = [alloc("pf", 1) for _ in range(6)]
+    def col():
+        return alloc("pf", 1)
+
+    def times(a, s, s2=None, eng="s"):
+        out = alloc("pb", cnt(a))
+        if eng == "s":
+            act(out, a, AF.Copy, scale=s)
+        elif s2 is None:
+            ts(out, a, s, OP.mult)
+        else:
+            ts(out, a, s, OP.mult, s2, OP.mult)
+        return out
+
+    def plus(a, b, o=OP.add):
+        out = alloc("pb", cnt(a))
+        tt(out, a, b, o)
+        return out
+
+    def shifted(c8):
+        z = alloc("pb", 144)
+        fill(z, 0.0)
+        cp(sub(z, 15, 143, 16), c8)
+        return lambda r: sub(z, 15 - r, 143 - r)
+
+    wtf, kapf, kc, k29, k256, sqb, cA, not15, one_k = [col() for _ in range(9)]
     ts(wtf, whole("wt0", 1), 0.5, OP.mult)
-    WB = alloc("pb", 128)
-    ts(WB, BO, wtf, OP.mult)
-    EA, FA, WA = alloc("pb", 2048), alloc("pb", 2048), alloc("pb", 2048)
-    fill(WA, 0.0)
-
-    def col8(t, r, k):
-        return sub(t, 128 * r + k, 128 * r + 128, 16)
+    WB = times(BO, wtf, eng="v")
+    EW = shifted(sub(WB, 0, 128, 16))
+    CM = alloc("pb", 128)
+    ts(CM, ID, 0.5, OP.mult, -16.0, OP.add)
+    CP = times(ID, 32.0)
+    nID = times(ID, -1.0)
     cp(kapf, whole("kap0", 1))
+    ts(sqb, kapf, 16.0, OP.mult, -32.0, OP.add)
+    k8 = col()
+    ts(k8, kapf, -8.0, OP.mult)
+    ts(cA, kapf, k8, OP.mult, -0.375, OP.add)
+    zz = {}
+    for b in range(2):
+        zz[b] = alloc("pb", w)
+        act(zz[b], sub(zed0, b * w, (b + 1) * w), AF.Copy, scale=2.0)
+    hID = times(ID, -0.5)
     kci = alloc("pi", 1)
     ts(kci, pidx, 15, OP.bitwise_and)
     cp(kc, kci)
     ts(k29, kci, 29.0, OP.mult)
-    for r in range(16):
-        if r % 2:
-            act(col8(WA, r, r), sub(WB, r, 128, 16), AF.Copy)
-        else:
-            cp(col8(WA, r, r), sub(WB, r, 128, 16))
-    zz = {}
-    for b in range(2):
-        zz[b] = alloc("pb", HALF)
-        act(zz[b], sub(zed0, b * HALF, (b + 1) * HALF), AF.Copy, scale=2.0)
-    nID, hID, mB, pB, TRB, BOM, I64, pS, nS = [alloc("pb", 128) for _ in range(9)]
-    ts(nID, ID, -1.0, OP.mult)
-    ts(hID, ID, -0.5, OP.mult)
     ts(k256, kci, 256.0, OP.mult)
+    E = shifted(G8)
     KD1, KD2 = alloc("pb", 128), alloc("pb", 128)
     ts(KD1, mq, kc, OP.is_equal, kapf, OP.mult)
     ts(KD2, mq, kc, OP.is_equal, k256, OP.mult)
-    fill(EA, 0.0)
-    for r in range(16):
-        act(col8(EA, r, r), sub(BO, r, 128, 16), AF.Copy)
-    il, l8c = alloc("pi", 16), alloc("pi", 16)
-    l32, l4c, neg = alloc("pb", 16), alloc("pb", 16), alloc("pb", NQ)
-    fill(neg, -1.0)
+    il = alloc("pi", 16)
+    l16, l8c, l4c = alloc("pb", 16), alloc("pb", 16), alloc("pb", 16)
     ts(il, q16, kc, OP.add)
-    ts(l32, il, 32.0, OP.mult)
-    ts(l8c, il, 8.0, OP.mult)
+    ts(l16, il, 16.0, OP.mult)
     ts(l4c, il, 4.0, OP.mult)
-    fill(FA, 0.0)
-    for k in range(16):
-        act(col8(FA, k, k), sub(BO, k, 128, 16), AF.Copy, scale=-0.5)
-        if k < 15:
-            act(col8(FA, k, k + 1), sub(BO, k, 128, 16), AF.Copy, scale=0.5)
-    fill(sub(mB, 0, 1), 0.0)
-    ts(sub(mB, 1, 128), sub(ID, 0, 127), -8192.0, OP.mult)
-    ts(pB, ID, 8192.0, OP.mult)
-    ts(TRB, TRI, 8192.0, OP.mult)
-    ts(BOM, BO, -1048576.0, OP.mult)
-    ts(pS, ID, 0.015625, OP.mult)
-    ts(nS, ID, -0.015625, OP.mult)
-    ts(I64, ID, 64.0, OP.mult)
-    ts(nbias, kc, 14.5, OP.is_lt, 2.0, OP.mult)
-    o16 = alloc("pf", 128)
-    fill(o16, 0.0625)
-    cntb, limf, b8b, b8f, nB0 = alloc("pb", LANES), alloc("pf", 2), alloc("pb", 128), alloc("pf", 128), alloc("pb", LANES)
-    cp(cntb, whole("cnt0", LANES), rows=8)
-    cp(limf, whole("lim0", 2), rows=8)
-    gps(lambda: g.affine_select(ap(b8b, 8), ap(ones, 8), [[1, 8], [0, 16]], OP.is_equal, 0.0, 0, -1), [ones], [b8b], 0.4)
-    cp(b8f, b8b, rows=8)
-    mm([(("ps7", 0, LANES, 1), [(b8b, cntb)])], k8=True)
-    ts(nB0, ("ps7", 0, LANES, 1), kc, OP.is_gt)
-    mm([(("ps7", 0, 2, 1), [(b8f, limf)])], k8=True)
-    thc, sbc = alloc("pf", 1), alloc("pf", 1)
-    act(thc, ("ps7", 0, 1, 1), AF.Copy, bias=1.0)
-    act(sbc, ("ps7", 1, 2, 1), AF.Copy, scale=-1.0)
-    G8 = alloc("pb", 8)
-    cp(G8, sub(BO, 0, 128, 16))
-
-    H16, w = 16 * HALF, HALF
-    Gb, Hb, ADb, AD2, ZY, REL = [[alloc("pb", n) for _ in range(2)] for n in (H16, H16, H16, H16, 2 * H16, 2 * H16)]
     for b in range(2):
-        fill(ZY[b], 0.0)
+        ts(sub(l8c, b * NQ, (b + 1) * NQ), sub(il, 0, NQ), 8.0, OP.mult)
+    g8 = alloc("pb", 8)
+    cp(g8, G8)
+    g8m2 = times(G8, -2.0)
+    ts(not15, kc, 14.5, OP.is_lt)
+    ts(one_k, kc, -1.0, OP.mult, 1.0, OP.add)
+    row1 = col()
+    ts(row1, kc, 1.0, OP.is_equal, 4.0, OP.mult)
+    E1 = shifted(times(G8, row1))
+    ETA = alloc("pb", 2048)
+    iota(ETA, [[0, 2048]], 1, 0)
+    sel(ETA, ETA, [[-1, 16], [-16, 8], [0, 16]], OP.is_equal, 0, 1)
+
+    def ET(r):
+        return sub(ETA, 128 * r, 128 * r + 128)
+    S0 = ET(0)
+    nB, p2B, PB, nS0 = times(ID, -B), times(ID, 2 * B), times(BO, B), times(S0, -B)
+    pBm = times(BO, not15, B, eng="v")
+    nBm = times(pBm, -1.0)
+    Mc1 = plus(nS0, nB, OP.subtract)
+    MN2 = plus(nB, nBm)
+    Mp3 = times(plus(PB, nB), -1.0)
+    ML = plus(BO, nS0)
+    nS1 = times(S0, -1.0)
+    SEL, RST = alloc("pb", 256), alloc("pb", 256)
+    for j in range(2):
+        act(sub(SEL, j, 256, 2), ID, AF.Copy, scale=8192.0)
+    fill(RST, 0.0)
+    fill(sub(RST, 0, 256, 32), 1.0)
+    o1 = alloc("pf", 128)
+    fill(o1, 1.0)
+    cntb, limi, limb, b8, nB0 = alloc("pb", LANES), alloc("pi", 4), alloc("pb", 4), alloc("pb", 128), alloc("pb", LANES)
+    cp(cntb, whole("cnt0", LANES), rows=8)
+    ts(sub(limi, 0, 2), whole("lim0", 2), 4032, OP.bitwise_and, rows=8)
+    ts(sub(limi, 2, 4), whole("lim0", 2), 63, OP.bitwise_and, rows=8)
+    cp(limb, limi, rows=8)
+    sel(b8, ones, [[1, 8], [0, 16]], OP.is_equal, 0, -1, rows=8)
+    sums([(ps(7, 0, LANES), [(b8, cntb)]), (ps(7, LANES, LANES + 4), [(b8, limb)])], rows=8)
+    lim4 = alloc("pf", 4)
+    act(lim4, ps(7, LANES, LANES + 4), AF.Copy)
+    ts(nB0, ps(7, 0, LANES), kc, OP.is_gt)
+    sbl, sbl2 = col(), col()
+    ts(sbl, sub(lim4, 3, 4), 2.0, OP.add, not15, OP.mult)
+    ts(sbl2, sbl, -1.0, OP.add)
+    CD = [alloc("pb", 256) for _ in range(2)]
+    ts(sub(CD[0], 0, 256, 2), ID, sub(lim4, 0, 1), OP.mult, -1.0, OP.mult)
+    ts(sub(CD[0], 1, 256, 2), ID, sub(lim4, 1, 2), OP.mult, not15, OP.mult)
+    ts(sub(CD[1], 0, 256, 2), ID, sub(lim4, 2, 3), OP.mult, -1.0, OP.mult)
+    ts(sub(CD[1], 1, 256, 2), ID, sbl2, OP.mult)
+    cA2 = col()
+    ts(cA2, cA, 2048.0, OP.add)
+
+    Gb, ADb, Yb, Hb, AH, MX = [[alloc("pb", H16) for _ in range(2)] for _ in range(6)]
     par = {}
 
     def til(pool, n, key, t, b):
@@ -337,201 +378,214 @@ def rank_program(g, core, T, topo):
         if k not in par:
             par[k] = alloc(pool, n)
         return par[k]
-    A0 = alloc("pf", 1)
-    fill(A0, 0.0)
     accs = [alloc("pf", 2) for _ in range(2)]
     state = {b: dict(z2=zz[b], R=sub(rend0, b * w, (b + 1) * w), L=sub(lend0, b * w, (b + 1) * w),
-                     n=sub(nB0, b * w, (b + 1) * w)) for b in range(2)}
+                     N=[sub(nB0, b * w, (b + 1) * w)]) for b in range(2)}
+    UW = w + NQ
 
-    def E(k):
-        return sub(EA, 128 * k, 128 * k + 128)
+    def banks(b):
+        return 2 + 3 * b, 3 + 3 * b, 4 + 3 * b
 
-    def F(k):
-        return sub(FA, 128 * k, 128 * k + 128)
-
-    def ps(bank, a, b):
-        return ("ps%d" % bank, a, b, 1)
-
-    def front(t, b, A):
+    def early(t, b):
         s = state[b]
-        BS, BM = 4 + 2 * b, 5 + 2 * b
+        P = banks(b)[0]
+        z2 = s["z2"]
+        U = ps(P, 0, UW)
+        weighted = [(ps(P, 0, w), WB, z2)] + [(ps(P, w, UW), EW(r), sub(z2, r, w, 16)) for r in range(16)]
+        mm([(U, CM, sub(ones144, 0, UW))] + weighted)
+        r4 = til("pb", UW, "r4", t, b)
+        ts(r4, U, M4096, OP.add, M4096, OP.subtract)
+        mm([(U, CP, sub(ones144, 0, UW))] + weighted + [(U, nID, r4)])
+        sq, sql, up, zm = til("pf", w, "sq", t, b), til("pf", NQ, "sql", t, b), til("pf", w, "up", t, b), til("pf", w, "zm", t, b)
+        ul = sub(til("pi", 2 * NQ, "ul", t, 0), b * NQ, (b + 1) * NQ)
+        act(sq, ps(P, 0, w), AF.Square, bias=sqb)
+        act(sql, ps(P, w, UW), AF.Square, bias=m32)
+        act(up, ps(P, 0, w), AF.Copy)
+        ts(ul, ps(P, w, UW), -32.0, OP.add)
+        act(zm, z2, AF.Copy, scale=0.5, bias=-0.5)
+        s.update(sq=sq, sql=sql, up=up, ul=ul, zm=zm)
+    m32 = col()
+    fill(m32, -32.0)
+
+    def front(t, b, A, AL):
+        s = state[b]
+        P, Q, Rb = banks(b)
 
         def ti(key, n=w):
             return til("pi", n, key, t, b)
-        z2 = s["z2"]
-        UW = w + NQ
-        U = ps(BS, 0, UW)
-        mm([(ps(BS, 0, w), [(WB, z2)]),
-            (ps(BS, w, UW), [(sub(WA, 128 * r, 128 * r + 128), sub(z2, r, w, 16)) for r in range(16)])])
-        ui, u, uu, s1 = [ti(k, UW) for k in ("ui", "u", "uu", "s1")]
-        u4 = ti("u4")
-        s3, c = ti("s3"), ti("c")
-        s2 = ps(BS, 256, 256 + w)
+        ci, c, cil = ti("ci"), ti("c"), ti("cil", NQ)
         cl = til("pu", w, "cl", t, b)
-        cp(ui, U)
-        ts(u, ui, 4095, OP.bitwise_and)
-        uA, ul, sA, sl = sub(u, 0, w), sub(u, w, UW), sub(s1, 0, w), sub(s1, w, UW)
-        tt(uu, u, u, OP.mult)
-        ts(s2, uA, kapf, OP.mult, A, OP.add)
-        ts(s1, uu, 5, OP.arith_shift_right)
-        tt(s3, sA, s2, OP.add)
-        ts(c, s3, 2047, OP.bitwise_and)
+        ts(ci, s["sq"], 0.03125, OP.mult, A, OP.add)
+        ts(c, ci, 2047, OP.bitwise_and)
         cp(cl, c)
-        gat2(GS[b], Gb[b], 1, sub(xs, 0, W), cl, w)
-        up, pr, pr2 = til("pf", w, "up", t, b), ti("pr"), ti("pr2")
-        hl = til("pu", w, "hl", t, b)
-        ts(up, uA, 32.0, OP.add)
-        tt(pr, s["R"], up, OP.mult)
-        ts(pr2, pr, 5, OP.arith_shift_right, 2047, OP.bitwise_and)
-        ts(hl, pr2, k29, OP.add)
-        if HS[b] >= 0:
-            gat2(HS[b], Hb[b], 1, xs, hl, w)
-        s1a, x8, l8 = [ti(k, NQ) for k in ("s1a", "x8", "l8")]
-        l8u = til("pu", NQ, "l8u", t, b)
-        ts(s1a, sl, A, OP.add)
-        ts(x8, ul, 7, OP.bitwise_and)
-        tt(l8, x8, sub(l8c, 0, NQ), OP.add)
-        cp(l8u, l8)
-        ts(u4, uA, 3, OP.bitwise_and)
-        ku = til("pb", w, "ku", t, b)
-        ts(ku, u4, kc, OP.is_ge)
-        zm = til("pf", w, "zm", t, b)
-        act(zm, z2, AF.Copy, scale=0.5, bias=-0.5)
+        gs = OPT["gs"][b]
+        if gs < w:
+            gat("v", sub(Gb[b], 16 * gs, H16), sub(xs, 0, W), sub(cl, gs, w))
+        if gs:
+            gat("s", sub(Gb[b], 0, 16 * gs), sub(xs, 0, W), sub(cl, 0, gs))
+        ts(cil, s["sql"], 0.03125, OP.mult, AL, OP.add)
+        pp, p2 = ti("pp", 2 * w), ti("p2", 2 * w)
+        ll = til("pu", 2 * w, "ll", t, b)
+        raw = [r for r in OPT["runs"][b] if r[2] == "raw"]
+        tt(sub(pp, w, 2 * w), s["R"], ps(P, 0, w), OP.mult)
+        if raw:
+            ts(sub(p2, w, 2 * w), sub(pp, w, 2 * w), 5, OP.arith_shift_right, 2047, OP.bitwise_and)
+            ts(sub(ll, w, 2 * w), sub(p2, w, 2 * w), k29, OP.add)
+            lo = 0
+            for n, _y, how in OPT["runs"][b]:
+                if how == "raw":
+                    gat("s", sub(Hb[b], 16 * lo, 16 * (lo + n)), xs, sub(ll, w + lo, w + lo + n))
+                lo += n
         k0 = til("pf", 8 * NQ, "k0", t, b)
         for mc in range(4):
-            D = 2 * b + mc % 2
-            mm([(ps(D, j * w, (j + 1) * w), [(ID, sub(Gb[b], 4 * mc + j, H16, 16)), (hID, z2)]) for j in range(4)])
+            D = mc % 2
+            sums([(ps(D, j * w, (j + 1) * w), [(ID, sub(Gb[b], 4 * mc + j, H16, 16)), (hID, s["z2"])]) for j in range(4)])
             act(sub(ADb[b], mc * 4 * w, (mc + 1) * 4 * w), ps(D, 0, 512), AF.Abs, scale=4096.0)
             if mc % 2 == 1:
                 h = mc // 2
-                K = ps(BS if h == 0 else BM, 0, 8 * NQ)
-                mm([(K, [(BO, sub(KD1, 64 * h, 64 * h + 64)), (BO, sub(KD2, 64 * h, 64 * h + 64))]
-                     + [(E(r), sub(ADb[b], h * 8 * w + r, (h + 1) * 8 * w, 16)) for r in range(16)])])
+                K = ps(Q if h == 0 else Rb, 0, 8 * NQ)
+                sums([(K, [(BO, sub(KD1, 64 * h, 64 * h + 64)), (BO, sub(KD2, 64 * h, 64 * h + 64))]
+                       + [(E(r), sub(ADb[b], h * 8 * w + r, (h + 1) * 8 * w, 16)) for r in range(16)])])
                 if h == 0:
                     act(k0, K, AF.Copy)
         t1, t2, t3 = [til("pf", n, "tm%d" % n, t, b) for n in (64, 32, 16)]
         vi, ka, pa, pc, cd, cx = [ti(k, NQ) for k in ("vi", "ka", "pa", "pc", "cd", "cx")]
         cdu, cxu = til("pu", NQ, "cdu", t, b), til("pu", NQ, "cxu", t, b)
-        tt(t1, ps(BM, 0, 64), k0, OP.min)
+        tt(t1, ps(Rb, 0, 64), k0, OP.min)
         tt(t2, sub(t1, 0, 32), sub(t1, 32, 64), OP.min)
         tt(t3, sub(t2, 0, 16), sub(t2, 16, 32), OP.min)
         tt(vi, sub(t3, 0, 8), sub(t3, 8, 16), OP.min)
         ts(ka, vi, 255, OP.bitwise_and)
-        tt(pa, ka, ul, OP.mult)
-        tt(pc, pa, s1a, OP.add)
+        tt(pa, ka, s["ul"], OP.mult)
+        tt(pc, pa, cil, OP.add)
         ts(cd, pc, 1023, OP.bitwise_and)
         cp(cdu, cd)
-        P, P2 = ti("P"), ti("P2")
-        yl = til("pu", w, "yl", t, b)
-        gtt(P, dn, cdu, up, OP.mult)
-        ts(P2, P, 5, OP.arith_shift_right, 2047, OP.bitwise_and)
-        ts(yl, P2, k29, OP.add)
+        gtt(sub(pp, 0, w), dn, cdu, s["up"], OP.mult)
+        n = w if raw else 2 * w
+        ts(sub(p2, 0, n), sub(pp, 0, n), 5, OP.arith_shift_right, 2047, OP.bitwise_and)
+        ts(sub(ll, 0, n), sub(p2, 0, n), k29, OP.add)
         ts(cx, pc, 2047, OP.bitwise_and)
         cp(cxu, cx)
         Dk, xc = til("pb", w, "Dk", t, b), til("pb", w, "xc", t, b)
-        for h in range(2):
-            gat(YE[b][h], sub(ZY[b], h * H16, (h + 1) * H16, 2), xs, sub(yl, h * w // 2, (h + 1) * w // 2))
         gat("s", Dk, dn, cdu)
         gat("s", xc, sub(xs, 0, W), cxu)
-        s.update(hl=hl, zm=zm, Dk=Dk, xc=xc, ku=ku, l8u=l8u)
+        s.update(ll=ll, Dk=Dk, xc=xc)
+
+    def own(t):
+        ul = til("pi", 2 * NQ, "ul", t, 0)
+        xi, xb = til("pi", 4 * NQ, "xi", t, 0), til("pb", 2 * NQ, "xb", t, 0)
+        l8, l8u = til("pi", 2 * NQ, "l8", t, 0), til("pu", 2 * NQ, "l8u", t, 0)
+        ts(sub(xi, 0, 2 * NQ), ul, 7, OP.bitwise_and)
+        ts(sub(xi, 2 * NQ, 4 * NQ), ul, 3, OP.bitwise_and)
+        cp(xb, sub(xi, 2 * NQ, 4 * NQ))
+        tt(l8, sub(xi, 0, 2 * NQ), l8c, OP.add)
+        cp(l8u, l8)
+        for b in range(2):
+            state[b].update(u3=sub(xb, b * NQ, (b + 1) * NQ), l8u=sub(l8u, b * NQ, (b + 1) * NQ))
 
     def tail(t, b):
         s = state[b]
-        BS, BM = 4 + 2 * b, 5 + 2 * b
-        z, H, rel = ZY[b], Hb[b], REL[b]
-        fused = HS[b] < 0
+        P, Q, Rb = banks(b)
+        y, H, mx, ah, ll = Yb[b], Hb[b], MX[b], AH[b], s["ll"]
+        lo, mins = 0, False
+        for n, who, how in OPT["runs"][b]:
+            a, e = 16 * lo, 16 * (lo + n)
+            gat(who, sub(y, a, e), xs, sub(ll, lo, lo + n))
+            scan(sub(mx, a, e - 1), sub(y, a, e - 1), sub(y, a + 1, e), 1000.0)
+            if how == "raw":
+                for j in range(a, e, 512):
+                    D = j // 512 % 2
+                    sums([(ps(D, 0, 512), [(ID, sub(H, j, j + 512)), (nID, sub(y, j, j + 512))])])
+                    act(sub(ah, j, j + 512), ps(D, 0, 512), AF.Abs)
+            else:
+                gtt(sub(H, a, e), xs, sub(ll, w + lo, w + lo + n), sub(y, a, e), OP.subtract)
+                if how == "va":
+                    act(sub(ah, a, e), sub(H, a, e), AF.Abs)
+                else:
+                    ts(sub(ah, a, e), sub(H, a, e), 0.0, OP.min)
+                    mins = True
+            lo += n
+        V = ps(Q, 0, 256)
 
-        def tb(key):
-            return til("pb", w, key, t, b)
-        J, M, e = ps(BS, 0, w), ps(BM, 0, w), w // 2
-        for h in range(2):
-            lo, hi = h * H16, (h + 1) * H16
-            op("v", [lambda lo=lo, hi=hi: g.vector.tensor_tensor_scan(
-                ap(sub(rel, lo, hi - 1)), ap(sub(z, lo + 1, hi)), ap(sub(z, lo, hi - 1)), 0.0, OP.subtract, OP.max)],
-               [sub(z, lo, hi)], [sub(rel, lo, hi - 1)], vd(0.5 * H16))
-            if fused:
-                gtt(sub(H, lo // 2, hi // 2), xs, sub(s["hl"], h * e, (h + 1) * e), sub(z, lo, hi, 2), OP.subtract)
-                act(sub(AD2[b], lo // 2, hi // 2), sub(H, lo // 2, hi // 2), AF.Abs)
-            for kq in range(0 if fused else 2):
-                D = 2 * b + kq
-                mm([(ps(D, j * e, (j + 1) * e), [(ID, sub(z, lo + 2 * (8 * kq + j), hi, 32)),
-                                                 (nID, sub(H, lo // 2 + 8 * kq + j, hi // 2, 16))]) for j in range(8)])
-                act(sub(AD2[b], lo // 2 + kq * 512, lo // 2 + (kq + 1) * 512), ps(D, 0, 512), AF.Abs)
-            jh, mh = sub(J, h * e, (h + 1) * e), sub(M, h * e, (h + 1) * e)
-            mm([(jh, ([(mB, (J, s["n"]))] if h == 0 else [])
-                 + [(F(k), sub(z, lo + 2 * k, hi, 32)) for k in range(16)]
-                 + [(E(k), sub(rel, lo + 2 * k - 1, hi - 1, 32)) for k in range(1, 16)])], keep_open=h == 0, cont=h == 1)
-            mm([(mh, ([(pB, (M, s["n"]))] if h == 0 else [])
-                 + [(E(k), sub(AD2[b], lo // 2 + k, hi // 2, 16) if fused else
-                     sub(AD2[b], lo // 2 + k * e, lo // 2 + (k + 1) * e)) for k in range(16)])], keep_open=True, cont=h == 1)
-        jm, me, ne = tb("jm"), tb("me"), tb("ne")
-        act(jm, J, AF.Relu, scale=2.0, bias=sbc)
-        mm([(M, [(TRB, jm)])], cont=True)
-        act(me, M, AF.Relu, scale=-1.0, bias=thc)
-        mm([(ps(BS, 0, w), [(TRI, me), (TRS, jm)])])
-        act(ne, ps(BS, 0, w), AF.Relu, scale=-2.0, bias=nbias)
-        mm([(ps(BM, 0, NQ), [(ID, sub(l32, 0, NQ))] + [(E(r), sub(ne, r, w, 16)) for r in range(16)])])
+        def vc(j):
+            return ps(Q, j, 256, 32)
+
+        def kth(a, k):
+            return sub(a, k, H16, 16)
+        mm([(V, ones, CD[0]), (V, ones, CD[1])] + [(V, n_, SEL) for n_ in s["N"]], stop=False)
+        mm([(vc(2 * k + 1), kth(y, k), g8) for k in range(1, 15)] + [(vc(2 * k - 1), kth(y, k), g8) for k in range(2, 16)],
+           start=False, stop=False, cont=True)
+        mm([(vc(2 * k + 1), kth(mx, k), g8m2) for k in range(1, 15)], start=False, stop=False, cont=True)
+        if mins:
+            mm([(vc(2 * k), kth(H, k), g8) for k in range(1, 16)], start=False, stop=False, cont=True)
+        mm([(vc(2 * k), kth(ah, k), g8m2 if mins else g8) for k in range(1, 16)], start=False, cont=True)
+        al = til("pb", 256, "al", t, b)
+        scan(al, V, RST, 1.0)
+        A1, Dl = til("pb", w, "A1", t, b), til("pb", w, "Dl", t, b)
+        sums([(ps(Rb, 0, w), [(sub(al, 1, 256, 2), ID)]),
+              (ps(Rb, w, 2 * w), [(sub(al, 1, 256, 2), ID), (sub(al, 0, 256, 2), nID)])])
+        act(A1, ps(Rb, 0, w), AF.Copy)
+        sums([(ps(P, 0, NQ), [(ID, sub(l16, 0, NQ))] + [(E(r), sub(A1, r, w, 16)) for r in range(16)])])
+        act(Dl, ps(Rb, w, 2 * w), AF.Copy, accum=sub(accs[t % 2], b, b + 1))
         yel = til("pu", NQ, "yel", t, b)
-        cp(yel, ps(BM, 0, NQ))
+        cp(yel, ps(P, 0, NQ))
         sz = til("pf", w, "sz", t, b)
         zo = whole("zo%d%d" % (t, b), w)
-        gtt(sz, z, yel, s["zm"], OP.add)
-        ts(zo, sz, MAGIC, OP.add, MAGIC, OP.subtract)
+        gtt(sz, y, yel, s["zm"], OP.add)
+        ts(zo, sz, M2, OP.add, M2, OP.subtract)
         if t < VISITS - 1:
             send("z", t, b, zo)
         sx, sx2 = til("pi", w, "sx", t, b), til("pi", w, "sx2", t, b)
-        gtt(sx, z, yel, s["xc"], OP.add)
+        gtt(sx, y, yel, s["xc"], OP.add)
         ts(sx2, sx, 1, OP.arith_shift_right)
-        mm([(ps(BS, 0, w), [(BO, me)]), (ps(BS, w, 2 * w), [(BO, jm), (BOM, me)]), (ps(BS, 2 * w, 3 * w), [(TRI, me)]),
-            (ps(BS, 3 * w, 4 * w), [(TRI, jm), (I64, s["n"])])])
-        an, nm2, m1, nd6 = tb("an"), tb("nm2"), tb("m1"), tb("nd6")
-        act(an, ps(BS, 0, w), AF.Sign, accum=sub(accs[t % 2], b, b + 1))
-        act(m1, ps(BS, 3 * w, 4 * w), AF.Relu, scale=-1.0, bias=1.0)
-        act(nm2, ps(BS, 2 * w, 3 * w), AF.Relu, scale=-1.0, bias=1.0)
-        ts(nd6, ps(BS, w, 2 * w), 0.5, OP.is_gt, 64.0, OP.mult)
-        s.update(sx2=sx2, nd6=nd6, m1=m1, nm2=nm2)
+        s.update(sx2=sx2, A1=A1, Dl=Dl)
 
     def count(t):
-        A = ps(6, 0, 1)
-        mm([(A, [(o16, sub(accs[t % 2], b, b + 1)) for b in range(2)])])
-        ac = til("pf", 1, "A", t, 0)
-        act(ac, A, AF.Copy)
-        return ac
+        A = ps(0, 0, 1)
+        sums([(A, [(o1, sub(accs[t % 2], b, b + 1)) for b in range(2)])])
+        ac, al = til("pf", 1, "A", t, 0), til("pf", 1, "AL", t, 0)
+        act(ac, A, AF.Identity, bias=cA2)
+        act(al, A, AF.Copy, bias=2047.625)
+        return ac, al
 
     def writes_x(t, b):
         scat(sub(xs, b * W // 2, (b + 1) * W // 2), state[b]["l8u"], state[b]["sx2"])
         if b == 0 and t < VISITS - 1:
-            cp(sub(xs, W, W + EXT), sub(xs, 0, EXT))
+            dma(T.xs[:, W:W + EXT], T.xs[:, 0:EXT], [sub(xs, 0, EXT)], [sub(xs, W, W + EXT)])
 
     def update(t, b):
         s = state[b]
-        BS, BM = 4 + 2 * b, 5 + 2 * b
-
-        def tb(key):
-            return til("pb", w, key, t, b)
-        tl, Q, Q2 = [tb(k) for k in ("tl", "Q", "Q2")]
-        r3 = til("pb", 4 * w, "r3", t, b)
-        L, R = s["L"], s["R"]
-        mm([(ps(BM, 0, w), [(ID, s["Dk"]), (nID, L)])])
-        mm([(ps(BS, 0, w), [(nID, ones), (ID, s["n"]), (ID, s["m1"]), (pS, s["nd6"])]),
-            (ps(BS, w, 2 * w), [(ID, s["ku"]), (nS, s["nd6"])]), (ps(BS, 2 * w, 3 * w), [(ID, s["nm2"]), (nS, s["nd6"])]),
-            (ps(BS, 3 * w, 4 * w), [(ID, s["ku"]), (ID, s["nd6"])])])
-        act(r3, ps(BS, 0, 4 * w), AF.Relu)
-        tt(tl, s["m1"], ps(BM, 0, w), OP.mult)
-        mm([(ps(BM, 0, w), [(ID, tl), (ID, L), (nID, R)])])
-        tt(Q, s["nm2"], ps(BM, 0, w), OP.mult)
-        tt(Q2, sub(r3, 2 * w, 3 * w), ps(BM, 0, w), OP.mult)
-        mm([(ps(BM, 0, w), [(ID, R), (ID, Q2)]), (ps(BM, w, 2 * w), [(ID, sub(r3, 0, w)), (ID, sub(r3, w, 2 * w))]),
-            (ps(BM, 2 * w, 3 * w), [(ID, R), (ID, Q)])])
-        ro = whole("ro%d%d" % (t, b), 3 * w)
-        act(ro, ps(BM, 0, 3 * w), AF.Copy)
-        if t < VISITS - 1:
-            send("r", t, b, ro)
-        mm([(ps(BS, 0, NQ), [(ID, sub(l4c, b * NQ, (b + 1) * NQ)), (ID, neg)]
-             + [(E(r), sub(r3, 3 * w + r, 4 * w, 16)) for r in range(16)])])
+        P, Q, Rb = banks(b)
+        L, R, N, A1, Dl = s["L"], s["R"], s["N"], s["A1"], s["Dl"]
+        last = t == VISITS - 1
+        ro = whole("ro%d%d" % (t, b), 5 * w)
+        Rn, Ln, N1, N2, Nd = [sub(ro, j * w, (j + 1) * w) for j in range(5)]
+        c3, r3 = til("pb", w, "c3", t, b), til("pb", 3 * w, "r3", t, b)
+        sums([(ps(Q, 0, w), [(ID, s["Dk"]), (Mc1, A1), (nB, Dl)] + [(nB, n_) for n_ in N]),
+              (ps(Q, w, 2 * w), [(ID, R), (nB, A1), (PB, Dl)]),
+              (ps(Q, 2 * w, 3 * w), [(ID, R), (nS0, A1), (nBm, Dl)])])
+        act(r3, ps(Q, 0, 3 * w), AF.Relu)
+        sums([(ps(Rb, 0, w), [(nB, A1), (Mp3, Dl)] + [(p2B, n_) for n_ in N])])
+        tt(c3, ps(Rb, 0, w), L, OP.min)
+        sums([(ps(Q, 0, w), [(ID, sub(r3, 0, w)), (ID, sub(r3, w, 2 * w))])])
+        tt(Ln, ps(Q, 0, w), c3, OP.max)
+        first = [(pBm, Dl)] + [(ET(r), (ps(Rb, r, w, 16), s["u3"])) for r in range(16)]
+        if last:
+            sums([(ps(Rb, 0, w), first), (ps(Rb, w, 2 * w), [(ML, A1), (nBm, Dl)]), (ps(Rb, 2 * w, 3 * w), [(nS1, A1), (nBm, Dl)])])
+            act(sub(ro, 2 * w, 5 * w), ps(Rb, 0, 3 * w), AF.Relu, bias=1.0)
+        else:
+            sums([(ps(Rb, 0, w), first), (ps(Rb, w, 2 * w), [(Mc1, A1), (MN2, Dl)])])
+            act(sub(ro, 2 * w, 4 * w), ps(Rb, 0, 2 * w), AF.Relu, bias=one_k)
+            Nd = N2
+        sums([(ps(Q, 0, w), [(ID, Ln), (pBm, Dl)])])
+        tt(Rn, ps(Q, 0, w), sub(r3, 2 * w, 3 * w), OP.max)
+        if not last:
+            send("r", t, b, sub(ro, 0, 4 * w))
+        sums([(ps(Rb, 0, NQ), [(ID, sub(l4c, b * NQ, (b + 1) * NQ)), (ID, s["u3"])]
+               + [(E1(r), sub(Nd, r, w, 16)) for r in range(16)])])
         dlu = til("pu", NQ, "dlu", t, b)
-        cp(dlu, ps(BS, 0, NQ))
-        scat(whole("dn", 2 * ND), dlu, sub(ro, 2 * w, 3 * w))
+        cp(dlu, ps(Rb, 0, NQ))
+        scat(whole("dn", 2 * ND), dlu, Ln)
 
     snt = {"z": 0, "r": 0}
 
@@ -544,38 +598,44 @@ def rank_program(g, core, T, topo):
         o = op("g", [lambda: g.remote_dma(T[k + "i" + name[1:]][:], ap(tile), T.sem["a" + name], T.sem[k + "sent"], pid, rid, m)],
                [tile], [], 1.0, done=(k + "sent", 0))
         n = len(topo.engines(relays(topo, cores, (rank - 1) % len(cores))["zr".index(k)], core))
-        op(None, [], [], [whole(k + "i" + name[1:], cnt(tile))], 0.0, done=("a" + name, n), lat=4.0, extra=(o,))
+        op(None, [], [], [whole(k + "i" + name[1:], cnt(tile))], 0.0, done=("a" + name, n), lat=4.0 if k == "z" else 6.0, extra=(o,))
 
-    A = A0
+    AL0 = col()
+    fill(AL0, -0.375)
+    A = (cA, AL0)
     for t in range(VISITS):
+        for name, step in (("early", early), ("front", lambda t, b: front(t, b, *A))):
+            for b in range(2):
+                stage[0] = name + str(b)
+                step(t, b)
+        stage[0] = "own"
+        own(t)
         for b in range(2):
-            stage[0] = "f%d%d" % (b, t)
-            front(t, b, A)
-        for b in range(2):
-            stage[0] = "t%d%d" % (b, t)
+            stage[0] = "tail%d" % b
             tail(t, b)
-        stage[0] = "w0%d" % t
-        A = count(t)
+        stage[0] = "write"
+        if t < VISITS - 1:
+            A = count(t)
         for b in range(2):
             writes_x(t, b)
         for b in range(2):
-            stage[0] = "u%d%d" % (b, t)
+            stage[0] = "update%d" % b
             update(t, b)
-        stage[0] = "e0%d" % t
+        stage[0] = "end"
         for b in range(2):
             if t < VISITS - 1:
-                r = whole("ri%d%d" % (t, b), 3 * w)
-                state[b] = dict(z2=whole("zi%d%d" % (t, b), w), R=sub(r, 0, w), n=sub(r, w, 2 * w), L=sub(r, 2 * w, 3 * w))
+                r = whole("ri%d%d" % (t, b), 4 * w)
+                state[b] = dict(z2=whole("zi%d%d" % (t, b), w), R=sub(r, 0, w), L=sub(r, w, 2 * w),
+                                N=[sub(r, 2 * w, 3 * w), sub(r, 3 * w, 4 * w)])
             else:
-                zo, r = whole("zo%d%d" % (t, b), w), whole("ro%d%d" % (t, b), 3 * w)
+                zo, r = whole("zo%d%d" % (t, b), w), whole("ro%d%d" % (t, b), 5 * w)
                 lo, hi = b * w, (b + 1) * w
                 act(sub(whole("yz0", LANES), lo, hi), zo, AF.Copy, scale=0.5)
                 dma(T.yz[:, lo:hi], T.yz0[:, lo:hi], [("yz0", lo, hi, 1)], [])
-                mm([(ps(4, 0, w), [(G8, sub(r, w, 2 * w))])], m8=True)
-                op("s", [lambda lo=lo, hi=hi: g.scalar.activation(T.yn0[:, lo:hi], T.ps4[0:8, 0:w], AF.Copy)],
-                   [ps(4, 0, w)], [("yn0", lo, hi, 1)], 0.2)
-                dma(T.yr[:, lo:hi], ap(sub(r, 0, w)), [r], [])
-                dma(T.yl[:, lo:hi], ap(sub(r, 2 * w, 3 * w)), [r], [])
+                sums([(ps(b, 0, w), [(g8, sub(r, 2 * w, 3 * w)), (g8, sub(r, 3 * w, 4 * w))])], out_rows=8)
+                act(("yn0", lo, hi, 1), ps(b, 0, w), AF.Copy, scale=0.0625, rows=8)
+                dma(T.yr[:, lo:hi], ap(sub(r, 0, w)), [sub(r, 0, w)], [])
+                dma(T.yl[:, lo:hi], ap(sub(r, w, 2 * w)), [sub(r, w, 2 * w)], [])
     dma(T.yn[:], T.yn0[:], [("yn0", 0, LANES, 1)], [])
     for b in range(2):
         lo, hi = b * W // 2, (b + 1) * W // 2
@@ -585,12 +645,12 @@ def rank_program(g, core, T, topo):
     N = len(ops)
     succ = [[] for _ in range(N)]
     for i, o in enumerate(ops):
-        for d in o["deps"]:
+        for d in o["after"]:
             succ[d].append(i)
     prio = [0.0] * N
     for i in range(N - 1, -1, -1):
-        prio[i] = ops[i]["dur"] + ops[i]["lat"] + max([prio[j] for j in succ[i]] + [0.0])
-    left = [len(o["deps"]) for o in ops]
+        prio[i] = ops[i]["dur"] + ops[i]["lat"] + 0.06 + max([prio[j] for j in succ[i]] + [0.0])
+    left = [len(o["after"]) for o in ops]
     ready = {e: [] for e in ("v", "s", "t", "g", "y", None)}
     avail = [0.0] * N
     free = {e: 0.0 for e in ready}

@@ -8,10 +8,13 @@ M2, M4096 = 1.5 * 2 ** 24, 1.5 * 2 ** 35
 B = 256.0
 
 OPT = dict(
-    gs=(64, 16),
-    runs=(((64, "s", "va"), (64, "s", "va")), ((64, "s", "va"), (64, "v", "va"))),
-    bias={},
+    gs=(64, 64),
+    runs=(((64, "v", "raw"), (64, "s", "raw")), ((64, "s", "va"), (64, "v", "va"))),
+    bias={}, slack=0.2, turns=12000, heat=0.5, seed=1, joint=(True, True), zlat=2.6, rlat=4.2,
+    models=((1.35, 2.5, 1.0, 1.0, 0.2), (1.1, 2.0, 1.0, 0.8, 0.17), (1.8, 5.0, 1.25, 1.4, 0.24)),
 )
+CY = 0.00083
+LOG = []
 
 SCRATCH = {
     "pi": ("sbuf", [128, 6144], "int32"), "pf": ("sbuf", [128, 4096], "float32"),
@@ -61,6 +64,95 @@ def relay_program(g, core, T, topo, dst, src, kinds):
         g.wait_ge(T.sem[k + "sent"], sent[k])
 
 
+ORDER = []
+
+
+def schedule(ops):
+    n = len(ops)
+    queue = {"v": 0, "s": 1, "t": 2, "g": 3, "y": 4, None: 5}
+    eng = [queue[o["eng"]] for o in ops]
+    pred = [sorted(o["after"]) for o in ops]
+    succ = [[] for _ in ops]
+    for i in range(n):
+        for d in pred[i]:
+            succ[d].append(i)
+    costs = [([(o["dur"] + CY * (gf * o["gather"] + sf * o["scatter"])) * f for o in ops],
+              [o["lat"] * lf + hop for o in ops]) for gf, sf, f, lf, hop in OPT["models"]]
+    dur, lat = costs[0]
+    way = [0.0] * n
+    for i in range(n - 1, -1, -1):
+        way[i] = dur[i] + lat[i] + max([way[j] for j in succ[i]] + [0.0])
+    slack = OPT["slack"]
+
+    def plan(prio):
+        left = [len(p) for p in pred]
+        ready = [[] for _ in range(6)]
+        avail, free, first, order, span = [0.0] * n, [0.0] * 6, [1e18] * 6, [], 0.0
+        for i in range(n):
+            if not left[i]:
+                ready[eng[i]].append(i)
+                first[eng[i]] = 0.0
+        for _ in range(n):
+            st = 1e17
+            for k in range(6):
+                x = first[k] if first[k] > free[k] else free[k]
+                if x < st:
+                    st, e = x, k
+            top, lim = -1e18, st + slack
+            for j in ready[e]:
+                if avail[j] <= lim and prio[j] > top:
+                    top, i = prio[j], j
+            ready[e].remove(i)
+            first[e] = min([avail[j] for j in ready[e]] + [1e18])
+            end = (st if st > avail[i] else avail[i]) + dur[i]
+            if e != 5:
+                free[e] = end
+            order.append(i)
+            end += lat[i]
+            if end > span:
+                span = end
+            for j in succ[i]:
+                if end > avail[j]:
+                    avail[j] = end
+                left[j] -= 1
+                if not left[j]:
+                    ready[eng[j]].append(j)
+                    if avail[j] < first[eng[j]]:
+                        first[eng[j]] = avail[j]
+        for d2, l2 in costs[1:]:
+            done, free = [0.0] * n, [0.0] * 6
+            for i in order:
+                st = free[eng[i]]
+                for j in pred[i]:
+                    if done[j] > st:
+                        st = done[j]
+                st += d2[i]
+                if eng[i] != 5:
+                    free[eng[i]] = st
+                done[i] = st + l2[i]
+            span += max(done)
+        return span / len(costs), order
+    steps = sorted(set(o["step"] for o in ops))
+    off = {k: OPT["bias"].get(k[0], 0.0) for k in steps}
+    seed = [OPT["seed"]]
+
+    def draw(k):
+        seed[0] = (seed[0] * 1103515245 + 12345) % 2 ** 31
+        return (seed[0] >> 8) % k
+    now, order = best = plan([way[i] + off[ops[i]["step"]] for i in range(n)])
+    for turn in range(OPT["turns"]):
+        new = dict(off)
+        for _ in range(1 + draw(3)):
+            new[steps[draw(len(steps))]] += (-4, -2, -1, -0.5, 0.5, 1, 2, 4)[draw(8)]
+        span, order = plan([way[i] + new[ops[i]["step"]] for i in range(n)])
+        if span <= now + OPT["heat"] * (1 - turn / OPT["turns"]) * (draw(1000) / 1000) ** 3:
+            now, off = span, new
+            if span < best[0]:
+                best = (span, order)
+    LOG.append((ops, way, succ, best[0]))
+    return best[1]
+
+
 def rank_program(g, core, T, topo):
     rank = T.rank_of(core)
     cores = list(T.cores)
@@ -100,7 +192,7 @@ def rank_program(g, core, T, topo):
 
     stage = ["c"]
 
-    def op(eng, fns, reads, writes, dur, done=None, lat=0.0, extra=(), cont=False):
+    def op(eng, fns, reads, writes, dur, done=None, lat=0.0, extra=(), cont=False, gather=0, scatter=0):
         me = len(ops)
         deps, soft = set(extra), set()
         for regs, wr in ((reads, False), (writes, True)):
@@ -116,14 +208,13 @@ def rank_program(g, core, T, topo):
                         keep.append((a, b, o, w_))
                 keep.append((lo, hi, me, wr or bank))
                 acc[name] = keep
-        ops.append(dict(eng=eng, fns=fns, deps=deps, after=deps | soft, dur=dur, done=done, lat=lat,
-                        bias=OPT["bias"].get(stage[0], 0)))
+        place = 0 if not ops or ops[-1]["step"][0] != stage[0] else ops[-1]["step"][1] + 1
+        ops.append(dict(eng=eng, step=(stage[0], place), fns=fns, deps=deps, after=deps | soft, dur=dur, done=done, lat=lat,
+                        gather=gather, scatter=scatter))
         return me
 
-    CY, GF = 0.00083, 1.45
-
     def vd(cyc):
-        return 0.06 + CY * max(64, cyc)
+        return 0.03 + CY * max(64, cyc)
 
     def fast(*tiles):
         return 0.5 if all(size(t) == 2 for t in tiles) else 1
@@ -167,7 +258,7 @@ def rank_program(g, core, T, topo):
                 kw["accum_out"] = ap(accum)
             return g.scalar.activation(ap(out, rows), ap(a, rows), f, **kw)
         rd = [a] + [s for s in (bias, scale) if isinstance(s, tuple)]
-        return op("s", [call], rd, [out] + ([accum] if accum else []), 0.08 + CY * cnt(out))
+        return op("s", [call], rd, [out] + ([accum] if accum else []), 0.04 + CY * cnt(out))
 
     def win(a, off):
         return T[a[0]][:, a[1]:a[2]].indirect(ap(off))
@@ -175,15 +266,15 @@ def rank_program(g, core, T, topo):
     def gat(eng, out, a, off):
         n = cnt(out)
         if eng == "v":
-            return op("v", [lambda: g.vector.tensor_copy(ap(out), win(a, off))], [a, off], [out], 0.05 + CY * GF * n)
-        return op("s", [lambda: g.scalar.activation(ap(out), win(a, off), AF.Copy)], [a, off], [out], 0.065 + CY * GF * n)
+            return op("v", [lambda: g.vector.tensor_copy(ap(out), win(a, off))], [a, off], [out], 0.05, gather=n)
+        return op("s", [lambda: g.scalar.activation(ap(out), win(a, off), AF.Copy)], [a, off], [out], 0.065, gather=n)
 
     def gtt(out, a, off, b, o):
         return op("v", [lambda: g.vector.tensor_tensor(ap(out), win(a, off), ap(b), o)], [a, off, b], [out],
-                  0.05 + CY * GF * cnt(out))
+                  0.05, gather=cnt(out))
 
     def scat(a, off, src):
-        return op("v", [lambda: g.vector.tensor_copy(win(a, off), ap(src))], [src, off], [a], 0.05 + CY * 3.8 * cnt(src))
+        return op("v", [lambda: g.vector.tensor_copy(win(a, off), ap(src))], [src, off], [a], 0.05, scatter=cnt(src))
 
     def mm(calls, start=True, stop=True, rows=128, out_rows=128, cont=False):
         fns, rd, wr, cyc = [], [], [], 0
@@ -194,7 +285,7 @@ def rank_program(g, core, T, topo):
             rd += [l, r]
             wr.append(o_)
             cyc += max(min(64, cnt(l)), cnt(r)) * (4 if size(l) == 4 else 1)
-        return op("t", fns, list(dict.fromkeys(rd)), list(dict.fromkeys(wr)), 0.05 + cyc * 0.00042, cont=cont)
+        return op("t", fns, list(dict.fromkeys(rd)), list(dict.fromkeys(wr)), cyc * 0.00042, lat=0.05, cont=cont)
 
     def sums(groups, **kw):
         fns, rd, wr, cyc = [], [], [], 0
@@ -210,7 +301,7 @@ def rank_program(g, core, T, topo):
                 rd += [l, r]
                 wr.append(o_)
                 cyc += max(min(64, cnt(l)), cnt(r)) * (4 if size(l) == 4 else 1)
-        return op("t", fns, list(dict.fromkeys(rd)), list(dict.fromkeys(wr)), 0.05 + cyc * 0.00042)
+        return op("t", fns, list(dict.fromkeys(rd)), list(dict.fromkeys(wr)), cyc * 0.00042, lat=0.05)
 
     def gps(fn, rd, wr, dur):
         return op("g", [fn], rd, wr, dur)
@@ -221,12 +312,12 @@ def rank_program(g, core, T, topo):
         sem = "dma%d" % n_dma[0]
         n_dma[0] += 1
         q = g.sync if eng == "y" else g.scalar
-        return op(eng, [lambda: q.dma_start(out_ap, in_ap)], rd, wr, 0.1, done=(sem, 16), lat=dur)
+        return op(eng, [lambda: q.dma_start(out_ap, in_ap)], rd, wr, 0.06, done=(sem, 16), lat=0.75 * dur)
 
     def ps(bank, a, b, s=1):
         return ("ps%d" % bank, a, b, s)
 
-    xs, dn = whole("xs", W + EXT), whole("dn", ND)
+    xs, dn = whole("xs", W + EXT), ("dn", ND // 2, 3 * ND // 2, 1)
     zed0, rend0, lend0 = whole("zed0", LANES), whole("rend0", LANES), whole("lend0", LANES)
     dma(T.zed0[:], T.zed[:], [], [zed0])
     dma(T.wt0[:], T.wt[:], [], [whole("wt0", 1)], "s")
@@ -234,7 +325,7 @@ def rank_program(g, core, T, topo):
     dma(T.xs[:, 0:W], T.stock[:], [], [sub(xs, 0, W)], dur=4.0)
     dma(T.xs[:, W:W + EXT], T.stock[:, 0:EXT], [], [sub(xs, W, W + EXT)])
     dma(T.rend0[:], T.rend[:], [], [rend0])
-    dma(T.dn[:, 0:ND], T.donor[:], [], [dn], dur=3.0)
+    dma(ap(dn), T.donor[:], [], [dn], dur=3.0)
     dma(T.cnt0[:], T.cnt[:], [], [whole("cnt0", LANES)])
     dma(T.lim0[:], T.lim[:], [], [whole("lim0", 2)])
     dma(T.lend0[:], T.lend[:], [], [lend0])
@@ -309,6 +400,7 @@ def rank_program(g, core, T, topo):
     ts(k29, kci, 29.0, OP.mult)
     ts(k256, kci, 256.0, OP.mult)
     E = shifted(G8)
+    En = shifted(times(G8, -0.0625))
     KD1, KD2 = alloc("pb", 128), alloc("pb", 128)
     ts(KD1, mq, kc, OP.is_equal, kapf, OP.mult)
     ts(KD2, mq, kc, OP.is_equal, k256, OP.mult)
@@ -316,8 +408,8 @@ def rank_program(g, core, T, topo):
     l16, l8c, l4c = alloc("pb", 16), alloc("pb", 16), alloc("pb", 16)
     ts(il, q16, kc, OP.add)
     ts(l16, il, 16.0, OP.mult)
-    ts(l4c, il, 4.0, OP.mult)
     for b in range(2):
+        ts(sub(l4c, b * NQ, (b + 1) * NQ), sub(il, 0, NQ), 4.0, OP.mult, (1 - b) * ND / 2, OP.add)
         ts(sub(l8c, b * NQ, (b + 1) * NQ), sub(il, 0, NQ), 8.0, OP.mult)
     g8 = alloc("pb", 8)
     cp(g8, G8)
@@ -325,8 +417,9 @@ def rank_program(g, core, T, topo):
     ts(not15, kc, 14.5, OP.is_lt)
     ts(one_k, kc, -1.0, OP.mult, 1.0, OP.add)
     row1 = col()
-    ts(row1, kc, 1.0, OP.is_equal, 4.0, OP.mult)
-    E1 = shifted(times(G8, row1))
+    ts(row1, kc, 1.0, OP.is_equal, 2.0, OP.mult)
+    g1 = times(G8, row1)
+    E1 = [shifted(times(g1, -1.0)), shifted(g1)]
     ETA = alloc("pb", 2048)
     iota(ETA, [[0, 2048]], 1, 0)
     sel(ETA, ETA, [[-1, 16], [-16, 8], [0, 16]], OP.is_equal, 0, 1)
@@ -388,24 +481,22 @@ def rank_program(g, core, T, topo):
 
     def early(t, b):
         s = state[b]
-        P = banks(b)[0]
+        P, Q, Rb = banks(b)
         z2 = s["z2"]
-        U = ps(P, 0, UW)
-        weighted = [(ps(P, 0, w), WB, z2)] + [(ps(P, w, UW), EW(r), sub(z2, r, w, 16)) for r in range(16)]
-        mm([(U, CM, sub(ones144, 0, UW))] + weighted)
-        r4 = til("pb", UW, "r4", t, b)
+        U, UL = ps(P, 0, w), ps(Rb, 0, NQ)
+        sums([(U, [(CM, ones), (WB, z2)])])
+        r4 = til("pb", w, "r4", t, b)
         ts(r4, U, M4096, OP.add, M4096, OP.subtract)
-        mm([(U, CP, sub(ones144, 0, UW))] + weighted + [(U, nID, r4)])
+        sums([(U, [(CP, ones), (WB, z2), (nID, r4)])])
         sq, sql, up, zm = til("pf", w, "sq", t, b), til("pf", NQ, "sql", t, b), til("pf", w, "up", t, b), til("pf", w, "zm", t, b)
         ul = sub(til("pi", 2 * NQ, "ul", t, 0), b * NQ, (b + 1) * NQ)
-        act(sq, ps(P, 0, w), AF.Square, bias=sqb)
-        act(sql, ps(P, w, UW), AF.Square, bias=m32)
-        act(up, ps(P, 0, w), AF.Copy)
-        ts(ul, ps(P, w, UW), -32.0, OP.add)
+        act(sq, U, AF.Square, bias=sqb)
+        act(up, U, AF.Copy)
+        sums([(UL, [(EW(r), sub(z2, r, w, 16)) for r in range(16)] + [(En(r), sub(r4, r, w, 16)) for r in range(16)])])
+        act(sql, UL, AF.Square)
+        cp(ul, UL)
         act(zm, z2, AF.Copy, scale=0.5, bias=-0.5)
         s.update(sq=sq, sql=sql, up=up, ul=ul, zm=zm)
-    m32 = col()
-    fill(m32, -32.0)
 
     def front(t, b, A, AL):
         s = state[b]
@@ -413,7 +504,7 @@ def rank_program(g, core, T, topo):
 
         def ti(key, n=w):
             return til("pi", n, key, t, b)
-        ci, c, cil = ti("ci"), ti("c"), ti("cil", NQ)
+        ci, c, cil = ti("ci"), ti("c"), til("pf", NQ, "cil", t, b)
         cl = til("pu", w, "cl", t, b)
         ts(ci, s["sq"], 0.03125, OP.mult, A, OP.add)
         ts(c, ci, 2047, OP.bitwise_and)
@@ -423,10 +514,10 @@ def rank_program(g, core, T, topo):
             gat("v", sub(Gb[b], 16 * gs, H16), sub(xs, 0, W), sub(cl, gs, w))
         if gs:
             gat("s", sub(Gb[b], 0, 16 * gs), sub(xs, 0, W), sub(cl, 0, gs))
-        ts(cil, s["sql"], 0.03125, OP.mult, AL, OP.add)
+        act(cil, s["sql"], AF.Identity, scale=0.03125, bias=AL)
         pp, p2 = ti("pp", 2 * w), ti("p2", 2 * w)
         ll = til("pu", 2 * w, "ll", t, b)
-        raw = [r for r in OPT["runs"][b] if r[2] == "raw"]
+        raw = [r for r in OPT["runs"][b] if r[2] == "raw"] or not OPT["joint"][b]
         tt(sub(pp, w, 2 * w), s["R"], ps(P, 0, w), OP.mult)
         if raw:
             ts(sub(p2, w, 2 * w), sub(pp, w, 2 * w), 5, OP.arith_shift_right, 2047, OP.bitwise_and)
@@ -582,10 +673,10 @@ def rank_program(g, core, T, topo):
         if not last:
             send("r", t, b, sub(ro, 0, 4 * w))
         sums([(ps(Rb, 0, NQ), [(ID, sub(l4c, b * NQ, (b + 1) * NQ)), (ID, s["u3"])]
-               + [(E1(r), sub(Nd, r, w, 16)) for r in range(16)])])
+               + [(E1[b](r), sub(Nd, r, w, 16)) for r in range(16)])])
         dlu = til("pu", NQ, "dlu", t, b)
         cp(dlu, ps(Rb, 0, NQ))
-        scat(whole("dn", 2 * ND), dlu, Ln)
+        scat(("dn", b * ND, (b + 1) * ND, 1), dlu, Ln)
 
     snt = {"z": 0, "r": 0}
 
@@ -596,9 +687,9 @@ def rank_program(g, core, T, topo):
         snt[k] += len(topo.engines(core, dst))
         name = "%s%d%d" % (k, t, b)
         o = op("g", [lambda: g.remote_dma(T[k + "i" + name[1:]][:], ap(tile), T.sem["a" + name], T.sem[k + "sent"], pid, rid, m)],
-               [tile], [], 1.0, done=(k + "sent", 0))
+               [tile], [], 0.4, done=(k + "sent", 0))
         n = len(topo.engines(relays(topo, cores, (rank - 1) % len(cores))["zr".index(k)], core))
-        op(None, [], [], [whole(k + "i" + name[1:], cnt(tile))], 0.0, done=("a" + name, n), lat=4.0 if k == "z" else 6.0, extra=(o,))
+        op(None, [], [], [whole(k + "i" + name[1:], cnt(tile))], 0.0, done=("a" + name, n), lat=OPT[k + "lat"], extra=(o,))
 
     AL0 = col()
     fill(AL0, -0.375)
@@ -639,51 +730,19 @@ def rank_program(g, core, T, topo):
     dma(T.yn[:], T.yn0[:], [("yn0", 0, LANES, 1)], [])
     for b in range(2):
         lo, hi = b * W // 2, (b + 1) * W // 2
-        dma(T.yx[:, lo:hi], T.xs[:, lo:hi], [sub(xs, lo, hi)], [])
-    dma(T.yd[:], T.dn[:, 0:ND], [dn], [])
+        dma(T.yx[:, lo:hi], T.xs[:, lo:hi], [sub(xs, lo, hi)], [], dur=4.0)
+        dma(T.yd[:, lo // 2:hi // 2], ap(sub(dn, lo // 2, hi // 2)), [sub(dn, lo // 2, hi // 2)], [], dur=3.0)
 
-    N = len(ops)
-    succ = [[] for _ in range(N)]
-    for i, o in enumerate(ops):
-        for d in o["after"]:
-            succ[d].append(i)
-    prio = [0.0] * N
-    for i in range(N - 1, -1, -1):
-        prio[i] = ops[i]["dur"] + ops[i]["lat"] + 0.06 + max([prio[j] for j in succ[i]] + [0.0])
-    left = [len(o["after"]) for o in ops]
-    ready = {e: [] for e in ("v", "s", "t", "g", "y", None)}
-    avail = [0.0] * N
-    free = {e: 0.0 for e in ready}
-    for i in range(N):
-        if left[i] == 0:
-            ready[ops[i]["eng"]].append(i)
-    order = []
-    while len(order) < N:
-        best = None
-        for e, lst in ready.items():
-            if lst:
-                st = max(free[e], min(avail[i] for i in lst)) if e is not None else min(avail[i] for i in lst)
-                if best is None or st < best[0]:
-                    best = (st, e)
-        st, e = best
-        i = max((j for j in ready[e] if avail[j] <= st + 1e-9), key=lambda j: prio[j] + ops[j]["bias"])
-        ready[e].remove(i)
-        end = st + ops[i]["dur"]
-        if e is not None:
-            free[e] = end
-        order.append((st, i))
-        for j in succ[i]:
-            left[j] -= 1
-            avail[j] = max(avail[j], end + ops[i]["lat"] + 0.06)
-            if left[j] == 0:
-                ready[ops[j]["eng"]].append(j)
+    if not ORDER:
+        ORDER.extend(schedule(ops))
+    order = ORDER
 
     QUEUE = {"v": g.vector, "s": g.scalar, "t": g.tensor, "g": g, "y": g.sync}
     SEM = {"v": "sv", "s": "ss", "t": "st", "g": "sg"}
     made = {k: 0 for k in SEM.values()}
     know = {e: {} for e in QUEUE}
     final = {}
-    for st, i in order:
+    for i in order:
         o = ops[i]
         e = o["eng"]
         if e is None:

@@ -9,9 +9,10 @@ B = 256.0
 
 OPT = dict(
     gs=(64, 64),
-    runs=(((64, "v", "raw"), (64, "s", "raw")), ((64, "s", "va"), (64, "v", "va"))),
-    bias={}, slack=0.2, turns=12000, heat=0.5, seed=1, joint=(True, True), zlat=2.6, rlat=4.2,
-    models=((1.35, 2.5, 1.0, 1.0, 0.2), (1.1, 2.0, 1.0, 0.8, 0.17), (1.8, 5.0, 1.25, 1.4, 0.24)),
+    runs=(((64, "v", "raw"), (64, "s", "raw")), ((32, "s", "va"),) * 4),
+    gp=(128, 16), hp=16, yp=16, three=True, pc=500, sp=32, fp=16, va=((), ()),
+    bias={}, slack=0.2, turns=1000, heat=2, aim=90, swaps=24000, heat2=0.8, share=10 ** 6, heat3=-9, tied=70, seed=1, joint=(False, False), zlat=2.6, rlat=4.2,
+    models=((1.35, 2.5, 1.0, 1.0, 0.2), (1.7, 4.5, 1.15, 1.3, 0.23)),
 )
 CY = 0.00083
 LOG = []
@@ -79,9 +80,11 @@ def schedule(ops):
     costs = [([(o["dur"] + CY * (gf * o["gather"] + sf * o["scatter"])) * f for o in ops],
               [o["lat"] * lf + hop for o in ops]) for gf, sf, f, lf, hop in OPT["models"]]
     dur, lat = costs[0]
+    need = [sorted(o["deps"]) for o in ops]
     way = [0.0] * n
     for i in range(n - 1, -1, -1):
-        way[i] = dur[i] + lat[i] + max([way[j] for j in succ[i]] + [0.0])
+        way[i] = dur[i] + max([way[j] + (lat[i] if i in ops[j]["deps"] else 0) for j in succ[i]] + [lat[i]])
+    hard = [[(j, i in ops[j]["deps"]) for j in succ[i]] for i in range(n)]
     slack = OPT["slack"]
 
     def plan(prio):
@@ -111,27 +114,30 @@ def schedule(ops):
             end += lat[i]
             if end > span:
                 span = end
-            for j in succ[i]:
-                if end > avail[j]:
+            for j, waits in hard[i]:
+                if waits and end > avail[j]:
                     avail[j] = end
                 left[j] -= 1
                 if not left[j]:
                     ready[eng[j]].append(j)
                     if avail[j] < first[eng[j]]:
                         first[eng[j]] = avail[j]
-        for d2, l2 in costs[1:]:
-            done, free = [0.0] * n, [0.0] * 6
-            for i in order:
-                st = free[eng[i]]
-                for j in pred[i]:
-                    if done[j] > st:
-                        st = done[j]
-                st += d2[i]
-                if eng[i] != 5:
-                    free[eng[i]] = st
-                done[i] = st + l2[i]
-            span += max(done)
-        return span / len(costs), order
+        return (span + sum(max(play(order, c)) for c in costs[1:])) / len(costs), order
+
+    def play(order, cost):
+        d2, l2 = cost
+        done, free = [0.0] * n, [0.0] * 6
+        for i in order:
+            e = eng[i]
+            st = free[e]
+            for j in need[i]:
+                if done[j] > st:
+                    st = done[j]
+            st += d2[i]
+            if e != 5:
+                free[e] = st
+            done[i] = st + l2[i]
+        return done
     steps = sorted(set(o["step"] for o in ops))
     off = {k: OPT["bias"].get(k[0], 0.0) for k in steps}
     seed = [OPT["seed"]]
@@ -139,14 +145,109 @@ def schedule(ops):
     def draw(k):
         seed[0] = (seed[0] * 1103515245 + 12345) % 2 ** 31
         return (seed[0] >> 8) % k
+    def held(order):
+        done, free, last, by = [0.0] * n, [0.0] * 6, [None] * 6, [None] * n
+        for i in order:
+            st, by[i] = free[eng[i]], (last[eng[i]], True)
+            for j in need[i]:
+                if done[j] >= st:
+                    st, by[i] = done[j], (j, False)
+            if eng[i] != 5:
+                free[eng[i]], last[eng[i]] = st + dur[i], i
+            done[i] = st + dur[i] + lat[i]
+        i, pairs = done.index(max(done)), []
+        while by[i][0] is not None:
+            if by[i][1] and by[i][0] not in pred[i]:
+                pairs.append((by[i][0], i))
+            i = by[i][0]
+        return pairs
     now, order = best = plan([way[i] + off[ops[i]["step"]] for i in range(n)])
+    pairs = held(order)
     for turn in range(OPT["turns"]):
         new = dict(off)
-        for _ in range(1 + draw(3)):
-            new[steps[draw(len(steps))]] += (-4, -2, -1, -0.5, 0.5, 1, 2, 4)[draw(8)]
+        if pairs and draw(100) < OPT["aim"]:
+            a, b = pairs[draw(len(pairs))]
+            gap = abs(way[a] + off[ops[a]["step"]] - way[b] - off[ops[b]["step"]]) + (0.1, 0.5, 1, 2)[draw(4)]
+            if draw(2):
+                new[ops[a]["step"]] -= gap
+            else:
+                new[ops[b]["step"]] += gap
+        else:
+            for _ in range(1 + draw(2)):
+                new[steps[draw(len(steps))]] += (-4, -2, -1, -0.5, 0.5, 1, 2, 4)[draw(8)]
         span, order = plan([way[i] + new[ops[i]["step"]] for i in range(n)])
         if span <= now + OPT["heat"] * (1 - turn / OPT["turns"]) * (draw(1000) / 1000) ** 3:
+            if span != now:
+                pairs = held(order)
             now, off = span, new
+            if span < best[0]:
+                best = (span, order)
+
+    def moved(order, a, b, early):
+        p, q = order.index(a), order.index(b)
+        mid = order[p:q + 1]
+        mark = {b if early else a}
+        for i in (mid[::-1] if early else mid):
+            if any(j in mark for j in (succ[i] if early else pred[i])):
+                mark.add(i)
+        if (a if early else b) in mark:
+            return None
+        one, two = [i for i in mid if i in mark], [i for i in mid if i not in mark]
+        return order[:p] + (one + two if early else two + one) + order[q + 1:]
+    def value(order):
+        return sum(max(play(order, c)) for c in costs) / len(costs)
+
+    def alike(order, v):
+        done = play(order, costs[0])
+        at = {(ops[i]["step"], ops[i]["visit"]): done[i] - lat[i] - dur[i] for i in range(n)}
+        ref = ("front0", 0)
+        period = at[ref, v + 1] - at[ref, v]
+        lag = {k: t - v for (k, t), x in at.items() if at[ref, v] <= x < at[ref, v + 1]}
+        aim = []
+        for o in ops:
+            k, t = o["step"], o["visit"]
+            u = t - lag.get(k, 0)
+            if k in lag and 1 <= u < VISITS - 1:
+                aim.append(at[k, v + lag[k]] - at[ref, v] + at[ref, 1] + (u - 1) * period)
+            else:
+                aim.append(at[k, t] + (u > 0) * (at[ref, 1] + (VISITS - 2) * period - at[ref, VISITS - 1]))
+        left, ready, new = [len(p) for p in pred], [i for i in range(n) if not pred[i]], []
+        while ready:
+            i = min(ready, key=lambda j: aim[j])
+            ready.remove(i)
+            new.append(i)
+            for j in succ[i]:
+                left[j] -= 1
+                if not left[j]:
+                    ready.append(j)
+        return new
+    which = {(o["step"], o["visit"]): i for i, o in enumerate(ops)}
+    now, order = best
+    pairs = held(order)
+    for turn in range(OPT["swaps"]):
+        if turn % OPT["share"] == OPT["share"] - 1:
+            span, new = min((value(x), x) for x in (alike(best[1], v) for v in range(1, VISITS - 1)))
+            if span < now + OPT["heat3"]:
+                now, order = span, new
+                pairs = held(order)
+        a, b = pairs[draw(len(pairs))]
+        for _ in range(draw(3)):
+            before = [i for i in order[max(0, order.index(a) - 12):order.index(a)] if eng[i] == eng[a]]
+            a = before[-1] if before else a
+        early = draw(2)
+        new = moved(order, a, b, early)
+        if new is None:
+            continue
+        if draw(100) < OPT["tied"]:
+            for d in range(1 - VISITS, VISITS):
+                x, y = which.get((ops[a]["step"], ops[a]["visit"] + d)), which.get((ops[b]["step"], ops[b]["visit"] + d))
+                if d and x and y and new.index(x) < new.index(y) < new.index(x) + 60:
+                    new = moved(new, x, y, early) or new
+        done = play(new, costs[0])
+        span = (max(done) + sum(max(play(new, c)) for c in costs[1:])) / len(costs)
+        if span <= now + OPT["heat2"] * (1 - turn / OPT["swaps"]) * (draw(1000) / 1000) ** 2:
+            now, order = span, sorted(new, key=lambda i: done[i] - lat[i] - dur[i])
+            pairs = held(order)
             if span < best[0]:
                 best = (span, order)
     LOG.append((ops, way, succ, best[0]))
@@ -190,7 +291,7 @@ def rank_program(g, core, T, topo):
     def size(t):
         return 4 if t[0][:2] == "ps" else SIZE.get(t[0], 2)
 
-    stage = ["c"]
+    stage = ["c", 0]
 
     def op(eng, fns, reads, writes, dur, done=None, lat=0.0, extra=(), cont=False, gather=0, scatter=0):
         me = len(ops)
@@ -203,13 +304,13 @@ def rank_program(g, core, T, topo):
                 keep = []
                 for (a, b, o, w_) in acc.get(name, []):
                     if o != me and a < hi and lo < b and (wr or w_ or bank):
-                        (soft if cont and bank and ops[o]["eng"] == "t" else deps).add(o)
+                        (soft if bank and ops[o]["eng"] == eng else deps).add(o)
                     if o == me or not ((wr or bank) and lo <= a and b <= hi):
                         keep.append((a, b, o, w_))
                 keep.append((lo, hi, me, wr or bank))
                 acc[name] = keep
         place = 0 if not ops or ops[-1]["step"][0] != stage[0] else ops[-1]["step"][1] + 1
-        ops.append(dict(eng=eng, step=(stage[0], place), fns=fns, deps=deps, after=deps | soft, dur=dur, done=done, lat=lat,
+        ops.append(dict(eng=eng, step=(stage[0], place), visit=stage[1], fns=fns, deps=deps, after=deps | soft, dur=dur, done=done, lat=lat,
                         gather=gather, scatter=scatter))
         return me
 
@@ -239,8 +340,8 @@ def rank_program(g, core, T, topo):
     def fill(out, v):
         return op("v", [lambda: g.vector.memset(ap(out), v)], [], [out], vd(cnt(out) * size(out) / 4))
 
-    def scan(out, d0, d1, first):
-        return op("v", [lambda: g.vector.tensor_tensor_scan(ap(out), ap(d0), ap(d1), first, OP.min, OP.max)],
+    def scan(out, d0, d1, first, o0=OP.min, o1=OP.max):
+        return op("v", [lambda: g.vector.tensor_tensor_scan(ap(out), ap(d0), ap(d1), first, o0, o1)],
                   [d0, d1], [out], vd(fast(out, d0, d1) * cnt(out)))
 
     def act(out, a, f, scale=1.0, bias=0.0, accum=None, rows=128):
@@ -277,31 +378,22 @@ def rank_program(g, core, T, topo):
         return op("v", [lambda: g.vector.tensor_copy(win(a, off), ap(src))], [src, off], [a], 0.05, scatter=cnt(src))
 
     def mm(calls, start=True, stop=True, rows=128, out_rows=128, cont=False):
+        pe([(o_, l, r, start and j == 0, stop and j == len(calls) - 1) for j, (o_, l, r) in enumerate(calls)], rows, out_rows)
+
+    def sums(groups, rows=128, out_rows=128):
+        pe([(r[0] if len(r) == 2 else out, l, r[1] if len(r) == 2 else r, j == 0, j == len(pairs) - 1)
+            for out, pairs in groups for j, (l, r) in enumerate(pairs)], rows, out_rows)
+
+    def pe(calls, rows, out_rows):
         fns, rd, wr, cyc = [], [], [], 0
-        for j, (o_, l, r) in enumerate(calls):
-            def call(o_=o_, l=l, r=r, a=start and j == 0, z=stop and j == len(calls) - 1):
-                return g.tensor.matmul(ap(o_, out_rows), ap(l, rows), ap(r, rows), a, z)
-            fns.append(call)
+        for j, (o_, l, r, a, z) in enumerate(calls):
+            fns.append(lambda o_=o_, l=l, r=r, a=a, z=z: g.tensor.matmul(ap(o_, out_rows), ap(l, rows), ap(r, rows), a, z))
             rd += [l, r]
             wr.append(o_)
             cyc += max(min(64, cnt(l)), cnt(r)) * (4 if size(l) == 4 else 1)
-        return op("t", fns, list(dict.fromkeys(rd)), list(dict.fromkeys(wr)), cyc * 0.00042, lat=0.05, cont=cont)
-
-    def sums(groups, **kw):
-        fns, rd, wr, cyc = [], [], [], 0
-        for out, pairs in groups:
-            for j, (l, r) in enumerate(pairs):
-                o_ = out
-                if len(r) == 2:
-                    o_, r = r
-
-                def call(o_=o_, l=l, r=r, a=j == 0, z=j == len(pairs) - 1):
-                    return g.tensor.matmul(ap(o_, kw.get("out_rows", 128)), ap(l, kw.get("rows", 128)), ap(r, kw.get("rows", 128)), a, z)
-                fns.append(call)
-                rd += [l, r]
-                wr.append(o_)
-                cyc += max(min(64, cnt(l)), cnt(r)) * (4 if size(l) == 4 else 1)
-        return op("t", fns, list(dict.fromkeys(rd)), list(dict.fromkeys(wr)), cyc * 0.00042, lat=0.05)
+            if cyc >= OPT["pc"] or j == len(calls) - 1:
+                op("t", fns, list(dict.fromkeys(rd)), list(dict.fromkeys(wr)), cyc * 0.00042, lat=0.05)
+                fns, rd, wr, cyc = [], [], [], 0
 
     def gps(fn, rd, wr, dur):
         return op("g", [fn], rd, wr, dur)
@@ -348,8 +440,8 @@ def rank_program(g, core, T, topo):
     pidx, q16 = alloc("pi", 1), alloc("pi", 16)
     iota(pidx, [[0, 1]], 0, 1)
     iota(q16, [[16, 16]], 0, 0)
-    mq = alloc("pf", 128)
-    iota(mq, [[1, 16], [0, NQ]], 0, 0)
+    mq = alloc("pf", 16)
+    iota(mq, [[1, 16]], 0, 0)
     G8 = sub(BO, 0, 128, 16)
 
     def col():
@@ -401,9 +493,26 @@ def rank_program(g, core, T, topo):
     ts(k256, kci, 256.0, OP.mult)
     E = shifted(G8)
     En = shifted(times(G8, -0.0625))
-    KD1, KD2 = alloc("pb", 128), alloc("pb", 128)
-    ts(KD1, mq, kc, OP.is_equal, kapf, OP.mult)
-    ts(KD2, mq, kc, OP.is_equal, k256, OP.mult)
+    KD1, KD2 = times(ID, kapf), times(ID, k256)
+    g8n, g8z = times(G8, -4096.0), times(G8, 2048.0)
+    RSK, QM, ZS, REP = alloc("pb", 128), alloc("pb", 64), alloc("pb", 240), alloc("pu", 4)
+    fill(RSK, -1.0)
+    fill(sub(RSK, 0, 128, 16), 2.0 ** 25)
+    sel(QM, sub(ones, 0, 64), [[0, 8], [-16, 8]], OP.is_ge, 0, 1)
+    sel(QM, QM, [[0, 8], [16, 8]], OP.is_ge, 15, -1)
+    fill(ZS, 0.0)
+    ts(sub(ZS, 112, 128), mq, kc, OP.is_equal)
+    hi8, r4i = col(), alloc("pi", 4)
+    ts(hi8, kc, 7.5, OP.is_gt)
+    iota(r4i, [[2, 4]], 0, 0)
+    ts(REP, r4i, hi8, OP.add)
+    RSE, REE = alloc("pb", 128), alloc("pu", 4)
+    fill(RSE, 1.0)
+    fill(sub(RSE, 0, 128, 16), 0.0)
+    ts(REE, REP, 16.0, OP.mult, 15.0, OP.add)
+
+    def SG(j):
+        return sub(ZS, 112 - 16 * j, 240 - 16 * j)
     il = alloc("pi", 16)
     l16, l8c, l4c = alloc("pb", 16), alloc("pb", 16), alloc("pb", 16)
     ts(il, q16, kc, OP.add)
@@ -498,6 +607,11 @@ def rank_program(g, core, T, topo):
         act(zm, z2, AF.Copy, scale=0.5, bias=-0.5)
         s.update(sq=sq, sql=sql, up=up, ul=ul, zm=zm)
 
+    def lanes(eng, out, a, off, lo, hi, piece):
+        for j in range(lo, hi, piece):
+            e = min(hi, j + piece)
+            gat(eng, sub(out, 16 * j, 16 * e), a, sub(off, j, e))
+
     def front(t, b, A, AL):
         s = state[b]
         P, Q, Rb = banks(b)
@@ -510,44 +624,43 @@ def rank_program(g, core, T, topo):
         ts(c, ci, 2047, OP.bitwise_and)
         cp(cl, c)
         gs = OPT["gs"][b]
-        if gs < w:
-            gat("v", sub(Gb[b], 16 * gs, H16), sub(xs, 0, W), sub(cl, gs, w))
-        if gs:
-            gat("s", sub(Gb[b], 0, 16 * gs), sub(xs, 0, W), sub(cl, 0, gs))
+        lanes("v", Gb[b], sub(xs, 0, W), cl, gs, w, OPT["gp"][b])
+        lanes("s", Gb[b], sub(xs, 0, W), cl, 0, gs, w)
         act(cil, s["sql"], AF.Identity, scale=0.03125, bias=AL)
         pp, p2 = ti("pp", 2 * w), ti("p2", 2 * w)
         ll = til("pu", 2 * w, "ll", t, b)
-        raw = [r for r in OPT["runs"][b] if r[2] == "raw"] or not OPT["joint"][b]
+        raw = [r for r in OPT["runs"][b] if r[2][:3] == "raw"] or not OPT["joint"][b]
         tt(sub(pp, w, 2 * w), s["R"], ps(P, 0, w), OP.mult)
         if raw:
             ts(sub(p2, w, 2 * w), sub(pp, w, 2 * w), 5, OP.arith_shift_right, 2047, OP.bitwise_and)
             ts(sub(ll, w, 2 * w), sub(p2, w, 2 * w), k29, OP.add)
             lo = 0
             for n, _y, how in OPT["runs"][b]:
-                if how == "raw":
-                    gat("s", sub(Hb[b], 16 * lo, 16 * (lo + n)), xs, sub(ll, w + lo, w + lo + n))
+                if how[:3] == "raw":
+                    lanes(how[3:] or "s", Hb[b], xs, sub(ll, w, 2 * w), lo, lo + n, OPT["hp"] if how[3:] else w)
                 lo += n
-        k0 = til("pf", 8 * NQ, "k0", t, b)
+        on_v = OPT["va"][b]
+        mm([(ps(Q, 0, w), ones, KD1), (ps(Q, 0, w), ones, KD2)]
+           + [(ps(Q, m, w, 16), x, y) for mc in on_v for m in range(4 * mc, 4 * mc + 4)
+              for x, y in ((sub(Gb[b], m, H16, 16), g8n), (s["z2"], g8z))], stop=False)
         for mc in range(4):
-            D = mc % 2
+            D = (0, 1, Rb, 0)[mc] if OPT["three"] else mc % 2
             sums([(ps(D, j * w, (j + 1) * w), [(ID, sub(Gb[b], 4 * mc + j, H16, 16)), (hID, s["z2"])]) for j in range(4)])
-            act(sub(ADb[b], mc * 4 * w, (mc + 1) * 4 * w), ps(D, 0, 512), AF.Abs, scale=4096.0)
-            if mc % 2 == 1:
-                h = mc // 2
-                K = ps(Q if h == 0 else Rb, 0, 8 * NQ)
-                sums([(K, [(BO, sub(KD1, 64 * h, 64 * h + 64)), (BO, sub(KD2, 64 * h, 64 * h + 64))]
-                       + [(E(r), sub(ADb[b], h * 8 * w + r, (h + 1) * 8 * w, 16)) for r in range(16)])])
-                if h == 0:
-                    act(k0, K, AF.Copy)
-        t1, t2, t3 = [til("pf", n, "tm%d" % n, t, b) for n in (64, 32, 16)]
+            ad = sub(ADb[b], mc * 4 * w, (mc + 1) * 4 * w)
+            if mc in on_v:
+                ts(ad, ps(D, 0, 512), 0.0, OP.max, 8192.0, OP.mult)
+            else:
+                act(ad, ps(D, 0, 512), AF.Abs, scale=4096.0)
+            mm([(ps(Q, 4 * mc + j, w, 16), sub(ad, j * w, (j + 1) * w), g8) for j in range(4)], start=False, stop=mc == 3, cont=True)
+        run, rep = til("pf", w, "run", t, b), til("pb", 8 * NQ, "rep", t, b)
         vi, ka, pa, pc, cd, cx = [ti(k, NQ) for k in ("vi", "ka", "pa", "pc", "cd", "cx")]
         cdu, cxu = til("pu", NQ, "cdu", t, b), til("pu", NQ, "cxu", t, b)
-        tt(t1, ps(Rb, 0, 64), k0, OP.min)
-        tt(t2, sub(t1, 0, 32), sub(t1, 32, 64), OP.min)
-        tt(t3, sub(t2, 0, 16), sub(t2, 16, 32), OP.min)
-        tt(vi, sub(t3, 0, 8), sub(t3, 8, 16), OP.min)
+        scan(run, RSK, ps(Q, 0, w), 0.0, OP.max, OP.min)
+        cp(vi, sub(run, 15, w, 16))
         ts(ka, vi, 255, OP.bitwise_and)
-        tt(pa, ka, s["ul"], OP.mult)
+        gtt(rep, ka, REP, QM, OP.mult)
+        sums([(ps(Rb, 0, NQ), [(SG(j), sub(rep, NQ * j, NQ * j + NQ)) for j in range(8)])])
+        tt(pa, ps(Rb, 0, NQ), s["ul"], OP.mult)
         tt(pc, pa, cil, OP.add)
         ts(cd, pc, 1023, OP.bitwise_and)
         cp(cdu, cd)
@@ -581,15 +694,19 @@ def rank_program(g, core, T, topo):
         lo, mins = 0, False
         for n, who, how in OPT["runs"][b]:
             a, e = 16 * lo, 16 * (lo + n)
-            gat(who, sub(y, a, e), xs, sub(ll, lo, lo + n))
-            scan(sub(mx, a, e - 1), sub(y, a, e - 1), sub(y, a + 1, e), 1000.0)
-            if how == "raw":
+            lanes(who, y, xs, ll, lo, lo + n, OPT["yp"] if who == "v" else w)
+            for j in range(a, e, 16 * OPT["sp"]):
+                k = min(e, j + 16 * OPT["sp"])
+                scan(sub(mx, j, k - 1), sub(y, j, k - 1), sub(y, j + 1, k), 1000.0)
+            if how[:3] == "raw":
                 for j in range(a, e, 512):
                     D = j // 512 % 2
                     sums([(ps(D, 0, 512), [(ID, sub(H, j, j + 512)), (nID, sub(y, j, j + 512))])])
                     act(sub(ah, j, j + 512), ps(D, 0, 512), AF.Abs)
             else:
-                gtt(sub(H, a, e), xs, sub(ll, w + lo, w + lo + n), sub(y, a, e), OP.subtract)
+                for j in range(lo, lo + n, OPT["fp"]):
+                    k = min(lo + n, j + OPT["fp"])
+                    gtt(sub(H, 16 * j, 16 * k), xs, sub(ll, w + j, w + k), sub(y, 16 * j, 16 * k), OP.subtract)
                 if how == "va":
                     act(sub(ah, a, e), sub(H, a, e), AF.Abs)
                 else:
@@ -616,7 +733,10 @@ def rank_program(g, core, T, topo):
         sums([(ps(Rb, 0, w), [(sub(al, 1, 256, 2), ID)]),
               (ps(Rb, w, 2 * w), [(sub(al, 1, 256, 2), ID), (sub(al, 0, 256, 2), nID)])])
         act(A1, ps(Rb, 0, w), AF.Copy)
-        sums([(ps(P, 0, NQ), [(ID, sub(l16, 0, NQ))] + [(E(r), sub(A1, r, w, 16)) for r in range(16)])])
+        ec, rep = til("pb", w, "ec", t, b), til("pb", 8 * NQ, "rep2", t, b)
+        scan(ec, RSE, sub(al, 1, 256, 2), 0.0, OP.mult, OP.add)
+        gtt(rep, ec, REE, QM, OP.mult)
+        sums([(ps(P, 0, NQ), [(ID, sub(l16, 0, NQ))] + [(SG(j), sub(rep, NQ * j, NQ * j + NQ)) for j in range(8)])])
         act(Dl, ps(Rb, w, 2 * w), AF.Copy, accum=sub(accs[t % 2], b, b + 1))
         yel = til("pu", NQ, "yel", t, b)
         cp(yel, ps(P, 0, NQ))
@@ -695,6 +815,7 @@ def rank_program(g, core, T, topo):
     fill(AL0, -0.375)
     A = (cA, AL0)
     for t in range(VISITS):
+        stage[1] = t
         for name, step in (("early", early), ("front", lambda t, b: front(t, b, *A))):
             for b in range(2):
                 stage[0] = name + str(b)

@@ -6,16 +6,14 @@ LANES, HALF, NQ, VISITS = 256, 128, 8, 5
 W, EXT, ND = 2048, 448, 1024
 M2, M4096 = 1.5 * 2 ** 24, 1.5 * 2 ** 35
 B = 256.0
+CY = 0.00083
 
 OPT = dict(
-    gs=(64, 64),
-    runs=(((64, "v", "raw"), (64, "s", "raw")), ((32, "s", "va"),) * 4),
-    gp=(128, 16), hp=16, yp=16, three=True, pc=500, sp=32, fp=16, va=((), ()),
-    bias={}, slack=0.2, turns=1000, heat=2, aim=90, swaps=24000, heat2=0.8, share=10 ** 6, heat3=-9, tied=70, seed=1, joint=(False, False), zlat=2.6, rlat=4.2,
-    models=((1.35, 2.5, 1.0, 1.0, 0.2), (1.7, 4.5, 1.15, 1.3, 0.23)),
+    gs=(64, 0), gp=(128, 16), picks=("ss", "ss"),
+    runs=(((64, "v", "raw"), (64, "s", "raw")), ((32, "s", "less"),) * 3 + ((32, "s", "raw"),)),
+    models=((1.3, 2.4, 1.0, 0.95, 0.19), (1.45, 3.3, 1.08, 1.45, 0.21)), zlat=2.6, rlat=2.6, qlat=4.0,
+    turns=2000, swaps=36000, seed=2,
 )
-CY = 0.00083
-LOG = []
 
 SCRATCH = {
     "pi": ("sbuf", [128, 6144], "int32"), "pf": ("sbuf", [128, 4096], "float32"),
@@ -26,7 +24,8 @@ SCRATCH = {
     "kap0": ("sbuf", [128, 1], "int32"), "wt0": ("sbuf", [128, 1], "int32"), "lim0": ("sbuf", [8, 2], "int32"),
     "yn0": ("sbuf", [8, LANES], "float32"), "yz0": ("sbuf", [128, LANES], "bfloat16"),
 }
-SEMAPHORES = ["sv", "ss", "st", "sg", "zsent", "rsent"]
+KINDS = "zrq"
+SEMAPHORES = ["sv", "ss", "st", "sg", "zsent", "rsent", "qsent"]
 for _i in range(8):
     SCRATCH["ps%d" % _i] = ("psum", [128, 512], "float32")
 for _i in range(28):
@@ -34,26 +33,25 @@ for _i in range(28):
 for _t in range(VISITS):
     for _b in range(2):
         SCRATCH["zo%d%d" % (_t, _b)] = ("sbuf", [128, HALF], "bfloat16")
-        SCRATCH["ro%d%d" % (_t, _b)] = ("sbuf", [128, 5 * HALF], "bfloat16")
+        SCRATCH["ro%d%d" % (_t, _b)] = ("sbuf", [128, 4 * HALF], "bfloat16")
         if _t < VISITS - 1:
-            SCRATCH["zi%d%d" % (_t, _b)] = ("sbuf", [128, HALF], "bfloat16")
-            SCRATCH["ri%d%d" % (_t, _b)] = ("sbuf", [128, 4 * HALF], "bfloat16")
-            SEMAPHORES.append("az%d%d" % (_t, _b))
-            SEMAPHORES.append("ar%d%d" % (_t, _b))
+            for _k, _n in zip(KINDS, (1, 1, 3)):
+                SCRATCH["%si%d%d" % (_k, _t, _b)] = ("sbuf", [128, _n * HALF], "bfloat16")
+                SEMAPHORES.append("a%s%d%d" % (_k, _t, _b))
 
 
 def relays(topo, cores, q):
     src, dst = cores[q], cores[(q + 1) % len(cores)]
-    c = [h for h in topo.cores_of(src) if h not in cores and topo.die(h) == topo.die(src)
-         and topo.may_write(src, h) and topo.may_write(h, dst)]
-    return c[0], c[1 % len(c)]
+    c = [h for h in topo.cores_of(src) if h not in cores and topo.may_write(src, h) and topo.may_write(h, dst)]
+    c.sort(key=lambda h: topo.die(h) != topo.die(src))
+    return [c[j % len(c)] for j in range(len(KINDS))]
 
 
 def relay_program(g, core, T, topo, dst, src, kinds):
     n_in = len(topo.engines(src, core))
     n_out = len(topo.engines(core, dst))
     rid, pid = topo.addr(dst, core)
-    sent = {"z": 0, "r": 0}
+    sent = {k: 0 for k in KINDS}
     for t in range(VISITS - 1):
         for b in range(2):
             for k in kinds:
@@ -81,11 +79,35 @@ def schedule(ops):
               [o["lat"] * lf + hop for o in ops]) for gf, sf, f, lf, hop in OPT["models"]]
     dur, lat = costs[0]
     need = [sorted(o["deps"]) for o in ops]
+    above = [0] * n
+    for i in range(n):
+        for j in need[i]:
+            above[i] |= above[j] | 1 << j
+        need[i] = [j for j in need[i] if not any(above[k] >> j & 1 for k in need[i])]
     way = [0.0] * n
     for i in range(n - 1, -1, -1):
         way[i] = dur[i] + max([way[j] + (lat[i] if i in ops[j]["deps"] else 0) for j in succ[i]] + [lat[i]])
     hard = [[(j, i in ops[j]["deps"]) for j in succ[i]] for i in range(n)]
-    slack = OPT["slack"]
+    seed = [OPT["seed"]]
+
+    def draw(k):
+        seed[0] = (seed[0] * 1103515245 + 12345) % 2 ** 31
+        return (seed[0] >> 8) % k
+
+    def play(order, cost):
+        d2, l2 = cost
+        done, free = [0.0] * n, [0.0] * 6
+        for i in order:
+            e = eng[i]
+            st = free[e]
+            for j in need[i]:
+                if done[j] > st:
+                    st = done[j]
+            st += d2[i]
+            if e != 5:
+                free[e] = st
+            done[i] = st + l2[i]
+        return done
 
     def plan(prio):
         left = [len(p) for p in pred]
@@ -101,7 +123,7 @@ def schedule(ops):
                 x = first[k] if first[k] > free[k] else free[k]
                 if x < st:
                     st, e = x, k
-            top, lim = -1e18, st + slack
+            top, lim = -1e18, st + 0.2
             for j in ready[e]:
                 if avail[j] <= lim and prio[j] > top:
                     top, i = prio[j], j
@@ -124,27 +146,6 @@ def schedule(ops):
                         first[eng[j]] = avail[j]
         return (span + sum(max(play(order, c)) for c in costs[1:])) / len(costs), order
 
-    def play(order, cost):
-        d2, l2 = cost
-        done, free = [0.0] * n, [0.0] * 6
-        for i in order:
-            e = eng[i]
-            st = free[e]
-            for j in need[i]:
-                if done[j] > st:
-                    st = done[j]
-            st += d2[i]
-            if e != 5:
-                free[e] = st
-            done[i] = st + l2[i]
-        return done
-    steps = sorted(set(o["step"] for o in ops))
-    off = {k: OPT["bias"].get(k[0], 0.0) for k in steps}
-    seed = [OPT["seed"]]
-
-    def draw(k):
-        seed[0] = (seed[0] * 1103515245 + 12345) % 2 ** 31
-        return (seed[0] >> 8) % k
     def held(order):
         done, free, last, by = [0.0] * n, [0.0] * 6, [None] * 6, [None] * n
         for i in order:
@@ -161,11 +162,26 @@ def schedule(ops):
                 pairs.append((by[i][0], i))
             i = by[i][0]
         return pairs
-    now, order = best = plan([way[i] + off[ops[i]["step"]] for i in range(n)])
+
+    def move(order, p, q, early):
+        mid = order[p:q + 1]
+        mark = {mid[-1] if early else mid[0]}
+        for i in (mid[::-1] if early else mid):
+            if not mark.isdisjoint(succ[i] if early else pred[i]):
+                mark.add(i)
+        if (mid[0] if early else mid[-1]) in mark:
+            return False
+        one, two = [i for i in mid if i in mark], [i for i in mid if i not in mark]
+        order[p:q + 1] = one + two if early else two + one
+        return True
+
+    steps = sorted(set(o["step"] for o in ops))
+    off = {k: 0.0 for k in steps}
+    now, order = best = plan(way)
     pairs = held(order)
     for turn in range(OPT["turns"]):
         new = dict(off)
-        if pairs and draw(100) < OPT["aim"]:
+        if pairs and draw(100) < 90:
             a, b = pairs[draw(len(pairs))]
             gap = abs(way[a] + off[ops[a]["step"]] - way[b] - off[ops[b]["step"]]) + (0.1, 0.5, 1, 2)[draw(4)]
             if draw(2):
@@ -176,81 +192,39 @@ def schedule(ops):
             for _ in range(1 + draw(2)):
                 new[steps[draw(len(steps))]] += (-4, -2, -1, -0.5, 0.5, 1, 2, 4)[draw(8)]
         span, order = plan([way[i] + new[ops[i]["step"]] for i in range(n)])
-        if span <= now + OPT["heat"] * (1 - turn / OPT["turns"]) * (draw(1000) / 1000) ** 3:
+        if span <= now + 2 * (1 - turn / OPT["turns"]) * (draw(1000) / 1000) ** 3:
             if span != now:
                 pairs = held(order)
             now, off = span, new
             if span < best[0]:
                 best = (span, order)
 
-    def moved(order, a, b, early):
-        p, q = order.index(a), order.index(b)
-        mid = order[p:q + 1]
-        mark = {b if early else a}
-        for i in (mid[::-1] if early else mid):
-            if any(j in mark for j in (succ[i] if early else pred[i])):
-                mark.add(i)
-        if (a if early else b) in mark:
-            return None
-        one, two = [i for i in mid if i in mark], [i for i in mid if i not in mark]
-        return order[:p] + (one + two if early else two + one) + order[q + 1:]
-    def value(order):
-        return sum(max(play(order, c)) for c in costs) / len(costs)
-
-    def alike(order, v):
-        done = play(order, costs[0])
-        at = {(ops[i]["step"], ops[i]["visit"]): done[i] - lat[i] - dur[i] for i in range(n)}
-        ref = ("front0", 0)
-        period = at[ref, v + 1] - at[ref, v]
-        lag = {k: t - v for (k, t), x in at.items() if at[ref, v] <= x < at[ref, v + 1]}
-        aim = []
-        for o in ops:
-            k, t = o["step"], o["visit"]
-            u = t - lag.get(k, 0)
-            if k in lag and 1 <= u < VISITS - 1:
-                aim.append(at[k, v + lag[k]] - at[ref, v] + at[ref, 1] + (u - 1) * period)
-            else:
-                aim.append(at[k, t] + (u > 0) * (at[ref, 1] + (VISITS - 2) * period - at[ref, VISITS - 1]))
-        left, ready, new = [len(p) for p in pred], [i for i in range(n) if not pred[i]], []
-        while ready:
-            i = min(ready, key=lambda j: aim[j])
-            ready.remove(i)
-            new.append(i)
-            for j in succ[i]:
-                left[j] -= 1
-                if not left[j]:
-                    ready.append(j)
-        return new
     which = {(o["step"], o["visit"]): i for i, o in enumerate(ops)}
+    twins = [[which.get((o["step"], t)) for t in range(-VISITS, 2 * VISITS)] for o in ops]
     now, order = best
-    pairs = held(order)
+    first, pairs, place = max(play(order, costs[0])), held(order), {i: p for p, i in enumerate(order)}
     for turn in range(OPT["swaps"]):
-        if turn % OPT["share"] == OPT["share"] - 1:
-            span, new = min((value(x), x) for x in (alike(best[1], v) for v in range(1, VISITS - 1)))
-            if span < now + OPT["heat3"]:
-                now, order = span, new
-                pairs = held(order)
         a, b = pairs[draw(len(pairs))]
-        for _ in range(draw(3)):
-            before = [i for i in order[max(0, order.index(a) - 12):order.index(a)] if eng[i] == eng[a]]
-            a = before[-1] if before else a
-        early = draw(2)
-        new = moved(order, a, b, early)
-        if new is None:
+        for _ in range(draw(4)):
+            a = ([a] + [i for i in order[max(0, place[a] - 12):place[a]] if eng[i] == eng[a]])[-1]
+        early, new = draw(2), list(order)
+        if not move(new, place[a], place[b], early):
             continue
-        if draw(100) < OPT["tied"]:
+        if draw(100) < 70:
             for d in range(1 - VISITS, VISITS):
-                x, y = which.get((ops[a]["step"], ops[a]["visit"] + d)), which.get((ops[b]["step"], ops[b]["visit"] + d))
-                if d and x and y and new.index(x) < new.index(y) < new.index(x) + 60:
-                    new = moved(new, x, y, early) or new
+                x, y = twins[a][VISITS + ops[a]["visit"] + d], twins[b][VISITS + ops[b]["visit"] + d]
+                if d and x and y and place[x] < place[y] < place[x] + 60:
+                    move(new, place[x], place[y], early)
+        room = 0.8 * (1 - turn / OPT["swaps"]) * (draw(1000) / 1000) ** 2
         done = play(new, costs[0])
+        if max(done) > first + len(costs) * room + 0.5:
+            continue
         span = (max(done) + sum(max(play(new, c)) for c in costs[1:])) / len(costs)
-        if span <= now + OPT["heat2"] * (1 - turn / OPT["swaps"]) * (draw(1000) / 1000) ** 2:
-            now, order = span, sorted(new, key=lambda i: done[i] - lat[i] - dur[i])
-            pairs = held(order)
+        if span <= now + room:
+            now, first, order = span, max(done), sorted(new, key=lambda i: done[i] - lat[i] - dur[i])
+            pairs, place = held(order), {i: p for p, i in enumerate(order)}
             if span < best[0]:
                 best = (span, order)
-    LOG.append((ops, way, succ, best[0]))
     return best[1]
 
 
@@ -261,7 +235,7 @@ def rank_program(g, core, T, topo):
         for q in range(len(cores)):
             rl = relays(topo, cores, q)
             if core in rl:
-                kinds = [k for k, h in zip("zr", rl) if h == core]
+                kinds = [k for k, h in zip(KINDS, rl) if h == core]
                 relay_program(g, core, T, topo, cores[(q + 1) % len(cores)], cores[q], kinds)
         return
 
@@ -281,6 +255,8 @@ def rank_program(g, core, T, topo):
 
     def ap(t, rows=128):
         buf = T[t[0]]
+        if len(t) > 4:
+            return buf[t[4]:t[4] + t[5], t[1]:t[2]:t[3]]
         if rows < 128:
             return buf[0:rows, t[1]:t[2]]
         return buf[:, t[1]:t[2]] if t[3] == 1 else buf[:, t[1]:t[2]:t[3]]
@@ -293,7 +269,7 @@ def rank_program(g, core, T, topo):
 
     stage = ["c", 0]
 
-    def op(eng, fns, reads, writes, dur, done=None, lat=0.0, extra=(), cont=False, gather=0, scatter=0):
+    def op(eng, fns, reads, writes, dur, done=None, lat=0.0, extra=(), gather=0, scatter=0):
         me = len(ops)
         deps, soft = set(extra), set()
         for regs, wr in ((reads, False), (writes, True)):
@@ -304,14 +280,14 @@ def rank_program(g, core, T, topo):
                 keep = []
                 for (a, b, o, w_) in acc.get(name, []):
                     if o != me and a < hi and lo < b and (wr or w_ or bank):
-                        (soft if bank and ops[o]["eng"] == eng else deps).add(o)
+                        (soft if bank and ops[o]["eng"] == eng and (eng == "t" or not (wr or ops[o]["fills"])) else deps).add(o)
                     if o == me or not ((wr or bank) and lo <= a and b <= hi):
                         keep.append((a, b, o, w_))
                 keep.append((lo, hi, me, wr or bank))
                 acc[name] = keep
         place = 0 if not ops or ops[-1]["step"][0] != stage[0] else ops[-1]["step"][1] + 1
-        ops.append(dict(eng=eng, step=(stage[0], place), visit=stage[1], fns=fns, deps=deps, after=deps | soft, dur=dur, done=done, lat=lat,
-                        gather=gather, scatter=scatter))
+        ops.append(dict(eng=eng, step=(stage[0], place), visit=stage[1], fills=any(x[0][:2] == "ps" for x in writes), fns=fns,
+                        deps=deps, after=deps | soft, dur=dur, done=done, lat=lat, gather=gather, scatter=scatter))
         return me
 
     def vd(cyc):
@@ -340,9 +316,10 @@ def rank_program(g, core, T, topo):
     def fill(out, v):
         return op("v", [lambda: g.vector.memset(ap(out), v)], [], [out], vd(cnt(out) * size(out) / 4))
 
-    def scan(out, d0, d1, first, o0=OP.min, o1=OP.max):
-        return op("v", [lambda: g.vector.tensor_tensor_scan(ap(out), ap(d0), ap(d1), first, o0, o1)],
-                  [d0, d1], [out], vd(fast(out, d0, d1) * cnt(out)))
+    def scan(out, d0, d1, first, o0=OP.min, o1=OP.max, back=False):
+        def call():
+            return g.vector.tensor_tensor_scan(ap(out), T[d0[0]][:, d0[2] - 1::-1] if back else ap(d0), ap(d1), first, o0, o1)
+        return op("v", [call], [d0, d1], [out], vd(fast(out, d0, d1) * cnt(out)))
 
     def act(out, a, f, scale=1.0, bias=0.0, accum=None, rows=128):
         def call():
@@ -370,6 +347,11 @@ def rank_program(g, core, T, topo):
             return op("v", [lambda: g.vector.tensor_copy(ap(out), win(a, off))], [a, off], [out], 0.05, gather=n)
         return op("s", [lambda: g.scalar.activation(ap(out), win(a, off), AF.Copy)], [a, off], [out], 0.065, gather=n)
 
+    def lanes(eng, out, a, off, lo, hi, piece):
+        for j in range(lo, hi, piece):
+            e = min(hi, j + piece)
+            gat(eng, sub(out, 16 * j, 16 * e), a, sub(off, j, e))
+
     def gtt(out, a, off, b, o):
         return op("v", [lambda: g.vector.tensor_tensor(ap(out), win(a, off), ap(b), o)], [a, off, b], [out],
                   0.05, gather=cnt(out))
@@ -377,34 +359,31 @@ def rank_program(g, core, T, topo):
     def scat(a, off, src):
         return op("v", [lambda: g.vector.tensor_copy(win(a, off), ap(src))], [src, off], [a], 0.05, scatter=cnt(src))
 
-    def mm(calls, start=True, stop=True, rows=128, out_rows=128, cont=False):
-        pe([(o_, l, r, start and j == 0, stop and j == len(calls) - 1) for j, (o_, l, r) in enumerate(calls)], rows, out_rows)
-
-    def sums(groups, rows=128, out_rows=128):
-        pe([(r[0] if len(r) == 2 else out, l, r[1] if len(r) == 2 else r, j == 0, j == len(pairs) - 1)
-            for out, pairs in groups for j, (l, r) in enumerate(pairs)], rows, out_rows)
-
     def pe(calls, rows, out_rows):
         fns, rd, wr, cyc = [], [], [], 0
         for j, (o_, l, r, a, z) in enumerate(calls):
             fns.append(lambda o_=o_, l=l, r=r, a=a, z=z: g.tensor.matmul(ap(o_, out_rows), ap(l, rows), ap(r, rows), a, z))
             rd += [l, r]
-            wr.append(o_)
+            wr.append(o_[:4])
             cyc += max(min(64, cnt(l)), cnt(r)) * (4 if size(l) == 4 else 1)
-            if cyc >= OPT["pc"] or j == len(calls) - 1:
+            if cyc >= 500 or j == len(calls) - 1:
                 op("t", fns, list(dict.fromkeys(rd)), list(dict.fromkeys(wr)), cyc * 0.00042, lat=0.05)
                 fns, rd, wr, cyc = [], [], [], 0
 
-    def gps(fn, rd, wr, dur):
-        return op("g", [fn], rd, wr, dur)
+    def mm(calls, start=True, stop=True):
+        pe([(o_, l, r, start and j == 0, stop and j == len(calls) - 1) for j, (o_, l, r) in enumerate(calls)], 128, 128)
+
+    def sums(groups, rows=128, out_rows=128):
+        pe([(r[0] if len(r) == 2 else out, l, r[1] if len(r) == 2 else r, j == 0, j == len(pairs) - 1)
+            for out, pairs in groups for j, (l, r) in enumerate(pairs)], rows, out_rows)
 
     n_dma = [0]
 
-    def dma(out_ap, in_ap, rd, wr, eng="y", dur=2.5):
+    def dma(out_ap, in_ap, rd, wr, eng="y", dur=1.9):
         sem = "dma%d" % n_dma[0]
         n_dma[0] += 1
         q = g.sync if eng == "y" else g.scalar
-        return op(eng, [lambda: q.dma_start(out_ap, in_ap)], rd, wr, 0.06, done=(sem, 16), lat=0.75 * dur)
+        return op(eng, [lambda: q.dma_start(out_ap, in_ap)], rd, wr, 0.06, done=(sem, 16), lat=dur)
 
     def ps(bank, a, b, s=1):
         return ("ps%d" % bank, a, b, s)
@@ -414,33 +393,31 @@ def rank_program(g, core, T, topo):
     dma(T.zed0[:], T.zed[:], [], [zed0])
     dma(T.wt0[:], T.wt[:], [], [whole("wt0", 1)], "s")
     dma(T.kap0[:], T.kap[:], [], [whole("kap0", 1)], "s")
-    dma(T.xs[:, 0:W], T.stock[:], [], [sub(xs, 0, W)], dur=4.0)
+    dma(T.xs[:, 0:W], T.stock[:], [], [sub(xs, 0, W)], dur=3.0)
     dma(T.xs[:, W:W + EXT], T.stock[:, 0:EXT], [], [sub(xs, W, W + EXT)])
     dma(T.rend0[:], T.rend[:], [], [rend0])
-    dma(ap(dn), T.donor[:], [], [dn], dur=3.0)
+    dma(ap(dn), T.donor[:], [], [dn], dur=2.3)
     dma(T.cnt0[:], T.cnt[:], [], [whole("cnt0", LANES)])
     dma(T.lim0[:], T.lim[:], [], [whole("lim0", 2)])
     dma(T.lend0[:], T.lend[:], [], [lend0])
 
     w, H16 = HALF, 16 * HALF
-    ones144 = alloc("pb", 144)
-    fill(ones144, 1.0)
-    ones = sub(ones144, 0, 128)
-    bo1, BO, ID = [alloc("pb", 128) for _ in range(3)]
+    ones, bo1, BO, ID = [alloc("pb", 128) for _ in range(4)]
+    fill(ones, 1.0)
 
     def sel(out, a, pattern, cmp_, base, cm, rows=128):
-        gps(lambda: g.affine_select(ap(out, rows), ap(a, rows), pattern, cmp_, 0.0, base, cm), [a], [out], 0.17 + 2 * CY * cnt(out))
+        op("g", [lambda: g.affine_select(ap(out, rows), ap(a, rows), pattern, cmp_, 0.0, base, cm)], [a], [out],
+           0.17 + 2 * CY * cnt(out))
 
     def iota(out, pattern, base, cm):
         small = dict(allow_small_or_imprecise_dtypes=True) if out[0] != "pi" else {}
-        gps(lambda: g.iota(ap(out), pattern, base, cm, **small), [], [out], 0.13 + 2 * CY * cnt(out))
+        op("g", [lambda: g.iota(ap(out), pattern, base, cm, **small)], [], [out], 0.13 + 2 * CY * cnt(out))
     sel(bo1, ones, [[-16, 8], [0, 16]], OP.is_ge, 0, 1)
     sel(BO, bo1, [[16, 8], [0, 16]], OP.is_ge, 15, -1)
     sel(ID, ones, [[-1, 128]], OP.is_equal, 0, 1)
-    pidx, q16 = alloc("pi", 1), alloc("pi", 16)
+    pidx, q16, mq = alloc("pi", 1), alloc("pi", 16), alloc("pf", 16)
     iota(pidx, [[0, 1]], 0, 1)
     iota(q16, [[16, 16]], 0, 0)
-    mq = alloc("pf", 16)
     iota(mq, [[1, 16]], 0, 0)
     G8 = sub(BO, 0, 128, 16)
 
@@ -468,64 +445,56 @@ def rank_program(g, core, T, topo):
         cp(sub(z, 15, 143, 16), c8)
         return lambda r: sub(z, 15 - r, 143 - r)
 
-    wtf, kapf, kc, k29, k256, sqb, cA, not15, one_k = [col() for _ in range(9)]
+    wtf, kapf, kc, k29, k256, sqb, k8, cA, cA2, not15, one_k, hi8, row1, AL0 = [col() for _ in range(14)]
     ts(wtf, whole("wt0", 1), 0.5, OP.mult)
     WB = times(BO, wtf, eng="v")
     EW = shifted(sub(WB, 0, 128, 16))
     CM = alloc("pb", 128)
     ts(CM, ID, 0.5, OP.mult, -16.0, OP.add)
-    CP = times(ID, 32.0)
-    nID = times(ID, -1.0)
+    CP, nID, hID = times(ID, 32.0), times(ID, -1.0), times(ID, -0.5)
     cp(kapf, whole("kap0", 1))
     ts(sqb, kapf, 16.0, OP.mult, -32.0, OP.add)
-    k8 = col()
     ts(k8, kapf, -8.0, OP.mult)
     ts(cA, kapf, k8, OP.mult, -0.375, OP.add)
+    ts(cA2, cA, 2048.0, OP.add)
+    fill(AL0, -0.375)
     zz = {}
     for b in range(2):
         zz[b] = alloc("pb", w)
         act(zz[b], sub(zed0, b * w, (b + 1) * w), AF.Copy, scale=2.0)
-    hID = times(ID, -0.5)
     kci = alloc("pi", 1)
     ts(kci, pidx, 15, OP.bitwise_and)
     cp(kc, kci)
     ts(k29, kci, 29.0, OP.mult)
     ts(k256, kci, 256.0, OP.mult)
-    E = shifted(G8)
     En = shifted(times(G8, -0.0625))
     KD1, KD2 = times(ID, kapf), times(ID, k256)
-    g8n, g8z = times(G8, -4096.0), times(G8, 2048.0)
-    RSK, QM, ZS, REP = alloc("pb", 128), alloc("pb", 64), alloc("pb", 240), alloc("pu", 4)
+    RSK, QM, ZS, CODE = alloc("pb", 128), alloc("pb", 64), alloc("pb", 240), alloc("pb", 256)
+    REP, REB, r4i = alloc("pu", 4), alloc("pu", 4), alloc("pi", 4)
     fill(RSK, -1.0)
     fill(sub(RSK, 0, 128, 16), 2.0 ** 25)
     sel(QM, sub(ones, 0, 64), [[0, 8], [-16, 8]], OP.is_ge, 0, 1)
     sel(QM, QM, [[0, 8], [16, 8]], OP.is_ge, 15, -1)
     fill(ZS, 0.0)
     ts(sub(ZS, 112, 128), mq, kc, OP.is_equal)
-    hi8, r4i = col(), alloc("pi", 4)
     ts(hi8, kc, 7.5, OP.is_gt)
     iota(r4i, [[2, 4]], 0, 0)
     ts(REP, r4i, hi8, OP.add)
-    RSE, REE = alloc("pb", 128), alloc("pu", 4)
-    fill(RSE, 1.0)
-    fill(sub(RSE, 0, 128, 16), 0.0)
-    ts(REE, REP, 16.0, OP.mult, 15.0, OP.add)
+    ts(REB, REP, -32.0, OP.mult, 255.0, OP.add)
+    iota(CODE, [[0, 8], [-1, 16], [0, 2]], 15, 0)
 
     def SG(j):
         return sub(ZS, 112 - 16 * j, 240 - 16 * j)
     il = alloc("pi", 16)
-    l16, l8c, l4c = alloc("pb", 16), alloc("pb", 16), alloc("pb", 16)
+    l16, l8c, l4c = alloc("pb", NQ), alloc("pb", 16), alloc("pb", 16)
     ts(il, q16, kc, OP.add)
-    ts(l16, il, 16.0, OP.mult)
+    ts(l16, sub(il, 0, NQ), 16.0, OP.mult)
     for b in range(2):
         ts(sub(l4c, b * NQ, (b + 1) * NQ), sub(il, 0, NQ), 4.0, OP.mult, (1 - b) * ND / 2, OP.add)
         ts(sub(l8c, b * NQ, (b + 1) * NQ), sub(il, 0, NQ), 8.0, OP.mult)
-    g8 = alloc("pb", 8)
-    cp(g8, G8)
-    g8m2 = times(G8, -2.0)
+    g8, g16, g32n = times(G8, 1.0), times(G8, 16.0), times(G8, -32.0)
     ts(not15, kc, 14.5, OP.is_lt)
     ts(one_k, kc, -1.0, OP.mult, 1.0, OP.add)
-    row1 = col()
     ts(row1, kc, 1.0, OP.is_equal, 2.0, OP.mult)
     g1 = times(G8, row1)
     E1 = [shifted(times(g1, -1.0)), shifted(g1)]
@@ -535,7 +504,12 @@ def rank_program(g, core, T, topo):
 
     def ET(r):
         return sub(ETA, 128 * r, 128 * r + 128)
-    S0 = ET(0)
+    ALT, REN, QD = alloc("pb", 256), alloc("pu", 4), [times(QM, ND / 2), times(QM, -ND / 2)]
+    fill(ALT, -1.0)
+    fill(sub(ALT, 0, 256, 32), 0.0)
+    ts(REN, REP, 32.0, OP.mult, 29.0, OP.add)
+    S0 = alloc("pb", 128)
+    sel(S0, ones, [[-16, 8], [0, 16]], OP.is_equal, 0, 1)
     nB, p2B, PB, nS0 = times(ID, -B), times(ID, 2 * B), times(BO, B), times(S0, -B)
     pBm = times(BO, not15, B, eng="v")
     nBm = times(pBm, -1.0)
@@ -543,10 +517,9 @@ def rank_program(g, core, T, topo):
     MN2 = plus(nB, nBm)
     Mp3 = times(plus(PB, nB), -1.0)
     ML = plus(BO, nS0)
-    nS1 = times(S0, -1.0)
     SEL, RST = alloc("pb", 256), alloc("pb", 256)
     for j in range(2):
-        act(sub(SEL, j, 256, 2), ID, AF.Copy, scale=8192.0)
+        act(sub(SEL, j, 256, 2), ID, AF.Copy, scale=131072.0)
     fill(RST, 0.0)
     fill(sub(RST, 0, 256, 32), 1.0)
     o1 = alloc("pf", 128)
@@ -558,19 +531,16 @@ def rank_program(g, core, T, topo):
     cp(limb, limi, rows=8)
     sel(b8, ones, [[1, 8], [0, 16]], OP.is_equal, 0, -1, rows=8)
     sums([(ps(7, 0, LANES), [(b8, cntb)]), (ps(7, LANES, LANES + 4), [(b8, limb)])], rows=8)
-    lim4 = alloc("pf", 4)
-    act(lim4, ps(7, LANES, LANES + 4), AF.Copy)
+    lim4, sbl, sbl2 = alloc("pf", 4), col(), col()
+    act(lim4, ps(7, LANES, LANES + 4), AF.Copy, scale=16.0)
     ts(nB0, ps(7, 0, LANES), kc, OP.is_gt)
-    sbl, sbl2 = col(), col()
-    ts(sbl, sub(lim4, 3, 4), 2.0, OP.add, not15, OP.mult)
-    ts(sbl2, sbl, -1.0, OP.add)
+    ts(sbl, sub(lim4, 3, 4), 32.0, OP.add, not15, OP.mult)
+    ts(sbl2, sbl, -16.0, OP.add)
     CD = [alloc("pb", 256) for _ in range(2)]
     ts(sub(CD[0], 0, 256, 2), ID, sub(lim4, 0, 1), OP.mult, -1.0, OP.mult)
     ts(sub(CD[0], 1, 256, 2), ID, sub(lim4, 1, 2), OP.mult, not15, OP.mult)
     ts(sub(CD[1], 0, 256, 2), ID, sub(lim4, 2, 3), OP.mult, -1.0, OP.mult)
     ts(sub(CD[1], 1, 256, 2), ID, sbl2, OP.mult)
-    cA2 = col()
-    ts(cA2, cA, 2048.0, OP.add)
 
     Gb, ADb, Yb, Hb, AH, MX = [[alloc("pb", H16) for _ in range(2)] for _ in range(6)]
     par = {}
@@ -583,7 +553,8 @@ def rank_program(g, core, T, topo):
     accs = [alloc("pf", 2) for _ in range(2)]
     state = {b: dict(z2=zz[b], R=sub(rend0, b * w, (b + 1) * w), L=sub(lend0, b * w, (b + 1) * w),
                      N=[sub(nB0, b * w, (b + 1) * w)]) for b in range(2)}
-    UW = w + NQ
+    UU = alloc("pf", 4 * NQ)
+    fill(UU, 0.0)
 
     def banks(b):
         return 2 + 3 * b, 3 + 3 * b, 4 + 3 * b
@@ -598,19 +569,13 @@ def rank_program(g, core, T, topo):
         ts(r4, U, M4096, OP.add, M4096, OP.subtract)
         sums([(U, [(CP, ones), (WB, z2), (nID, r4)])])
         sq, sql, up, zm = til("pf", w, "sq", t, b), til("pf", NQ, "sql", t, b), til("pf", w, "up", t, b), til("pf", w, "zm", t, b)
-        ul = sub(til("pi", 2 * NQ, "ul", t, 0), b * NQ, (b + 1) * NQ)
         act(sq, U, AF.Square, bias=sqb)
         act(up, U, AF.Copy)
         sums([(UL, [(EW(r), sub(z2, r, w, 16)) for r in range(16)] + [(En(r), sub(r4, r, w, 16)) for r in range(16)])])
         act(sql, UL, AF.Square)
-        cp(ul, UL)
+        act(sub(UU, 2 * NQ * b + 1, 2 * NQ * (b + 1), 2), UL, AF.Copy)
         act(zm, z2, AF.Copy, scale=0.5, bias=-0.5)
-        s.update(sq=sq, sql=sql, up=up, ul=ul, zm=zm)
-
-    def lanes(eng, out, a, off, lo, hi, piece):
-        for j in range(lo, hi, piece):
-            e = min(hi, j + piece)
-            gat(eng, sub(out, 16 * j, 16 * e), a, sub(off, j, e))
+        s.update(sq=sq, sql=sql, up=up, zm=zm)
 
     def front(t, b, A, AL):
         s = state[b]
@@ -618,67 +583,57 @@ def rank_program(g, core, T, topo):
 
         def ti(key, n=w):
             return til("pi", n, key, t, b)
-        ci, c, cil = ti("ci"), ti("c"), til("pf", NQ, "cil", t, b)
-        cl = til("pu", w, "cl", t, b)
+        ci, c, cl = ti("ci"), ti("c"), til("pu", w, "cl", t, b)
         ts(ci, s["sq"], 0.03125, OP.mult, A, OP.add)
         ts(c, ci, 2047, OP.bitwise_and)
         cp(cl, c)
-        gs = OPT["gs"][b]
-        lanes("v", Gb[b], sub(xs, 0, W), cl, gs, w, OPT["gp"][b])
-        lanes("s", Gb[b], sub(xs, 0, W), cl, 0, gs, w)
-        act(cil, s["sql"], AF.Identity, scale=0.03125, bias=AL)
+        lanes("v", Gb[b], sub(xs, 0, W), cl, OPT["gs"][b], w, OPT["gp"][b])
+        lanes("s", Gb[b], sub(xs, 0, W), cl, 0, OPT["gs"][b], w)
         pp, p2 = ti("pp", 2 * w), ti("p2", 2 * w)
         ll = til("pu", 2 * w, "ll", t, b)
-        raw = [r for r in OPT["runs"][b] if r[2][:3] == "raw"] or not OPT["joint"][b]
+
+        def hashes(lo):
+            ts(sub(p2, lo, lo + w), sub(pp, lo, lo + w), 5, OP.arith_shift_right, 2047, OP.bitwise_and)
+            ts(sub(ll, lo, lo + w), sub(p2, lo, lo + w), k29, OP.add)
         tt(sub(pp, w, 2 * w), s["R"], ps(P, 0, w), OP.mult)
-        if raw:
-            ts(sub(p2, w, 2 * w), sub(pp, w, 2 * w), 5, OP.arith_shift_right, 2047, OP.bitwise_and)
-            ts(sub(ll, w, 2 * w), sub(p2, w, 2 * w), k29, OP.add)
-            lo = 0
-            for n, _y, how in OPT["runs"][b]:
-                if how[:3] == "raw":
-                    lanes(how[3:] or "s", Hb[b], xs, sub(ll, w, 2 * w), lo, lo + n, OPT["hp"] if how[3:] else w)
-                lo += n
-        on_v = OPT["va"][b]
-        mm([(ps(Q, 0, w), ones, KD1), (ps(Q, 0, w), ones, KD2)]
-           + [(ps(Q, m, w, 16), x, y) for mc in on_v for m in range(4 * mc, 4 * mc + 4)
-              for x, y in ((sub(Gb[b], m, H16, 16), g8n), (s["z2"], g8z))], stop=False)
+        hashes(w)
+        lo = 0
+        for n, _y, how in OPT["runs"][b]:
+            if how == "raw":
+                lanes("s", Hb[b], xs, sub(ll, w, 2 * w), lo, lo + n, w)
+            lo += n
+        mm([(ps(Q, 0, w), ones, KD1), (ps(Q, 0, w), ones, KD2)], stop=False)
         for mc in range(4):
-            D = (0, 1, Rb, 0)[mc] if OPT["three"] else mc % 2
+            D = (0, 1, Rb, 0)[mc]
             sums([(ps(D, j * w, (j + 1) * w), [(ID, sub(Gb[b], 4 * mc + j, H16, 16)), (hID, s["z2"])]) for j in range(4)])
             ad = sub(ADb[b], mc * 4 * w, (mc + 1) * 4 * w)
-            if mc in on_v:
-                ts(ad, ps(D, 0, 512), 0.0, OP.max, 8192.0, OP.mult)
-            else:
-                act(ad, ps(D, 0, 512), AF.Abs, scale=4096.0)
-            mm([(ps(Q, 4 * mc + j, w, 16), sub(ad, j * w, (j + 1) * w), g8) for j in range(4)], start=False, stop=mc == 3, cont=True)
-        run, rep = til("pf", w, "run", t, b), til("pb", 8 * NQ, "rep", t, b)
-        vi, ka, pa, pc, cd, cx = [ti(k, NQ) for k in ("vi", "ka", "pa", "pc", "cd", "cx")]
+            act(ad, ps(D, 0, 512), AF.Abs, scale=4096.0)
+            mm([(ps(Q, 4 * mc + j, w, 16), sub(ad, j * w, (j + 1) * w), g8) for j in range(4)], start=False, stop=mc == 3)
+        run, rep, pq = ti("run"), til("pb", 8 * NQ, "rep", t, b), ti("pq", 2 * NQ)
+        ka, cd, cx = [ti(k, NQ) for k in ("ka", "cd", "cx")]
         cdu, cxu = til("pu", NQ, "cdu", t, b), til("pu", NQ, "cxu", t, b)
         scan(run, RSK, ps(Q, 0, w), 0.0, OP.max, OP.min)
-        cp(vi, sub(run, 15, w, 16))
-        ts(ka, vi, 255, OP.bitwise_and)
+        ts(ka, sub(run, 15, w, 16), 255, OP.bitwise_and)
         gtt(rep, ka, REP, QM, OP.mult)
-        sums([(ps(Rb, 0, NQ), [(SG(j), sub(rep, NQ * j, NQ * j + NQ)) for j in range(8)])])
-        tt(pa, ps(Rb, 0, NQ), s["ul"], OP.mult)
-        tt(pc, pa, cil, OP.add)
+        act(ps(Rb, 1, 2 * NQ, 2), s["sql"], AF.Identity, scale=0.03125, bias=AL)
+        sums([(ps(Rb, 0, 2 * NQ, 2), [(SG(j), sub(rep, NQ * j, NQ * j + NQ)) for j in range(8)])])
+        scan(pq, sub(UU, 2 * NQ * b, 2 * NQ * (b + 1)), ps(Rb, 0, 2 * NQ), 0.0, OP.mult, OP.add)
+        pc = sub(pq, 1, 2 * NQ, 2)
         ts(cd, pc, 1023, OP.bitwise_and)
         cp(cdu, cd)
         gtt(sub(pp, 0, w), dn, cdu, s["up"], OP.mult)
-        n = w if raw else 2 * w
-        ts(sub(p2, 0, n), sub(pp, 0, n), 5, OP.arith_shift_right, 2047, OP.bitwise_and)
-        ts(sub(ll, 0, n), sub(p2, 0, n), k29, OP.add)
+        hashes(0)
         ts(cx, pc, 2047, OP.bitwise_and)
         cp(cxu, cx)
         Dk, xc = til("pb", w, "Dk", t, b), til("pb", w, "xc", t, b)
-        gat("s", Dk, dn, cdu)
-        gat("s", xc, sub(xs, 0, W), cxu)
+        gat(OPT["picks"][b][0], Dk, dn, cdu)
+        gat(OPT["picks"][b][1], xc, sub(xs, 0, W), cxu)
         s.update(ll=ll, Dk=Dk, xc=xc)
 
     def own(t):
-        ul = til("pi", 2 * NQ, "ul", t, 0)
-        xi, xb = til("pi", 4 * NQ, "xi", t, 0), til("pb", 2 * NQ, "xb", t, 0)
+        ul, xi, xb = til("pi", 2 * NQ, "ul", t, 0), til("pi", 4 * NQ, "xi", t, 0), til("pb", 2 * NQ, "xb", t, 0)
         l8, l8u = til("pi", 2 * NQ, "l8", t, 0), til("pu", 2 * NQ, "l8u", t, 0)
+        cp(ul, sub(UU, 1, 4 * NQ, 2))
         ts(sub(xi, 0, 2 * NQ), ul, 7, OP.bitwise_and)
         ts(sub(xi, 2 * NQ, 4 * NQ), ul, 3, OP.bitwise_and)
         cp(xb, sub(xi, 2 * NQ, 4 * NQ))
@@ -691,27 +646,25 @@ def rank_program(g, core, T, topo):
         s = state[b]
         P, Q, Rb = banks(b)
         y, H, mx, ah, ll = Yb[b], Hb[b], MX[b], AH[b], s["ll"]
-        lo, mins = 0, False
+        lo, plain = 0, []
         for n, who, how in OPT["runs"][b]:
             a, e = 16 * lo, 16 * (lo + n)
-            lanes(who, y, xs, ll, lo, lo + n, OPT["yp"] if who == "v" else w)
-            for j in range(a, e, 16 * OPT["sp"]):
-                k = min(e, j + 16 * OPT["sp"])
-                scan(sub(mx, j, k - 1), sub(y, j, k - 1), sub(y, j + 1, k), 1000.0)
-            if how[:3] == "raw":
+            lanes(who, y, xs, ll, lo, lo + n, 16 if who == "v" else w)
+            for j in range(a, e, 512):
+                scan(sub(mx, j, j + 511), sub(y, j, j + 511), sub(y, j + 1, j + 512), 1000.0)
+            if how == "raw":
                 for j in range(a, e, 512):
                     D = j // 512 % 2
                     sums([(ps(D, 0, 512), [(ID, sub(H, j, j + 512)), (nID, sub(y, j, j + 512))])])
                     act(sub(ah, j, j + 512), ps(D, 0, 512), AF.Abs)
             else:
-                for j in range(lo, lo + n, OPT["fp"]):
-                    k = min(lo + n, j + OPT["fp"])
-                    gtt(sub(H, 16 * j, 16 * k), xs, sub(ll, w + j, w + k), sub(y, 16 * j, 16 * k), OP.subtract)
-                if how == "va":
+                for j in range(lo, lo + n, 16):
+                    gtt(sub(H, 16 * j, 16 * j + 256), xs, sub(ll, w + j, w + j + 16), sub(y, 16 * j, 16 * j + 256), OP.subtract)
+                if how == "less":
                     act(sub(ah, a, e), sub(H, a, e), AF.Abs)
                 else:
-                    ts(sub(ah, a, e), sub(H, a, e), 0.0, OP.min)
-                    mins = True
+                    ts(sub(ah, a, e), sub(H, a, e), 0.0, OP.min, -2.0, OP.mult)
+                    plain.append((lo, n))
             lo += n
         V = ps(Q, 0, 256)
 
@@ -721,22 +674,21 @@ def rank_program(g, core, T, topo):
         def kth(a, k):
             return sub(a, k, H16, 16)
         mm([(V, ones, CD[0]), (V, ones, CD[1])] + [(V, n_, SEL) for n_ in s["N"]], stop=False)
-        mm([(vc(2 * k + 1), kth(y, k), g8) for k in range(1, 15)] + [(vc(2 * k - 1), kth(y, k), g8) for k in range(2, 16)],
-           start=False, stop=False, cont=True)
-        mm([(vc(2 * k + 1), kth(mx, k), g8m2) for k in range(1, 15)], start=False, stop=False, cont=True)
-        if mins:
-            mm([(vc(2 * k), kth(H, k), g8) for k in range(1, 16)], start=False, stop=False, cont=True)
-        mm([(vc(2 * k), kth(ah, k), g8m2 if mins else g8) for k in range(1, 16)], start=False, cont=True)
-        al = til("pb", 256, "al", t, b)
+        mm([(vc(2 * k + 1), kth(y, k), g16) for k in range(1, 15)] + [(vc(2 * k - 1), kth(y, k), g16) for k in range(2, 16)],
+           start=False, stop=False)
+        mm([(vc(2 * k + 1), kth(mx, k), g32n) for k in range(1, 15)], start=False, stop=False)
+        for lo, n in plain:
+            mm([(vc(2 * k) + (lo, n), sub(H, 16 * lo + k, 16 * (lo + n), 16), g16) for k in range(1, 16)], start=False, stop=False)
+        mm([(vc(2 * k), kth(ah, k), g16) for k in range(1, 16)], start=False)
+        al, back, rep = til("pb", 256, "al", t, b), til("pb", 256, "back", t, b), til("pb", 8 * NQ, "rep2", t, b)
+        scan(back, V, CODE, 0.0, back=True)
         scan(al, V, RST, 1.0)
         A1, Dl = til("pb", w, "A1", t, b), til("pb", w, "Dl", t, b)
         sums([(ps(Rb, 0, w), [(sub(al, 1, 256, 2), ID)]),
               (ps(Rb, w, 2 * w), [(sub(al, 1, 256, 2), ID), (sub(al, 0, 256, 2), nID)])])
         act(A1, ps(Rb, 0, w), AF.Copy)
-        ec, rep = til("pb", w, "ec", t, b), til("pb", 8 * NQ, "rep2", t, b)
-        scan(ec, RSE, sub(al, 1, 256, 2), 0.0, OP.mult, OP.add)
-        gtt(rep, ec, REE, QM, OP.mult)
-        sums([(ps(P, 0, NQ), [(ID, sub(l16, 0, NQ))] + [(SG(j), sub(rep, NQ * j, NQ * j + NQ)) for j in range(8)])])
+        gtt(rep, back, REB, QM, OP.mult)
+        sums([(ps(P, 0, NQ), [(ID, l16)] + [(SG(j), sub(rep, NQ * j, NQ * j + NQ)) for j in range(8)])])
         act(Dl, ps(Rb, w, 2 * w), AF.Copy, accum=sub(accs[t % 2], b, b + 1))
         yel = til("pu", NQ, "yel", t, b)
         cp(yel, ps(P, 0, NQ))
@@ -749,7 +701,7 @@ def rank_program(g, core, T, topo):
         sx, sx2 = til("pi", w, "sx", t, b), til("pi", w, "sx2", t, b)
         gtt(sx, y, yel, s["xc"], OP.add)
         ts(sx2, sx, 1, OP.arith_shift_right)
-        s.update(sx2=sx2, A1=A1, Dl=Dl)
+        s.update(sx2=sx2, A1=A1, Dl=Dl, al=al)
 
     def count(t):
         A = ps(0, 0, 1)
@@ -769,8 +721,8 @@ def rank_program(g, core, T, topo):
         P, Q, Rb = banks(b)
         L, R, N, A1, Dl = s["L"], s["R"], s["N"], s["A1"], s["Dl"]
         last = t == VISITS - 1
-        ro = whole("ro%d%d" % (t, b), 5 * w)
-        Rn, Ln, N1, N2, Nd = [sub(ro, j * w, (j + 1) * w) for j in range(5)]
+        ro = whole("ro%d%d" % (t, b), 4 * w)
+        Rn, Ln, N2 = [sub(ro, j * w, (j + 1) * w) for j in (0, 1, 3)]
         c3, r3 = til("pb", w, "c3", t, b), til("pb", 3 * w, "r3", t, b)
         sums([(ps(Q, 0, w), [(ID, s["Dk"]), (Mc1, A1), (nB, Dl)] + [(nB, n_) for n_ in N]),
               (ps(Q, w, 2 * w), [(ID, R), (nB, A1), (PB, Dl)]),
@@ -780,39 +732,41 @@ def rank_program(g, core, T, topo):
         tt(c3, ps(Rb, 0, w), L, OP.min)
         sums([(ps(Q, 0, w), [(ID, sub(r3, 0, w)), (ID, sub(r3, w, 2 * w))])])
         tt(Ln, ps(Q, 0, w), c3, OP.max)
-        first = [(pBm, Dl)] + [(ET(r), (ps(Rb, r, w, 16), s["u3"])) for r in range(16)]
+        first = [(pBm, Dl)] + [(ET(r), (ps(P, r, w, 16), s["u3"])) for r in range(16)]
+        dlu, own_ = til("pu", NQ, "dlu", t, b), [(ID, sub(l4c, b * NQ, (b + 1) * NQ)), (ID, s["u3"])]
         if last:
-            sums([(ps(Rb, 0, w), first), (ps(Rb, w, 2 * w), [(ML, A1), (nBm, Dl)]), (ps(Rb, 2 * w, 3 * w), [(nS1, A1), (nBm, Dl)])])
-            act(sub(ro, 2 * w, 5 * w), ps(Rb, 0, 3 * w), AF.Relu, bias=1.0)
+            nd, rep = til("pb", 256, "nd", t, b), til("pb", 8 * NQ, "rep3", t, b)
+            scan(nd, ALT, s["al"], 0.0, OP.mult, OP.add)
+            gtt(rep, nd, REN, QD[b], OP.mult)
+            sums([(ps(P, 0, NQ), own_ + [(SG(j), sub(rep, NQ * j, NQ * j + NQ)) for j in range(8)])])
+            cp(dlu, ps(P, 0, NQ))
+            sums([(ps(P, 0, w), first), (ps(P, w, 2 * w), [(ML, A1), (nBm, Dl)])])
+            act(sub(ro, 2 * w, 4 * w), ps(P, 0, 2 * w), AF.Relu, bias=1.0)
         else:
-            sums([(ps(Rb, 0, w), first), (ps(Rb, w, 2 * w), [(Mc1, A1), (MN2, Dl)])])
-            act(sub(ro, 2 * w, 4 * w), ps(Rb, 0, 2 * w), AF.Relu, bias=one_k)
-            Nd = N2
+            sums([(ps(P, 0, w), first), (ps(P, w, 2 * w), [(Mc1, A1), (MN2, Dl)])])
+            act(sub(ro, 2 * w, 4 * w), ps(P, 0, 2 * w), AF.Relu, bias=one_k)
         sums([(ps(Q, 0, w), [(ID, Ln), (pBm, Dl)])])
         tt(Rn, ps(Q, 0, w), sub(r3, 2 * w, 3 * w), OP.max)
         if not last:
-            send("r", t, b, sub(ro, 0, 4 * w))
-        sums([(ps(Rb, 0, NQ), [(ID, sub(l4c, b * NQ, (b + 1) * NQ)), (ID, s["u3"])]
-               + [(E1[b](r), sub(Nd, r, w, 16)) for r in range(16)])])
-        dlu = til("pu", NQ, "dlu", t, b)
-        cp(dlu, ps(Rb, 0, NQ))
+            send("r", t, b, Rn)
+            send("q", t, b, sub(ro, w, 4 * w))
+            sums([(ps(Rb, 0, NQ), own_ + [(E1[b](r), sub(N2, r, w, 16)) for r in range(16)])])
+            cp(dlu, ps(Rb, 0, NQ))
         scat(("dn", b * ND, (b + 1) * ND, 1), dlu, Ln)
 
-    snt = {"z": 0, "r": 0}
+    snt = {k: 0 for k in KINDS}
 
     def send(k, t, b, tile):
-        dst = relays(topo, cores, rank)["zr".index(k)]
+        dst = relays(topo, cores, rank)[KINDS.index(k)]
         rid, pid = topo.addr(dst, core)
         m = topo.mask(core, dst)
         snt[k] += len(topo.engines(core, dst))
         name = "%s%d%d" % (k, t, b)
         o = op("g", [lambda: g.remote_dma(T[k + "i" + name[1:]][:], ap(tile), T.sem["a" + name], T.sem[k + "sent"], pid, rid, m)],
                [tile], [], 0.4, done=(k + "sent", 0))
-        n = len(topo.engines(relays(topo, cores, (rank - 1) % len(cores))["zr".index(k)], core))
+        n = len(topo.engines(relays(topo, cores, (rank - 1) % len(cores))[KINDS.index(k)], core))
         op(None, [], [], [whole(k + "i" + name[1:], cnt(tile))], 0.0, done=("a" + name, n), lat=OPT[k + "lat"], extra=(o,))
 
-    AL0 = col()
-    fill(AL0, -0.375)
     A = (cA, AL0)
     for t in range(VISITS):
         stage[1] = t
@@ -836,11 +790,11 @@ def rank_program(g, core, T, topo):
         stage[0] = "end"
         for b in range(2):
             if t < VISITS - 1:
-                r = whole("ri%d%d" % (t, b), 4 * w)
-                state[b] = dict(z2=whole("zi%d%d" % (t, b), w), R=sub(r, 0, w), L=sub(r, w, 2 * w),
-                                N=[sub(r, 2 * w, 3 * w), sub(r, 3 * w, 4 * w)])
+                r = whole("qi%d%d" % (t, b), 3 * w)
+                state[b] = dict(z2=whole("zi%d%d" % (t, b), w), R=whole("ri%d%d" % (t, b), w), L=sub(r, 0, w),
+                                N=[sub(r, w, 2 * w), sub(r, 2 * w, 3 * w)])
             else:
-                zo, r = whole("zo%d%d" % (t, b), w), whole("ro%d%d" % (t, b), 5 * w)
+                zo, r = whole("zo%d%d" % (t, b), w), whole("ro%d%d" % (t, b), 4 * w)
                 lo, hi = b * w, (b + 1) * w
                 act(sub(whole("yz0", LANES), lo, hi), zo, AF.Copy, scale=0.5)
                 dma(T.yz[:, lo:hi], T.yz0[:, lo:hi], [("yz0", lo, hi, 1)], [])
@@ -851,19 +805,17 @@ def rank_program(g, core, T, topo):
     dma(T.yn[:], T.yn0[:], [("yn0", 0, LANES, 1)], [])
     for b in range(2):
         lo, hi = b * W // 2, (b + 1) * W // 2
-        dma(T.yx[:, lo:hi], T.xs[:, lo:hi], [sub(xs, lo, hi)], [], dur=4.0)
-        dma(T.yd[:, lo // 2:hi // 2], ap(sub(dn, lo // 2, hi // 2)), [sub(dn, lo // 2, hi // 2)], [], dur=3.0)
+        dma(T.yx[:, lo:hi], T.xs[:, lo:hi], [sub(xs, lo, hi)], [], dur=3.0)
+        dma(T.yd[:, lo // 2:hi // 2], ap(sub(dn, lo // 2, hi // 2)), [sub(dn, lo // 2, hi // 2)], [], dur=2.3)
 
     if not ORDER:
         ORDER.extend(schedule(ops))
-    order = ORDER
-
     QUEUE = {"v": g.vector, "s": g.scalar, "t": g.tensor, "g": g, "y": g.sync}
     SEM = {"v": "sv", "s": "ss", "t": "st", "g": "sg"}
     made = {k: 0 for k in SEM.values()}
     know = {e: {} for e in QUEUE}
     final = {}
-    for i in order:
+    for i in ORDER:
         o = ops[i]
         e = o["eng"]
         if e is None:
@@ -908,5 +860,5 @@ def rank_program(g, core, T, topo):
         g.wait_ge(T.sem[k], made[k])
     for k, v in final.items():
         g.wait_ge(T.sem[k], v)
-    for k in ("z", "r"):
+    for k in KINDS:
         g.wait_ge(T.sem[k + "sent"], snt[k])

from concourse.mybir import AluOpType, ActivationFunctionType

OP = AluOpType
AF = ActivationFunctionType
LANES, HALF, NQ, VISITS = 256, 128, 8, 5
W, EXT, ND = 2048, 448, 1024
M2, M4096 = 1.5 * 2 ** 24, 1.5 * 2 ** 35
B = 256.0
CY = 0.00083

OPT = dict(
    gs=(64, 0), gp=(128, 16), picks=("ss", "ss"),
    runs=(((64, "v", "raw"), (64, "s", "raw")), ((32, "s", "less"),) * 3 + ((32, "s", "raw"),)),
    models=((1.3, 2.4, 1.0, 0.95, 0.19), (1.45, 3.3, 1.08, 1.45, 0.21)), zlat=2.6, rlat=2.6, qlat=4.0,
    turns=2000, swaps=36000, seed=2,
)

SCRATCH = {
    "pi": ("sbuf", [128, 6144], "int32"), "pf": ("sbuf", [128, 4096], "float32"),
    "pb": ("sbuf", [128, 44000], "bfloat16"), "pu": ("sbuf", [128, 2048], "uint16"),
    "xs": ("sbuf", [128, W + EXT], "bfloat16"), "dn": ("sbuf", [128, 2 * ND], "bfloat16"),
    "zed0": ("sbuf", [128, LANES], "bfloat16"), "rend0": ("sbuf", [128, LANES], "bfloat16"),
    "lend0": ("sbuf", [128, LANES], "bfloat16"), "cnt0": ("sbuf", [8, LANES], "int32"),
    "kap0": ("sbuf", [128, 1], "int32"), "wt0": ("sbuf", [128, 1], "int32"), "lim0": ("sbuf", [8, 2], "int32"),
    "yn0": ("sbuf", [8, LANES], "float32"), "yz0": ("sbuf", [128, LANES], "bfloat16"),
}
KINDS = "zrq"
SEMAPHORES = ["sv", "ss", "st", "sg", "zsent", "rsent", "qsent"]
for _i in range(8):
    SCRATCH["ps%d" % _i] = ("psum", [128, 512], "float32")
for _i in range(28):
    SEMAPHORES.append("dma%d" % _i)
for _t in range(VISITS):
    for _b in range(2):
        SCRATCH["zo%d%d" % (_t, _b)] = ("sbuf", [128, HALF], "bfloat16")
        SCRATCH["ro%d%d" % (_t, _b)] = ("sbuf", [128, 4 * HALF], "bfloat16")
        if _t < VISITS - 1:
            for _k, _n in zip(KINDS, (1, 1, 3)):
                SCRATCH["%si%d%d" % (_k, _t, _b)] = ("sbuf", [128, _n * HALF], "bfloat16")
                SEMAPHORES.append("a%s%d%d" % (_k, _t, _b))


def relays(topo, cores, q):
    src, dst = cores[q], cores[(q + 1) % len(cores)]
    c = [h for h in topo.cores_of(src) if h not in cores and topo.may_write(src, h) and topo.may_write(h, dst)]
    c.sort(key=lambda h: topo.die(h) != topo.die(src))
    return [c[j % len(c)] for j in range(len(KINDS))]


def relay_program(g, core, T, topo, dst, src, kinds):
    n_in = len(topo.engines(src, core))
    n_out = len(topo.engines(core, dst))
    rid, pid = topo.addr(dst, core)
    sent = {k: 0 for k in KINDS}
    for t in range(VISITS - 1):
        for b in range(2):
            for k in kinds:
                g.wait_ge(T.sem["a%s%d%d" % (k, t, b)], n_in)
                buf = T["%si%d%d" % (k, t, b)]
                g.remote_dma(buf[:], buf[:], T.sem["a%s%d%d" % (k, t, b)], T.sem[k + "sent"], pid, rid, topo.mask(core, dst))
                sent[k] += n_out
    for k in kinds:
        g.wait_ge(T.sem[k + "sent"], sent[k])


ORDER = []


def schedule(ops):
    n = len(ops)
    queue = {"v": 0, "s": 1, "t": 2, "g": 3, "y": 4, None: 5}
    eng = [queue[o["eng"]] for o in ops]
    pred = [sorted(o["after"]) for o in ops]
    succ = [[] for _ in ops]
    for i in range(n):
        for d in pred[i]:
            succ[d].append(i)
    costs = [([(o["dur"] + CY * (gf * o["gather"] + sf * o["scatter"])) * f for o in ops],
              [o["lat"] * lf + hop for o in ops]) for gf, sf, f, lf, hop in OPT["models"]]
    dur, lat = costs[0]
    need = [sorted(o["deps"]) for o in ops]
    above = [0] * n
    for i in range(n):
        for j in need[i]:
            above[i] |= above[j] | 1 << j
        need[i] = [j for j in need[i] if not any(above[k] >> j & 1 for k in need[i])]
    way = [0.0] * n
    for i in range(n - 1, -1, -1):
        way[i] = dur[i] + max([way[j] + (lat[i] if i in ops[j]["deps"] else 0) for j in succ[i]] + [lat[i]])
    hard = [[(j, i in ops[j]["deps"]) for j in succ[i]] for i in range(n)]
    seed = [OPT["seed"]]

    def draw(k):
        seed[0] = (seed[0] * 1103515245 + 12345) % 2 ** 31
        return (seed[0] >> 8) % k

    def play(order, cost):
        d2, l2 = cost
        done, free = [0.0] * n, [0.0] * 6
        for i in order:
            e = eng[i]
            st = free[e]
            for j in need[i]:
                if done[j] > st:
                    st = done[j]
            st += d2[i]
            if e != 5:
                free[e] = st
            done[i] = st + l2[i]
        return done

    def plan(prio):
        left = [len(p) for p in pred]
        ready = [[] for _ in range(6)]
        avail, free, first, order, span = [0.0] * n, [0.0] * 6, [1e18] * 6, [], 0.0
        for i in range(n):
            if not left[i]:
                ready[eng[i]].append(i)
                first[eng[i]] = 0.0
        for _ in range(n):
            st = 1e17
            for k in range(6):
                x = first[k] if first[k] > free[k] else free[k]
                if x < st:
                    st, e = x, k
            top, lim = -1e18, st + 0.2
            for j in ready[e]:
                if avail[j] <= lim and prio[j] > top:
                    top, i = prio[j], j
            ready[e].remove(i)
            first[e] = min([avail[j] for j in ready[e]] + [1e18])
            end = (st if st > avail[i] else avail[i]) + dur[i]
            if e != 5:
                free[e] = end
            order.append(i)
            end += lat[i]
            if end > span:
                span = end
            for j, waits in hard[i]:
                if waits and end > avail[j]:
                    avail[j] = end
                left[j] -= 1
                if not left[j]:
                    ready[eng[j]].append(j)
                    if avail[j] < first[eng[j]]:
                        first[eng[j]] = avail[j]
        return (span + sum(max(play(order, c)) for c in costs[1:])) / len(costs), order

    def held(order):
        done, free, last, by = [0.0] * n, [0.0] * 6, [None] * 6, [None] * n
        for i in order:
            st, by[i] = free[eng[i]], (last[eng[i]], True)
            for j in need[i]:
                if done[j] >= st:
                    st, by[i] = done[j], (j, False)
            if eng[i] != 5:
                free[eng[i]], last[eng[i]] = st + dur[i], i
            done[i] = st + dur[i] + lat[i]
        i, pairs = done.index(max(done)), []
        while by[i][0] is not None:
            if by[i][1] and by[i][0] not in pred[i]:
                pairs.append((by[i][0], i))
            i = by[i][0]
        return pairs

    def move(order, p, q, early):
        mid = order[p:q + 1]
        mark = {mid[-1] if early else mid[0]}
        for i in (mid[::-1] if early else mid):
            if not mark.isdisjoint(succ[i] if early else pred[i]):
                mark.add(i)
        if (mid[0] if early else mid[-1]) in mark:
            return False
        one, two = [i for i in mid if i in mark], [i for i in mid if i not in mark]
        order[p:q + 1] = one + two if early else two + one
        return True

    steps = sorted(set(o["step"] for o in ops))
    off = {k: 0.0 for k in steps}
    now, order = best = plan(way)
    pairs = held(order)
    for turn in range(OPT["turns"]):
        new = dict(off)
        if pairs and draw(100) < 90:
            a, b = pairs[draw(len(pairs))]
            gap = abs(way[a] + off[ops[a]["step"]] - way[b] - off[ops[b]["step"]]) + (0.1, 0.5, 1, 2)[draw(4)]
            if draw(2):
                new[ops[a]["step"]] -= gap
            else:
                new[ops[b]["step"]] += gap
        else:
            for _ in range(1 + draw(2)):
                new[steps[draw(len(steps))]] += (-4, -2, -1, -0.5, 0.5, 1, 2, 4)[draw(8)]
        span, order = plan([way[i] + new[ops[i]["step"]] for i in range(n)])
        if span <= now + 2 * (1 - turn / OPT["turns"]) * (draw(1000) / 1000) ** 3:
            if span != now:
                pairs = held(order)
            now, off = span, new
            if span < best[0]:
                best = (span, order)

    which = {(o["step"], o["visit"]): i for i, o in enumerate(ops)}
    twins = [[which.get((o["step"], t)) for t in range(-VISITS, 2 * VISITS)] for o in ops]
    now, order = best
    first, pairs, place = max(play(order, costs[0])), held(order), {i: p for p, i in enumerate(order)}
    for turn in range(OPT["swaps"]):
        a, b = pairs[draw(len(pairs))]
        for _ in range(draw(4)):
            a = ([a] + [i for i in order[max(0, place[a] - 12):place[a]] if eng[i] == eng[a]])[-1]
        early, new = draw(2), list(order)
        if not move(new, place[a], place[b], early):
            continue
        if draw(100) < 70:
            for d in range(1 - VISITS, VISITS):
                x, y = twins[a][VISITS + ops[a]["visit"] + d], twins[b][VISITS + ops[b]["visit"] + d]
                if d and x and y and place[x] < place[y] < place[x] + 60:
                    move(new, place[x], place[y], early)
        room = 0.8 * (1 - turn / OPT["swaps"]) * (draw(1000) / 1000) ** 2
        done = play(new, costs[0])
        if max(done) > first + len(costs) * room + 0.5:
            continue
        span = (max(done) + sum(max(play(new, c)) for c in costs[1:])) / len(costs)
        if span <= now + room:
            now, first, order = span, max(done), sorted(new, key=lambda i: done[i] - lat[i] - dur[i])
            pairs, place = held(order), {i: p for p, i in enumerate(order)}
            if span < best[0]:
                best = (span, order)
    return best[1]


def rank_program(g, core, T, topo):
    rank = T.rank_of(core)
    cores = list(T.cores)
    if rank is None:
        for q in range(len(cores)):
            rl = relays(topo, cores, q)
            if core in rl:
                kinds = [k for k, h in zip(KINDS, rl) if h == core]
                relay_program(g, core, T, topo, cores[(q + 1) % len(cores)], cores[q], kinds)
        return

    ops, acc, used = [], {}, {"pi": 0, "pf": 0, "pb": 0, "pu": 0}
    SIZE = {"pi": 4, "pf": 4, "pb": 2, "pu": 2}

    def alloc(pool, n):
        lo = used[pool]
        used[pool] = lo + -(-n // 16) * 16
        return (pool, lo, lo + n, 1)

    def sub(t, a, b, s=1):
        return (t[0], t[1] + a, t[1] + b, s)

    def whole(name, n):
        return (name, 0, n, 1)

    def ap(t, rows=128):
        buf = T[t[0]]
        if len(t) > 4:
            return buf[t[4]:t[4] + t[5], t[1]:t[2]:t[3]]
        if rows < 128:
            return buf[0:rows, t[1]:t[2]]
        return buf[:, t[1]:t[2]] if t[3] == 1 else buf[:, t[1]:t[2]:t[3]]

    def cnt(t):
        return -(-(t[2] - t[1]) // t[3])

    def size(t):
        return 4 if t[0][:2] == "ps" else SIZE.get(t[0], 2)

    stage = ["c", 0]

    def op(eng, fns, reads, writes, dur, done=None, lat=0.0, extra=(), gather=0, scatter=0):
        me = len(ops)
        deps, soft = set(extra), set()
        for regs, wr in ((reads, False), (writes, True)):
            for name, lo, hi, _s in regs:
                bank = name[:2] == "ps"
                if bank:
                    lo, hi = 0, 512
                keep = []
                for (a, b, o, w_) in acc.get(name, []):
                    if o != me and a < hi and lo < b and (wr or w_ or bank):
                        (soft if bank and ops[o]["eng"] == eng and (eng == "t" or not (wr or ops[o]["fills"])) else deps).add(o)
                    if o == me or not ((wr or bank) and lo <= a and b <= hi):
                        keep.append((a, b, o, w_))
                keep.append((lo, hi, me, wr or bank))
                acc[name] = keep
        place = 0 if not ops or ops[-1]["step"][0] != stage[0] else ops[-1]["step"][1] + 1
        ops.append(dict(eng=eng, step=(stage[0], place), visit=stage[1], fills=any(x[0][:2] == "ps" for x in writes), fns=fns,
                        deps=deps, after=deps | soft, dur=dur, done=done, lat=lat, gather=gather, scatter=scatter))
        return me

    def vd(cyc):
        return 0.03 + CY * max(64, cyc)

    def fast(*tiles):
        return 0.5 if all(size(t) == 2 for t in tiles) else 1

    def tt(out, a, b, o):
        c = 1 if "ps" in (a[0][:2], b[0][:2]) else 2
        return op("v", [lambda: g.vector.tensor_tensor(ap(out), ap(a), ap(b), o)], [a, b], [out], vd(c * cnt(out)))

    def ts(out, a, s1, o1, s2=None, o2=None, rows=128):
        def val(s):
            return ap(s) if isinstance(s, tuple) else s

        def call():
            if o2 is None:
                return g.vector.tensor_scalar(ap(out, rows), ap(a, rows), val(s1), None, o1)
            return g.vector.tensor_scalar(ap(out, rows), ap(a, rows), val(s1), val(s2), o1, o2)
        return op("v", [call], [a] + [s for s in (s1, s2) if isinstance(s, tuple)], [out], vd(fast(out, a) * cnt(out)))

    def cp(out, a, rows=128):
        return op("v", [lambda: g.vector.tensor_copy(ap(out, rows), ap(a, rows))], [a], [out], vd(fast(out, a) * cnt(out)))

    def fill(out, v):
        return op("v", [lambda: g.vector.memset(ap(out), v)], [], [out], vd(cnt(out) * size(out) / 4))

    def scan(out, d0, d1, first, o0=OP.min, o1=OP.max, back=False):
        def call():
            return g.vector.tensor_tensor_scan(ap(out), T[d0[0]][:, d0[2] - 1::-1] if back else ap(d0), ap(d1), first, o0, o1)
        return op("v", [call], [d0, d1], [out], vd(fast(out, d0, d1) * cnt(out)))

    def act(out, a, f, scale=1.0, bias=0.0, accum=None, rows=128):
        def call():
            kw = {}
            if isinstance(scale, tuple):
                kw["scale"] = ap(scale)
            elif scale != 1.0:
                kw["scale"] = scale
            if isinstance(bias, tuple):
                kw["bias"] = ap(bias)
            elif bias != 0.0:
                kw["bias"] = bias
            if accum is not None:
                kw["accum_out"] = ap(accum)
            return g.scalar.activation(ap(out, rows), ap(a, rows), f, **kw)
        rd = [a] + [s for s in (bias, scale) if isinstance(s, tuple)]
        return op("s", [call], rd, [out] + ([accum] if accum else []), 0.04 + CY * cnt(out))

    def win(a, off):
        return T[a[0]][:, a[1]:a[2]].indirect(ap(off))

    def gat(eng, out, a, off):
        n = cnt(out)
        if eng == "v":
            return op("v", [lambda: g.vector.tensor_copy(ap(out), win(a, off))], [a, off], [out], 0.05, gather=n)
        return op("s", [lambda: g.scalar.activation(ap(out), win(a, off), AF.Copy)], [a, off], [out], 0.065, gather=n)

    def lanes(eng, out, a, off, lo, hi, piece):
        for j in range(lo, hi, piece):
            e = min(hi, j + piece)
            gat(eng, sub(out, 16 * j, 16 * e), a, sub(off, j, e))

    def gtt(out, a, off, b, o):
        return op("v", [lambda: g.vector.tensor_tensor(ap(out), win(a, off), ap(b), o)], [a, off, b], [out],
                  0.05, gather=cnt(out))

    def scat(a, off, src):
        return op("v", [lambda: g.vector.tensor_copy(win(a, off), ap(src))], [src, off], [a], 0.05, scatter=cnt(src))

    def pe(calls, rows, out_rows):
        fns, rd, wr, cyc = [], [], [], 0
        for j, (o_, l, r, a, z) in enumerate(calls):
            fns.append(lambda o_=o_, l=l, r=r, a=a, z=z: g.tensor.matmul(ap(o_, out_rows), ap(l, rows), ap(r, rows), a, z))
            rd += [l, r]
            wr.append(o_[:4])
            cyc += max(min(64, cnt(l)), cnt(r)) * (4 if size(l) == 4 else 1)
            if cyc >= 500 or j == len(calls) - 1:
                op("t", fns, list(dict.fromkeys(rd)), list(dict.fromkeys(wr)), cyc * 0.00042, lat=0.05)
                fns, rd, wr, cyc = [], [], [], 0

    def mm(calls, start=True, stop=True):
        pe([(o_, l, r, start and j == 0, stop and j == len(calls) - 1) for j, (o_, l, r) in enumerate(calls)], 128, 128)

    def sums(groups, rows=128, out_rows=128):
        pe([(r[0] if len(r) == 2 else out, l, r[1] if len(r) == 2 else r, j == 0, j == len(pairs) - 1)
            for out, pairs in groups for j, (l, r) in enumerate(pairs)], rows, out_rows)

    n_dma = [0]

    def dma(out_ap, in_ap, rd, wr, eng="y", dur=1.9):
        sem = "dma%d" % n_dma[0]
        n_dma[0] += 1
        q = g.sync if eng == "y" else g.scalar
        return op(eng, [lambda: q.dma_start(out_ap, in_ap)], rd, wr, 0.06, done=(sem, 16), lat=dur)

    def ps(bank, a, b, s=1):
        return ("ps%d" % bank, a, b, s)

    xs, dn = whole("xs", W + EXT), ("dn", ND // 2, 3 * ND // 2, 1)
    zed0, rend0, lend0 = whole("zed0", LANES), whole("rend0", LANES), whole("lend0", LANES)
    dma(T.zed0[:], T.zed[:], [], [zed0])
    dma(T.wt0[:], T.wt[:], [], [whole("wt0", 1)], "s")
    dma(T.kap0[:], T.kap[:], [], [whole("kap0", 1)], "s")
    dma(T.xs[:, 0:W], T.stock[:], [], [sub(xs, 0, W)], dur=3.0)
    dma(T.xs[:, W:W + EXT], T.stock[:, 0:EXT], [], [sub(xs, W, W + EXT)])
    dma(T.rend0[:], T.rend[:], [], [rend0])
    dma(ap(dn), T.donor[:], [], [dn], dur=2.3)
    dma(T.cnt0[:], T.cnt[:], [], [whole("cnt0", LANES)])
    dma(T.lim0[:], T.lim[:], [], [whole("lim0", 2)])
    dma(T.lend0[:], T.lend[:], [], [lend0])

    w, H16 = HALF, 16 * HALF
    ones, bo1, BO, ID = [alloc("pb", 128) for _ in range(4)]
    fill(ones, 1.0)

    def sel(out, a, pattern, cmp_, base, cm, rows=128):
        op("g", [lambda: g.affine_select(ap(out, rows), ap(a, rows), pattern, cmp_, 0.0, base, cm)], [a], [out],
           0.17 + 2 * CY * cnt(out))

    def iota(out, pattern, base, cm):
        small = dict(allow_small_or_imprecise_dtypes=True) if out[0] != "pi" else {}
        op("g", [lambda: g.iota(ap(out), pattern, base, cm, **small)], [], [out], 0.13 + 2 * CY * cnt(out))
    sel(bo1, ones, [[-16, 8], [0, 16]], OP.is_ge, 0, 1)
    sel(BO, bo1, [[16, 8], [0, 16]], OP.is_ge, 15, -1)
    sel(ID, ones, [[-1, 128]], OP.is_equal, 0, 1)
    pidx, q16, mq = alloc("pi", 1), alloc("pi", 16), alloc("pf", 16)
    iota(pidx, [[0, 1]], 0, 1)
    iota(q16, [[16, 16]], 0, 0)
    iota(mq, [[1, 16]], 0, 0)
    G8 = sub(BO, 0, 128, 16)

    def col():
        return alloc("pf", 1)

    def times(a, s, s2=None, eng="s"):
        out = alloc("pb", cnt(a))
        if eng == "s":
            act(out, a, AF.Copy, scale=s)
        elif s2 is None:
            ts(out, a, s, OP.mult)
        else:
            ts(out, a, s, OP.mult, s2, OP.mult)
        return out

    def plus(a, b, o=OP.add):
        out = alloc("pb", cnt(a))
        tt(out, a, b, o)
        return out

    def shifted(c8):
        z = alloc("pb", 144)
        fill(z, 0.0)
        cp(sub(z, 15, 143, 16), c8)
        return lambda r: sub(z, 15 - r, 143 - r)

    wtf, kapf, kc, k29, k256, sqb, k8, cA, cA2, not15, one_k, hi8, row1, AL0 = [col() for _ in range(14)]
    ts(wtf, whole("wt0", 1), 0.5, OP.mult)
    WB = times(BO, wtf, eng="v")
    EW = shifted(sub(WB, 0, 128, 16))
    CM = alloc("pb", 128)
    ts(CM, ID, 0.5, OP.mult, -16.0, OP.add)
    CP, nID, hID = times(ID, 32.0), times(ID, -1.0), times(ID, -0.5)
    cp(kapf, whole("kap0", 1))
    ts(sqb, kapf, 16.0, OP.mult, -32.0, OP.add)
    ts(k8, kapf, -8.0, OP.mult)
    ts(cA, kapf, k8, OP.mult, -0.375, OP.add)
    ts(cA2, cA, 2048.0, OP.add)
    fill(AL0, -0.375)
    zz = {}
    for b in range(2):
        zz[b] = alloc("pb", w)
        act(zz[b], sub(zed0, b * w, (b + 1) * w), AF.Copy, scale=2.0)
    kci = alloc("pi", 1)
    ts(kci, pidx, 15, OP.bitwise_and)
    cp(kc, kci)
    ts(k29, kci, 29.0, OP.mult)
    ts(k256, kci, 256.0, OP.mult)
    En = shifted(times(G8, -0.0625))
    KD1, KD2 = times(ID, kapf), times(ID, k256)
    RSK, QM, ZS, CODE = alloc("pb", 128), alloc("pb", 64), alloc("pb", 240), alloc("pb", 256)
    REP, REB, r4i = alloc("pu", 4), alloc("pu", 4), alloc("pi", 4)
    fill(RSK, -1.0)
    fill(sub(RSK, 0, 128, 16), 2.0 ** 25)
    sel(QM, sub(ones, 0, 64), [[0, 8], [-16, 8]], OP.is_ge, 0, 1)
    sel(QM, QM, [[0, 8], [16, 8]], OP.is_ge, 15, -1)
    fill(ZS, 0.0)
    ts(sub(ZS, 112, 128), mq, kc, OP.is_equal)
    ts(hi8, kc, 7.5, OP.is_gt)
    iota(r4i, [[2, 4]], 0, 0)
    ts(REP, r4i, hi8, OP.add)
    ts(REB, REP, -32.0, OP.mult, 255.0, OP.add)
    iota(CODE, [[0, 8], [-1, 16], [0, 2]], 15, 0)

    def SG(j):
        return sub(ZS, 112 - 16 * j, 240 - 16 * j)
    il = alloc("pi", 16)
    l16, l8c, l4c = alloc("pb", NQ), alloc("pb", 16), alloc("pb", 16)
    ts(il, q16, kc, OP.add)
    ts(l16, sub(il, 0, NQ), 16.0, OP.mult)
    for b in range(2):
        ts(sub(l4c, b * NQ, (b + 1) * NQ), sub(il, 0, NQ), 4.0, OP.mult, (1 - b) * ND / 2, OP.add)
        ts(sub(l8c, b * NQ, (b + 1) * NQ), sub(il, 0, NQ), 8.0, OP.mult)
    g8, g16, g32n = times(G8, 1.0), times(G8, 16.0), times(G8, -32.0)
    ts(not15, kc, 14.5, OP.is_lt)
    ts(one_k, kc, -1.0, OP.mult, 1.0, OP.add)
    ts(row1, kc, 1.0, OP.is_equal, 2.0, OP.mult)
    g1 = times(G8, row1)
    E1 = [shifted(times(g1, -1.0)), shifted(g1)]
    ETA = alloc("pb", 2048)
    iota(ETA, [[0, 2048]], 1, 0)
    sel(ETA, ETA, [[-1, 16], [-16, 8], [0, 16]], OP.is_equal, 0, 1)

    def ET(r):
        return sub(ETA, 128 * r, 128 * r + 128)
    ALT, REN, QD = alloc("pb", 256), alloc("pu", 4), [times(QM, ND / 2), times(QM, -ND / 2)]
    fill(ALT, -1.0)
    fill(sub(ALT, 0, 256, 32), 0.0)
    ts(REN, REP, 32.0, OP.mult, 29.0, OP.add)
    S0 = alloc("pb", 128)
    sel(S0, ones, [[-16, 8], [0, 16]], OP.is_equal, 0, 1)
    nB, p2B, PB, nS0 = times(ID, -B), times(ID, 2 * B), times(BO, B), times(S0, -B)
    pBm = times(BO, not15, B, eng="v")
    nBm = times(pBm, -1.0)
    Mc1 = plus(nS0, nB, OP.subtract)
    MN2 = plus(nB, nBm)
    Mp3 = times(plus(PB, nB), -1.0)
    ML = plus(BO, nS0)
    SEL, RST = alloc("pb", 256), alloc("pb", 256)
    for j in range(2):
        act(sub(SEL, j, 256, 2), ID, AF.Copy, scale=131072.0)
    fill(RST, 0.0)
    fill(sub(RST, 0, 256, 32), 1.0)
    o1 = alloc("pf", 128)
    fill(o1, 1.0)
    cntb, limi, limb, b8, nB0 = alloc("pb", LANES), alloc("pi", 4), alloc("pb", 4), alloc("pb", 128), alloc("pb", LANES)
    cp(cntb, whole("cnt0", LANES), rows=8)
    ts(sub(limi, 0, 2), whole("lim0", 2), 4032, OP.bitwise_and, rows=8)
    ts(sub(limi, 2, 4), whole("lim0", 2), 63, OP.bitwise_and, rows=8)
    cp(limb, limi, rows=8)
    sel(b8, ones, [[1, 8], [0, 16]], OP.is_equal, 0, -1, rows=8)
    sums([(ps(7, 0, LANES), [(b8, cntb)]), (ps(7, LANES, LANES + 4), [(b8, limb)])], rows=8)
    lim4, sbl, sbl2 = alloc("pf", 4), col(), col()
    act(lim4, ps(7, LANES, LANES + 4), AF.Copy, scale=16.0)
    ts(nB0, ps(7, 0, LANES), kc, OP.is_gt)
    ts(sbl, sub(lim4, 3, 4), 32.0, OP.add, not15, OP.mult)
    ts(sbl2, sbl, -16.0, OP.add)
    CD = [alloc("pb", 256) for _ in range(2)]
    ts(sub(CD[0], 0, 256, 2), ID, sub(lim4, 0, 1), OP.mult, -1.0, OP.mult)
    ts(sub(CD[0], 1, 256, 2), ID, sub(lim4, 1, 2), OP.mult, not15, OP.mult)
    ts(sub(CD[1], 0, 256, 2), ID, sub(lim4, 2, 3), OP.mult, -1.0, OP.mult)
    ts(sub(CD[1], 1, 256, 2), ID, sbl2, OP.mult)

    Gb, ADb, Yb, Hb, AH, MX = [[alloc("pb", H16) for _ in range(2)] for _ in range(6)]
    par = {}

    def til(pool, n, key, t, b):
        k = (key, t % 2, b)
        if k not in par:
            par[k] = alloc(pool, n)
        return par[k]
    accs = [alloc("pf", 2) for _ in range(2)]
    state = {b: dict(z2=zz[b], R=sub(rend0, b * w, (b + 1) * w), L=sub(lend0, b * w, (b + 1) * w),
                     N=[sub(nB0, b * w, (b + 1) * w)]) for b in range(2)}
    UU = alloc("pf", 4 * NQ)
    fill(UU, 0.0)

    def banks(b):
        return 2 + 3 * b, 3 + 3 * b, 4 + 3 * b

    def early(t, b):
        s = state[b]
        P, Q, Rb = banks(b)
        z2 = s["z2"]
        U, UL = ps(P, 0, w), ps(Rb, 0, NQ)
        sums([(U, [(CM, ones), (WB, z2)])])
        r4 = til("pb", w, "r4", t, b)
        ts(r4, U, M4096, OP.add, M4096, OP.subtract)
        sums([(U, [(CP, ones), (WB, z2), (nID, r4)])])
        sq, sql, up, zm = til("pf", w, "sq", t, b), til("pf", NQ, "sql", t, b), til("pf", w, "up", t, b), til("pf", w, "zm", t, b)
        act(sq, U, AF.Square, bias=sqb)
        act(up, U, AF.Copy)
        sums([(UL, [(EW(r), sub(z2, r, w, 16)) for r in range(16)] + [(En(r), sub(r4, r, w, 16)) for r in range(16)])])
        act(sql, UL, AF.Square)
        act(sub(UU, 2 * NQ * b + 1, 2 * NQ * (b + 1), 2), UL, AF.Copy)
        act(zm, z2, AF.Copy, scale=0.5, bias=-0.5)
        s.update(sq=sq, sql=sql, up=up, zm=zm)

    def front(t, b, A, AL):
        s = state[b]
        P, Q, Rb = banks(b)

        def ti(key, n=w):
            return til("pi", n, key, t, b)
        ci, c, cl = ti("ci"), ti("c"), til("pu", w, "cl", t, b)
        ts(ci, s["sq"], 0.03125, OP.mult, A, OP.add)
        ts(c, ci, 2047, OP.bitwise_and)
        cp(cl, c)
        lanes("v", Gb[b], sub(xs, 0, W), cl, OPT["gs"][b], w, OPT["gp"][b])
        lanes("s", Gb[b], sub(xs, 0, W), cl, 0, OPT["gs"][b], w)
        pp, p2 = ti("pp", 2 * w), ti("p2", 2 * w)
        ll = til("pu", 2 * w, "ll", t, b)

        def hashes(lo):
            ts(sub(p2, lo, lo + w), sub(pp, lo, lo + w), 5, OP.arith_shift_right, 2047, OP.bitwise_and)
            ts(sub(ll, lo, lo + w), sub(p2, lo, lo + w), k29, OP.add)
        tt(sub(pp, w, 2 * w), s["R"], ps(P, 0, w), OP.mult)
        hashes(w)
        lo = 0
        for n, _y, how in OPT["runs"][b]:
            if how == "raw":
                lanes("s", Hb[b], xs, sub(ll, w, 2 * w), lo, lo + n, w)
            lo += n
        mm([(ps(Q, 0, w), ones, KD1), (ps(Q, 0, w), ones, KD2)], stop=False)
        for mc in range(4):
            D = (0, 1, Rb, 0)[mc]
            sums([(ps(D, j * w, (j + 1) * w), [(ID, sub(Gb[b], 4 * mc + j, H16, 16)), (hID, s["z2"])]) for j in range(4)])
            ad = sub(ADb[b], mc * 4 * w, (mc + 1) * 4 * w)
            act(ad, ps(D, 0, 512), AF.Abs, scale=4096.0)
            mm([(ps(Q, 4 * mc + j, w, 16), sub(ad, j * w, (j + 1) * w), g8) for j in range(4)], start=False, stop=mc == 3)
        run, rep, pq = ti("run"), til("pb", 8 * NQ, "rep", t, b), ti("pq", 2 * NQ)
        ka, cd, cx = [ti(k, NQ) for k in ("ka", "cd", "cx")]
        cdu, cxu = til("pu", NQ, "cdu", t, b), til("pu", NQ, "cxu", t, b)
        scan(run, RSK, ps(Q, 0, w), 0.0, OP.max, OP.min)
        ts(ka, sub(run, 15, w, 16), 255, OP.bitwise_and)
        gtt(rep, ka, REP, QM, OP.mult)
        act(ps(Rb, 1, 2 * NQ, 2), s["sql"], AF.Identity, scale=0.03125, bias=AL)
        sums([(ps(Rb, 0, 2 * NQ, 2), [(SG(j), sub(rep, NQ * j, NQ * j + NQ)) for j in range(8)])])
        scan(pq, sub(UU, 2 * NQ * b, 2 * NQ * (b + 1)), ps(Rb, 0, 2 * NQ), 0.0, OP.mult, OP.add)
        pc = sub(pq, 1, 2 * NQ, 2)
        ts(cd, pc, 1023, OP.bitwise_and)
        cp(cdu, cd)
        gtt(sub(pp, 0, w), dn, cdu, s["up"], OP.mult)
        hashes(0)
        ts(cx, pc, 2047, OP.bitwise_and)
        cp(cxu, cx)
        Dk, xc = til("pb", w, "Dk", t, b), til("pb", w, "xc", t, b)
        gat(OPT["picks"][b][0], Dk, dn, cdu)
        gat(OPT["picks"][b][1], xc, sub(xs, 0, W), cxu)
        s.update(ll=ll, Dk=Dk, xc=xc)

    def own(t):
        ul, xi, xb = til("pi", 2 * NQ, "ul", t, 0), til("pi", 4 * NQ, "xi", t, 0), til("pb", 2 * NQ, "xb", t, 0)
        l8, l8u = til("pi", 2 * NQ, "l8", t, 0), til("pu", 2 * NQ, "l8u", t, 0)
        cp(ul, sub(UU, 1, 4 * NQ, 2))
        ts(sub(xi, 0, 2 * NQ), ul, 7, OP.bitwise_and)
        ts(sub(xi, 2 * NQ, 4 * NQ), ul, 3, OP.bitwise_and)
        cp(xb, sub(xi, 2 * NQ, 4 * NQ))
        tt(l8, sub(xi, 0, 2 * NQ), l8c, OP.add)
        cp(l8u, l8)
        for b in range(2):
            state[b].update(u3=sub(xb, b * NQ, (b + 1) * NQ), l8u=sub(l8u, b * NQ, (b + 1) * NQ))

    def tail(t, b):
        s = state[b]
        P, Q, Rb = banks(b)
        y, H, mx, ah, ll = Yb[b], Hb[b], MX[b], AH[b], s["ll"]
        lo, plain = 0, []
        for n, who, how in OPT["runs"][b]:
            a, e = 16 * lo, 16 * (lo + n)
            lanes(who, y, xs, ll, lo, lo + n, 16 if who == "v" else w)
            for j in range(a, e, 512):
                scan(sub(mx, j, j + 511), sub(y, j, j + 511), sub(y, j + 1, j + 512), 1000.0)
            if how == "raw":
                for j in range(a, e, 512):
                    D = j // 512 % 2
                    sums([(ps(D, 0, 512), [(ID, sub(H, j, j + 512)), (nID, sub(y, j, j + 512))])])
                    act(sub(ah, j, j + 512), ps(D, 0, 512), AF.Abs)
            else:
                for j in range(lo, lo + n, 16):
                    gtt(sub(H, 16 * j, 16 * j + 256), xs, sub(ll, w + j, w + j + 16), sub(y, 16 * j, 16 * j + 256), OP.subtract)
                if how == "less":
                    act(sub(ah, a, e), sub(H, a, e), AF.Abs)
                else:
                    ts(sub(ah, a, e), sub(H, a, e), 0.0, OP.min, -2.0, OP.mult)
                    plain.append((lo, n))
            lo += n
        V = ps(Q, 0, 256)

        def vc(j):
            return ps(Q, j, 256, 32)

        def kth(a, k):
            return sub(a, k, H16, 16)
        mm([(V, ones, CD[0]), (V, ones, CD[1])] + [(V, n_, SEL) for n_ in s["N"]], stop=False)
        mm([(vc(2 * k + 1), kth(y, k), g16) for k in range(1, 15)] + [(vc(2 * k - 1), kth(y, k), g16) for k in range(2, 16)],
           start=False, stop=False)
        mm([(vc(2 * k + 1), kth(mx, k), g32n) for k in range(1, 15)], start=False, stop=False)
        for lo, n in plain:
            mm([(vc(2 * k) + (lo, n), sub(H, 16 * lo + k, 16 * (lo + n), 16), g16) for k in range(1, 16)], start=False, stop=False)
        mm([(vc(2 * k), kth(ah, k), g16) for k in range(1, 16)], start=False)
        al, back, rep = til("pb", 256, "al", t, b), til("pb", 256, "back", t, b), til("pb", 8 * NQ, "rep2", t, b)
        scan(back, V, CODE, 0.0, back=True)
        scan(al, V, RST, 1.0)
        A1, Dl = til("pb", w, "A1", t, b), til("pb", w, "Dl", t, b)
        sums([(ps(Rb, 0, w), [(sub(al, 1, 256, 2), ID)]),
              (ps(Rb, w, 2 * w), [(sub(al, 1, 256, 2), ID), (sub(al, 0, 256, 2), nID)])])
        act(A1, ps(Rb, 0, w), AF.Copy)
        gtt(rep, back, REB, QM, OP.mult)
        sums([(ps(P, 0, NQ), [(ID, l16)] + [(SG(j), sub(rep, NQ * j, NQ * j + NQ)) for j in range(8)])])
        act(Dl, ps(Rb, w, 2 * w), AF.Copy, accum=sub(accs[t % 2], b, b + 1))
        yel = til("pu", NQ, "yel", t, b)
        cp(yel, ps(P, 0, NQ))
        sz = til("pf", w, "sz", t, b)
        zo = whole("zo%d%d" % (t, b), w)
        gtt(sz, y, yel, s["zm"], OP.add)
        ts(zo, sz, M2, OP.add, M2, OP.subtract)
        if t < VISITS - 1:
            send("z", t, b, zo)
        sx, sx2 = til("pi", w, "sx", t, b), til("pi", w, "sx2", t, b)
        gtt(sx, y, yel, s["xc"], OP.add)
        ts(sx2, sx, 1, OP.arith_shift_right)
        s.update(sx2=sx2, A1=A1, Dl=Dl, al=al)

    def count(t):
        A = ps(0, 0, 1)
        sums([(A, [(o1, sub(accs[t % 2], b, b + 1)) for b in range(2)])])
        ac, al = til("pf", 1, "A", t, 0), til("pf", 1, "AL", t, 0)
        act(ac, A, AF.Identity, bias=cA2)
        act(al, A, AF.Copy, bias=2047.625)
        return ac, al

    def writes_x(t, b):
        scat(sub(xs, b * W // 2, (b + 1) * W // 2), state[b]["l8u"], state[b]["sx2"])
        if b == 0 and t < VISITS - 1:
            dma(T.xs[:, W:W + EXT], T.xs[:, 0:EXT], [sub(xs, 0, EXT)], [sub(xs, W, W + EXT)])

    def update(t, b):
        s = state[b]
        P, Q, Rb = banks(b)
        L, R, N, A1, Dl = s["L"], s["R"], s["N"], s["A1"], s["Dl"]
        last = t == VISITS - 1
        ro = whole("ro%d%d" % (t, b), 4 * w)
        Rn, Ln, N2 = [sub(ro, j * w, (j + 1) * w) for j in (0, 1, 3)]
        c3, r3 = til("pb", w, "c3", t, b), til("pb", 3 * w, "r3", t, b)
        sums([(ps(Q, 0, w), [(ID, s["Dk"]), (Mc1, A1), (nB, Dl)] + [(nB, n_) for n_ in N]),
              (ps(Q, w, 2 * w), [(ID, R), (nB, A1), (PB, Dl)]),
              (ps(Q, 2 * w, 3 * w), [(ID, R), (nS0, A1), (nBm, Dl)])])
        act(r3, ps(Q, 0, 3 * w), AF.Relu)
        sums([(ps(Rb, 0, w), [(nB, A1), (Mp3, Dl)] + [(p2B, n_) for n_ in N])])
        tt(c3, ps(Rb, 0, w), L, OP.min)
        sums([(ps(Q, 0, w), [(ID, sub(r3, 0, w)), (ID, sub(r3, w, 2 * w))])])
        tt(Ln, ps(Q, 0, w), c3, OP.max)
        first = [(pBm, Dl)] + [(ET(r), (ps(P, r, w, 16), s["u3"])) for r in range(16)]
        dlu, own_ = til("pu", NQ, "dlu", t, b), [(ID, sub(l4c, b * NQ, (b + 1) * NQ)), (ID, s["u3"])]
        if last:
            nd, rep = til("pb", 256, "nd", t, b), til("pb", 8 * NQ, "rep3", t, b)
            scan(nd, ALT, s["al"], 0.0, OP.mult, OP.add)
            gtt(rep, nd, REN, QD[b], OP.mult)
            sums([(ps(P, 0, NQ), own_ + [(SG(j), sub(rep, NQ * j, NQ * j + NQ)) for j in range(8)])])
            cp(dlu, ps(P, 0, NQ))
            sums([(ps(P, 0, w), first), (ps(P, w, 2 * w), [(ML, A1), (nBm, Dl)])])
            act(sub(ro, 2 * w, 4 * w), ps(P, 0, 2 * w), AF.Relu, bias=1.0)
        else:
            sums([(ps(P, 0, w), first), (ps(P, w, 2 * w), [(Mc1, A1), (MN2, Dl)])])
            act(sub(ro, 2 * w, 4 * w), ps(P, 0, 2 * w), AF.Relu, bias=one_k)
        sums([(ps(Q, 0, w), [(ID, Ln), (pBm, Dl)])])
        tt(Rn, ps(Q, 0, w), sub(r3, 2 * w, 3 * w), OP.max)
        if not last:
            send("r", t, b, Rn)
            send("q", t, b, sub(ro, w, 4 * w))
            sums([(ps(Rb, 0, NQ), own_ + [(E1[b](r), sub(N2, r, w, 16)) for r in range(16)])])
            cp(dlu, ps(Rb, 0, NQ))
        scat(("dn", b * ND, (b + 1) * ND, 1), dlu, Ln)

    snt = {k: 0 for k in KINDS}

    def send(k, t, b, tile):
        dst = relays(topo, cores, rank)[KINDS.index(k)]
        rid, pid = topo.addr(dst, core)
        m = topo.mask(core, dst)
        snt[k] += len(topo.engines(core, dst))
        name = "%s%d%d" % (k, t, b)
        o = op("g", [lambda: g.remote_dma(T[k + "i" + name[1:]][:], ap(tile), T.sem["a" + name], T.sem[k + "sent"], pid, rid, m)],
               [tile], [], 0.4, done=(k + "sent", 0))
        n = len(topo.engines(relays(topo, cores, (rank - 1) % len(cores))[KINDS.index(k)], core))
        op(None, [], [], [whole(k + "i" + name[1:], cnt(tile))], 0.0, done=("a" + name, n), lat=OPT[k + "lat"], extra=(o,))

    A = (cA, AL0)
    for t in range(VISITS):
        stage[1] = t
        for name, step in (("early", early), ("front", lambda t, b: front(t, b, *A))):
            for b in range(2):
                stage[0] = name + str(b)
                step(t, b)
        stage[0] = "own"
        own(t)
        for b in range(2):
            stage[0] = "tail%d" % b
            tail(t, b)
        stage[0] = "write"
        if t < VISITS - 1:
            A = count(t)
        for b in range(2):
            writes_x(t, b)
        for b in range(2):
            stage[0] = "update%d" % b
            update(t, b)
        stage[0] = "end"
        for b in range(2):
            if t < VISITS - 1:
                r = whole("qi%d%d" % (t, b), 3 * w)
                state[b] = dict(z2=whole("zi%d%d" % (t, b), w), R=whole("ri%d%d" % (t, b), w), L=sub(r, 0, w),
                                N=[sub(r, w, 2 * w), sub(r, 2 * w, 3 * w)])
            else:
                zo, r = whole("zo%d%d" % (t, b), w), whole("ro%d%d" % (t, b), 4 * w)
                lo, hi = b * w, (b + 1) * w
                act(sub(whole("yz0", LANES), lo, hi), zo, AF.Copy, scale=0.5)
                dma(T.yz[:, lo:hi], T.yz0[:, lo:hi], [("yz0", lo, hi, 1)], [])
                sums([(ps(b, 0, w), [(g8, sub(r, 2 * w, 3 * w)), (g8, sub(r, 3 * w, 4 * w))])], out_rows=8)
                act(("yn0", lo, hi, 1), ps(b, 0, w), AF.Copy, scale=0.0625, rows=8)
                dma(T.yr[:, lo:hi], ap(sub(r, 0, w)), [sub(r, 0, w)], [])
                dma(T.yl[:, lo:hi], ap(sub(r, w, 2 * w)), [sub(r, w, 2 * w)], [])
    dma(T.yn[:], T.yn0[:], [("yn0", 0, LANES, 1)], [])
    for b in range(2):
        lo, hi = b * W // 2, (b + 1) * W // 2
        dma(T.yx[:, lo:hi], T.xs[:, lo:hi], [sub(xs, lo, hi)], [], dur=3.0)
        dma(T.yd[:, lo // 2:hi // 2], ap(sub(dn, lo // 2, hi // 2)), [sub(dn, lo // 2, hi // 2)], [], dur=2.3)

    if not ORDER:
        ORDER.extend(schedule(ops))
    QUEUE = {"v": g.vector, "s": g.scalar, "t": g.tensor, "g": g, "y": g.sync}
    SEM = {"v": "sv", "s": "ss", "t": "st", "g": "sg"}
    made = {k: 0 for k in SEM.values()}
    know = {e: {} for e in QUEUE}
    final = {}
    for i in ORDER:
        o = ops[i]
        e = o["eng"]
        if e is None:
            o["clock"], o["mark"] = {}, o["done"]
            final[o["done"][0]] = o["done"][1]
            continue
        kn = know[e]
        need = {}
        for d in o["deps"]:
            m = ops[d]["mark"]
            if m is not None and kn.get(m[0], 0) < m[1]:
                need[m[0]] = max(need.get(m[0], 0), m[1])
        for d in sorted(o["deps"], reverse=True):
            m = ops[d]["mark"]
            if m is None or need.get(m[0], 0) != m[1]:
                continue
            for k, v in ops[d]["clock"].items():
                if k != m[0] and k in need and need[k] <= v:
                    need.pop(k)
        for k in need:
            QUEUE[e].wait_ge(T.sem[k], need[k])
        for d in o["deps"]:
            m = ops[d]["mark"]
            if m is not None:
                kn[m[0]] = max(kn.get(m[0], 0), m[1])
                for k, v in ops[d]["clock"].items():
                    kn[k] = max(kn.get(k, 0), v)
        o["clock"] = dict(kn)
        for f in o["fns"]:
            ins = f()
        if o["done"] is None:
            made[SEM[e]] += 1
            ins.then_inc(T.sem[SEM[e]], 1)
            o["mark"] = (SEM[e], made[SEM[e]])
        elif o["done"][1] == 16:
            ins.then_inc(T.sem[o["done"][0]], 16)
            o["mark"] = o["done"]
            final[o["done"][0]] = 16
        else:
            o["mark"] = None
    for k in SEM.values():
        g.wait_ge(T.sem[k], made[k])
    for k, v in final.items():
        g.wait_ge(T.sem[k], v)
    for k in KINDS:
        g.wait_ge(T.sem[k + "sent"], snt[k])
